import numpy as np
import ml_dtypes


def mxq(x, axis, fmt="e4m3"):
    dtype, down = {"e4m3": (ml_dtypes.float8_e4m3fn, 7), "e5m2": (ml_dtypes.float8_e5m2, 14)}[fmt]
    v = np.moveaxis(np.asarray(x, np.float32).astype(ml_dtypes.bfloat16).astype(np.float64), axis, -1)
    blocks = v.reshape(v.shape[:-1] + (-1, 32))
    amax = np.abs(blocks).max(-1, keepdims=True)
    byte = np.maximum(np.where(amax > 0, np.frexp(amax)[1] - 1 + 127, 0) - down, 1)
    scale = np.exp2(byte - 127.0)
    codes = (blocks / scale).astype(np.float32).astype(dtype).astype(np.float64)
    return np.moveaxis((codes * scale).reshape(v.shape), -1, axis)


WIDE = False


def mx_kscale(k):
    if not WIDE:
        return np.ones(k)
    levels = np.array([10, -10, 5, -5, 0])
    if k % 512:
        return np.exp2(np.random.permutation(np.resize(levels, k // 32))).repeat(32)
    a = np.empty((k // 512, 16))
    for p in range(k // 512):
        a[p, :8] = np.random.permutation(np.resize(levels, 8))
        for g in range(8):
            far = levels[np.abs(levels - a[p, g]) >= 10]
            a[p, g + 8] = far[np.random.randint(len(far))]
    return np.exp2(a.ravel()).repeat(32)


def f64(x):
    return np.asarray(x).astype(np.float64)


def striped(idx):
    return np.tile(idx.reshape(-1, 16).T, (8, 1)).astype(np.uint16)


def unstriped(offs):
    return offs[:16].T.reshape(-1).astype(np.int64)


E2M1 = np.array([0.0, 0.5, 1.0, 1.5, 2.0, 3.0, 4.0, 6.0, -0.0, -0.5, -1.0, -1.5, -2.0, -3.0, -4.0, -6.0])


def pack_weight(w, fmt):
    k, n = w.shape
    w = f64(np.asarray(w, np.float32).astype(ml_dtypes.bfloat16)).reshape(k // 32, 32, n)
    amax = np.abs(w).max(1)
    if fmt == "e4m3":
        byte = np.frexp(amax)[1] - 1 + 127 - 7
    else:
        mant, ex = np.frexp(amax / 6.0)
        byte = np.where(mant > 0.5, ex, ex - 1) + 127
    byte = np.clip(np.where(amax > 0, byte, 1), 1, 254)
    scaled = (w * np.exp2(127.0 - byte)[:, None, :]).reshape(k, n).astype(np.float32)
    by_word = np.ascontiguousarray(scaled.reshape(k // 512, 128, 4, n).transpose(0, 1, 3, 2))
    if fmt == "e4m3":
        words = by_word.astype(ml_dtypes.float8_e4m3fn).view(np.uint8)
    else:
        c = by_word.astype(ml_dtypes.float4_e2m1fn).view(np.uint8) & 0xF
        words = (c[..., 0::2] | (c[..., 1::2] << 4)).reshape(k // 512, 128, 2 * n)
    return np.ascontiguousarray(words), np.ascontiguousarray(byte.astype(np.uint8).reshape(k // 512, 16, n))


def unpack_weight(words, scales, fmt):
    g, _, n = scales.shape
    words = np.ascontiguousarray(words).reshape(g, 128, n, -1)
    if fmt == "e4m3":
        vals = words.view(ml_dtypes.float8_e4m3fn).astype(np.float64)
    else:
        nib = np.empty((g, 128, n, 4), np.uint8)
        nib[..., 0::2] = words & 0xF
        nib[..., 1::2] = words >> 4
        vals = E2M1[nib]
    vals = vals * np.repeat(np.exp2(scales.astype(np.float64) - 127.0), 8, axis=1)[..., None]
    return vals.transpose(0, 1, 3, 2).reshape(g * 512, n)


def relu(v):
    return np.maximum(v, 0.0)


K, T, E, C, H, N = 512, 512, 16, 128, 512, 128
TOP = 4


def by_expert(wq, xq):
    return np.concatenate([wq[e].T @ xq[:, e * C:(e + 1) * C] for e in range(E)], axis=1)


def setup_inputs():
    n = np.random.standard_normal
    s = mx_kscale(K)[:, None]
    u = mx_kscale(H)
    deal = np.repeat(np.arange(E), C).reshape(TOP, T)[:, np.random.permutation(T)]
    deal = np.take_along_axis(deal, np.argsort(np.random.rand(TOP, T), axis=0), axis=0)
    for _ in range(8):
        s_, t_ = np.random.permutation(T).reshape(2, -1); r = np.random.randint(TOP, size=T // 2); x, y = deal[r, s_].copy(), deal[r, t_].copy()
        ok = ~((deal[:, s_] == y).any(0) | (deal[:, t_] == x).any(0)); deal[r[ok], s_[ok]] = y[ok]; deal[r[ok], t_[ok]] = x[ok]
    order = np.lexsort((np.random.rand(TOP * T), deal.reshape(-1)))
    slot_token = order % T; pos = np.empty(TOP * T, np.int64); pos[order] = np.arange(TOP * T); pos = pos.reshape(TOP, T)
    g = np.random.uniform(0.5, 1.5, (TOP, T)); g = g / g.sum(0)
    w1 = [pack_weight(m, "e2m1") for m in n((E + 1, K, H)) / np.sqrt(K) / s[None]]
    w3 = [pack_weight(m, "e2m1") for m in n((E + 1, K, H)) / np.sqrt(K) / s[None] * u[None, None, :]]
    w2 = [pack_weight(m, "e2m1") for m in n((E + 1, H, N)) / np.sqrt(H) / u[None, :, None]]
    x = pack_weight(n((K, T)) * s, "e4m3")
    return {
        "x_words": x[0],
        "x_scales": x[1],
        "w1_words": np.stack([m[0] for m in w1]),
        "w1_scales": np.stack([m[1] for m in w1]),
        "w3_words": np.stack([m[0] for m in w3]),
        "w3_scales": np.stack([m[1] for m in w3]),
        "w2_words": np.stack([m[0] for m in w2]),
        "w2_scales": np.stack([m[1] for m in w2]),
        "gate": np.stack([np.tile(r, (N, 1)) for r in g]).astype(np.float32),
        "offs": striped(slot_token),
        "pos1": striped(pos[0]),
        "pos2": striped(pos[1]),
        "pos3": striped(pos[2]),
        "pos4": striped(pos[3]),
    }


def reference(x_words, x_scales, w1_words, w1_scales, w3_words, w3_scales, w2_words, w2_scales, gate, offs, pos1, pos2, pos3, pos4):
    idx = unstriped(offs)
    w1 = np.stack([unpack_weight(w1_words[e], w1_scales[e], "e2m1") for e in range(E + 1)])
    w3 = np.stack([unpack_weight(w3_words[e], w3_scales[e], "e2m1") for e in range(E + 1)])
    w2 = np.stack([unpack_weight(w2_words[e], w2_scales[e], "e2m1") for e in range(E + 1)])
    w1q, w3q, w2q = w1, w3, w2
    xs = unpack_weight(x_words, x_scales, "e4m3")
    hs = relu(w1q[E].T @ xs) * (w3q[E].T @ xs)
    ys = w2q[E].T @ mxq(hs, 0, "e4m3")
    xq = unpack_weight(x_words, x_scales, "e4m3")[:, idx]
    h = relu(by_expert(w1q, xq))
    h = h * by_expert(w3q, xq)
    y = by_expert(w2q, mxq(h, 0, "e4m3"))
    return ys + sum(f64(gate[r]) * y[:, unstriped(p)] for r, p in enumerate((pos1, pos2, pos3, pos4)))

@@ -1,0 +1,233 @@
+from contextlib import ExitStack
+
+import concourse.mybir as mybir
+from concourse.masks import make_identity
+
+K, T, E, C, H, N = 512, 512, 16, 128, 512, 128
+TOP = 4
+FLOPS = 3019898880
+
+F32 = mybir.dt.float32
+BF16 = mybir.dt.bfloat16
+I32 = mybir.dt.int32
+U32 = mybir.dt.uint32
+U16 = mybir.dt.uint16
+U8 = mybir.dt.uint8
+FP8X4 = mybir.dt.float8_e4m3fn_x4
+FP4X4 = mybir.dt.float4_e2m1fn_x4
+MULT = mybir.AluOpType.mult
+ADD = mybir.AluOpType.add
+RELU = mybir.ActivationFunctionType.Relu
+
+P = 128
+PAIRS = E // 2
+SHARED_PAIRS = T // (2 * C)
+WORD_GROUPS = [(0, 2), (2, 5), (5, 9), (9, 13), (13, 17)]
+SCALE_GROUPS = [(0, 4), (4, 10), (10, 17)]
+W2_GROUPS = [(0, 6), (6, 17)]
+GATHER_LEAD = 3
+
+
+def group_of(groups, e):
+    return [g for g, (lo, hi) in enumerate(groups) if lo <= e < hi][0]
+
+
+def tile_moe_shr_glu_relu_kernel(
+    tc, x_words, x_scales, w1_words, w1_scales, w3_words, w3_scales, w2_words, w2_scales,
+    gate, offs, pos1, pos2, pos3, pos4, out,
+):
+    nc = tc.nc
+    with ExitStack() as ctx:
+        lists = ctx.enter_context(tc.tile_pool(name="lists", bufs=1))
+        keep = ctx.enter_context(tc.tile_pool(name="keep", bufs=1))
+        work = ctx.enter_context(tc.tile_pool(name="work", bufs=4))
+        psum = ctx.enter_context(tc.psum_pool(name="psum", bufs=1))
+
+        offs_t = lists.tile([P, E * C // 16], U16, name="offs_t")
+        pos_t = [lists.tile([P, T // 16], U16, name=f"pos_t{r}") for r in range(TOP)]
+        xw = keep.tile([P, T], I32, name="xw", align_bytes=64)
+        xs = keep.tile([P, T], U8, name="xs", align_bytes=64)
+        up_words = [[keep.tile([P, hi - lo, 2 * H], U8, name=f"up_words{m}_{g}", align_bytes=64)
+                     for g, (lo, hi) in enumerate(WORD_GROUPS)] for m in range(2)]
+        up_scales = [keep.tile([P, 2, hi - lo, H], U8, name=f"up_scales{g}", align_bytes=64)
+                     for g, (lo, hi) in enumerate(SCALE_GROUPS)]
+        down_words = [keep.tile([P, hi - lo, 2 * N], U8, name=f"down_words{g}", align_bytes=64)
+                      for g, (lo, hi) in enumerate(W2_GROUPS)]
+        down_scales = keep.tile([P, E + 1, N], U8, name="down_scales", align_bytes=64)
+        gate_t = keep.tile([P, TOP, T], F32, name="gate_t")
+        y_slots = keep.tile([P, E * C], F32, name="y_slots")
+        ident = keep.tile([P, P], F32, name="ident")
+        warm = keep.tile([P, 16], F32, name="warm")
+
+        nc.vector.memset(warm[:, 0:8], 0.0)
+        nc.scalar.activation(out=warm[:, 8:16], in_=warm[:, 0:8], func=RELU)
+        nc.gpsimd.memset(xs[:].bitcast(I32), 0)
+        nc.gpsimd.memset(up_scales[0][:].bitcast(I32), 0)
+        nc.gpsimd.memset(down_scales[:].bitcast(I32), 0)
+        nc.gpsimd.memset(up_scales[1][:].bitcast(I32), 0)
+        make_identity(nc, ident[:])
+        nc.gpsimd.memset(up_scales[2][:].bitcast(I32), 0)
+        s_banks = [psum.tile([P, H], F32, name=f"s_bank{b}") for b in range(4)]
+        b_banks = [psum.tile([P, H], F32, name=f"b_bank{b}") for b in range(4)]
+
+        def load_up_words(g):
+            lo, hi = WORD_GROUPS[g]
+            for m, w in enumerate((w1_words, w3_words)):
+                nc.sync.dma_start(out=up_words[m][g][:].bitcast(I32),
+                                  in_=w[lo:hi, 0].rearrange("e p b -> p e b").bitcast(I32))
+
+        def load_up_scales(g):
+            lo, hi = SCALE_GROUPS[g]
+            for m, s in enumerate((w1_scales, w3_scales)):
+                for r in range(4):
+                    nc.sync.dma_start(out=up_scales[g][:].bitcast(I32)[r:P:32, m],
+                                      in_=s[lo:hi, 0, r:16:4, :].rearrange("e q i -> q e i").bitcast(I32))
+
+        def load_down_words(g):
+            lo, hi = W2_GROUPS[g]
+            nc.sync.dma_start(out=down_words[g][:].bitcast(I32),
+                              in_=w2_words[lo:hi, 0].rearrange("e p b -> p e b").bitcast(I32))
+
+        nc.sync.dma_start(offs_t[:], offs)
+        nc.sync.dma_start(out=xw[:], in_=x_words[0].rearrange("p t r -> p (t r)").bitcast(I32))
+        for r in range(4):
+            nc.sync.dma_start(out=xs[:].bitcast(I32)[r:P:32, :], in_=x_scales[0, r:16:4, :].bitcast(I32))
+        load_up_words(0)
+        load_up_scales(0)
+        load_up_words(1)
+        load_down_words(0)
+        for r in range(4):
+            nc.sync.dma_start(out=down_scales[:].bitcast(I32)[r:P:32],
+                              in_=w2_scales[:, 0, r:16:4, :].rearrange("e q n -> q e n").bitcast(I32))
+        load_up_scales(1)
+        load_up_words(2)
+        load_down_words(1)
+        load_up_words(3)
+        load_up_scales(2)
+        load_up_words(4)
+        for r, pos in enumerate((pos1, pos2, pos3, pos4)):
+            nc.sync.dma_start(pos_t[r][:], pos)
+        nc.sync.dma_start(out=gate_t[:], in_=gate.rearrange("r p t -> p r t"))
+
+        slot_words = [keep.tile([P, 2 * C], U32, name=f"slot_words{q}", align_bytes=64) for q in range(GATHER_LEAD)]
+        slot_scales = [keep.tile([P, 2 * C], U8, name=f"slot_scales{q}", align_bytes=64) for q in range(GATHER_LEAD)]
+
+        def gather_words(q):
+            nc.vector.tensor_copy(out=slot_words[q % GATHER_LEAD][:],
+                                  in_=xw[:].bitcast(U32).indirect(offs_t[:, 16 * q:16 * (q + 1)]))
+
+        def gather_scales(q):
+            nc.vector.tensor_copy(out=slot_scales[q % GATHER_LEAD][:], in_=xs[:].indirect(offs_t[:, 16 * q:16 * (q + 1)]))
+
+        by_word = "s (p u e) -> s u p e"
+        as_laid = "s (u p e) -> s u p e"
+        h_tiles, turned, quantised = {}, {}, {}
+
+        def up(u):
+            q, j = divmod(u, 2)
+            if q < PAIRS:
+                e = u
+                cols = slice(j * C, (j + 1) * C)
+                words, scales = slot_words[q % GATHER_LEAD][:, cols], slot_scales[q % GATHER_LEAD][:, cols]
+            else:
+                e = E
+                cols = slice((u - E) * C, (u - E + 1) * C)
+                words, scales = xw[:, cols], xs[:, cols]
+            gw, gs = group_of(WORD_GROUPS, e), group_of(SCALE_GROUPS, e)
+            ew, es = e - WORD_GROUPS[gw][0], e - SCALE_GROUPS[gs][0]
+            a_ps, b_ps = s_banks[u % 4], b_banks[u % 4]
+            for m, acc in enumerate((a_ps, b_ps)):
+                nc.tensor.matmul_mx(out=acc[:], lhsT=words.bitcast(FP8X4), lhsT_scale=scales,
+                                    rhs=up_words[m][gw][:, ew, :].bitcast(FP4X4),
+                                    rhs_scale=up_scales[gs][:, m, es, :], start=True, stop=True)
+            relu_a = work.tile([P, H], F32, name="relu_a")
+            nc.scalar.activation(out=relu_a[:].rearrange(as_laid, u=2, e=2),
+                                 in_=a_ps[:].rearrange(by_word, u=2, e=2), func=RELU)
+            h = work.tile([P, H], BF16, name="h", align_bytes=64)
+            nc.vector.tensor_tensor(out=h[:].rearrange(as_laid, u=2, e=2),
+                                    in0=b_ps[:].rearrange(by_word, u=2, e=2),
+                                    in1=relu_a[:].rearrange(as_laid, u=2, e=2), op=MULT)
+            h_tiles[u] = h
+
+        def turn(q, bank):
+            t_ps = bank[:].rearrange("p (j u s) -> p j u s", j=2, u=2)
+            for j in range(2):
+                words = h_tiles[2 * q + j][:].bitcast(F32)
+                for u in range(2):
+                    nc.tensor.transpose(t_ps[:, j, u, :], words[:, u * P:(u + 1) * P], ident[:])
+            ht = work.tile([P, 2 * C * 4], BF16, name="ht", align_bytes=64)
+            nc.scalar.copy(out=ht[:].bitcast(F32).rearrange("p (j s u) -> p j s u", j=2, u=2),
+                           in_=t_ps.rearrange("p j u s -> p j s u"))
+            turned[q] = ht
+
+        def quantise(q):
+            codes = work.tile([P, 2 * C], U32, name="codes", align_bytes=64)
+            scales = work.tile([P, 2 * C], U8, name="scales", align_bytes=64)
+            nc.vector.quantize_mx(out=codes[:].bitcast(FP8X4), scales=scales[:], in_=turned[q][:])
+            quantised[q] = (codes, scales)
+
+        def down_weights(e):
+            g = group_of(W2_GROUPS, e)
+            return down_words[g][:, e - W2_GROUPS[g][0], :].bitcast(FP4X4), down_scales[:, e, :]
+
+        def down(q, y_ps):
+            codes, scales = quantised[q]
+            for j in range(2):
+                cols = slice(j * C, (j + 1) * C)
+                w, s = down_weights(2 * q + j)
+                nc.tensor.matmul_mx(out=y_ps[:, cols], lhsT=w, lhsT_scale=s,
+                                    rhs=codes[:, cols].bitcast(FP8X4), rhs_scale=scales[:, cols],
+                                    start=True, stop=True)
+            nc.scalar.copy(out=y_slots[:, 2 * C * q:2 * C * (q + 1)], in_=y_ps[:, 0:2 * C])
+
+        def down_shared(q, ys_ps):
+            codes, scales = quantised[q]
+            w, s = down_weights(E)
+            nc.tensor.matmul_mx(out=ys_ps[:, 2 * C * (q - PAIRS):2 * C * (q - PAIRS + 1)], lhsT=w, lhsT_scale=s,
+                                rhs=codes[:].bitcast(FP8X4), rhs_scale=scales[:], start=True, stop=True)
+
+        for q in range(GATHER_LEAD):
+            gather_words(q)
+            gather_scales(q)
+        for q in range(PAIRS + 1):
+            up(2 * q)
+            up(2 * q + 1)
+            if q + GATHER_LEAD < PAIRS:
+                gather_words(q + GATHER_LEAD)
+                gather_scales(q + GATHER_LEAD)
+            if q >= 1:
+                turn(q - 1, s_banks[(2 * q) % 4])
+                quantise(q - 1)
+            if q >= 2:
+                down(q - 2, s_banks[(2 * q + 1) % 4])
+
+        last = PAIRS + SHARED_PAIRS - 1
+        down(PAIRS - 1, b_banks[0])
+        up(2 * last)
+        up(2 * last + 1)
+        turn(last - 1, s_banks[0])
+        quantise(last - 1)
+        ys_ps = b_banks[1]
+        down_shared(last - 1, ys_ps)
+        turn(last, s_banks[1])
+        prod = [keep.tile([P, T], F32, name=f"prod{r}") for r in range(TOP)]
+
+        def fetch(r):
+            nc.vector.tensor_tensor(out=prod[r][:], in0=y_slots[:].indirect(pos_t[r][:]), in1=gate_t[:, r, :], op=MULT)
+
+        fetch(0)
+        quantise(last)
+        down_shared(last, ys_ps)
+        fetch(1)
+        sum_a = keep.tile([P, T], F32, name="sum_a")
+        sum_b = keep.tile([P, T], F32, name="sum_b")
+        nc.vector.tensor_tensor(out=sum_a[:], in0=ys_ps[:], in1=prod[0][:], op=ADD)
+        fetch(2)
+        nc.vector.tensor_tensor(out=sum_b[:], in0=sum_a[:], in1=prod[1][:], op=ADD)
+        fetch(3)
+        halves = [slice(0, T // 2), slice(T // 2, T)]
+        for cols in halves:
+            nc.vector.tensor_tensor(out=sum_a[:, cols], in0=sum_b[:, cols], in1=prod[2][:, cols], op=ADD)
+        for cols in halves:
+            nc.vector.tensor_tensor(out=sum_b[:, cols], in0=sum_a[:, cols], in1=prod[3][:, cols], op=ADD)
+            nc.sync.dma_start(out=out[:, cols], in_=sum_b[:, cols])

@@ -22,14 +22,21 @@ RELU = mybir.ActivationFunctionType.Relu
 P = 128
 PAIRS = E // 2
 SHARED_PAIRS = T // (2 * C)
-WORD_GROUPS = [(0, 2), (2, 5), (5, 9), (9, 13), (13, 17)]
-SCALE_GROUPS = [(0, 4), (4, 10), (10, 17)]
+WORD_GROUPS = [(e, min(e + 2, E + 1)) for e in range(0, E + 1, 2)]
+SCALE_GROUPS = [(0, 6), (6, 12), (12, 17)]
 W2_GROUPS = [(0, 6), (6, 17)]
-GATHER_LEAD = 3
+GATHER_LEAD = 4
+TURNED = 3 * C
+WORD_TILE = [0, 1, 2, 3, 0, 1, 3, 0]
+SCALE_TILE = [0, 1, 2, 3, 1, 2, 3, 1]
 
 
 def group_of(groups, e):
     return [g for g, (lo, hi) in enumerate(groups) if lo <= e < hi][0]
+
+
+def previous_tenant(tiles, q):
+    return max(p for p in range(q) if tiles[p] == tiles[q])
 
 
 def tile_moe_shr_glu_relu_kernel(
@@ -50,23 +57,22 @@ def tile_moe_shr_glu_relu_kernel(
         up_words = [[keep.tile([P, hi - lo, 2 * H], U8, name=f"up_words{m}_{g}", align_bytes=64)
                      for g, (lo, hi) in enumerate(WORD_GROUPS)] for m in range(2)]
         up_scales = [keep.tile([P, 2, hi - lo, H], U8, name=f"up_scales{g}", align_bytes=64)
-                     for g, (lo, hi) in enumerate(SCALE_GROUPS)]
+                     for g, (lo, hi) in enumerate(SCALE_GROUPS[:2])]
         down_words = [keep.tile([P, hi - lo, 2 * N], U8, name=f"down_words{g}", align_bytes=64)
                       for g, (lo, hi) in enumerate(W2_GROUPS)]
         down_scales = keep.tile([P, E + 1, N], U8, name="down_scales", align_bytes=64)
         gate_t = keep.tile([P, TOP, T], F32, name="gate_t")
         y_slots = keep.tile([P, E * C], F32, name="y_slots")
         ident = keep.tile([P, P], F32, name="ident")
-        warm = keep.tile([P, 16], F32, name="warm")
+        warm = keep.tile([P, 8], F32, name="warm")
 
-        nc.vector.memset(warm[:, 0:8], 0.0)
-        nc.scalar.activation(out=warm[:, 8:16], in_=warm[:, 0:8], func=RELU)
         nc.gpsimd.memset(xs[:].bitcast(I32), 0)
-        nc.gpsimd.memset(up_scales[0][:].bitcast(I32), 0)
-        nc.gpsimd.memset(down_scales[:].bitcast(I32), 0)
-        nc.gpsimd.memset(up_scales[1][:].bitcast(I32), 0)
+        nc.vector.memset(up_scales[0][:, 0].bitcast(I32), 0)
+        nc.vector.memset(up_scales[0][:, 1].bitcast(I32), 0)
+        nc.vector.memset(down_scales[:].bitcast(I32), 0)
+        nc.vector.memset(up_scales[1][:].bitcast(I32), 0)
         make_identity(nc, ident[:])
-        nc.gpsimd.memset(up_scales[2][:].bitcast(I32), 0)
+        nc.scalar.activation(out=warm[:], in_=ident[:, 0:8], func=RELU)
         s_banks = [psum.tile([P, H], F32, name=f"s_bank{b}") for b in range(4)]
         b_banks = [psum.tile([P, H], F32, name=f"b_bank{b}") for b in range(4)]
 
@@ -80,7 +86,7 @@ def tile_moe_shr_glu_relu_kernel(
             lo, hi = SCALE_GROUPS[g]
             for m, s in enumerate((w1_scales, w3_scales)):
                 for r in range(4):
-                    nc.sync.dma_start(out=up_scales[g][:].bitcast(I32)[r:P:32, m],
+                    nc.sync.dma_start(out=up_scales[g % 2][:].bitcast(I32)[r:P:32, m, 0:hi - lo],
                                       in_=s[lo:hi, 0, r:16:4, :].rearrange("e q i -> q e i").bitcast(I32))
 
         def load_down_words(g):
@@ -89,57 +95,54 @@ def tile_moe_shr_glu_relu_kernel(
                               in_=w2_words[lo:hi, 0].rearrange("e p b -> p e b").bitcast(I32))
 
         nc.sync.dma_start(offs_t[:], offs)
-        nc.sync.dma_start(out=xw[:], in_=x_words[0].rearrange("p t r -> p (t r)").bitcast(I32))
         for r in range(4):
             nc.sync.dma_start(out=xs[:].bitcast(I32)[r:P:32, :], in_=x_scales[0, r:16:4, :].bitcast(I32))
-        load_up_words(0)
+        nc.sync.dma_start(out=xw[:], in_=x_words[0].rearrange("p t r -> p (t r)").bitcast(I32))
         load_up_scales(0)
+        load_up_words(0)
         load_up_words(1)
         load_down_words(0)
+        load_up_words(2)
         for r in range(4):
             nc.sync.dma_start(out=down_scales[:].bitcast(I32)[r:P:32],
                               in_=w2_scales[:, 0, r:16:4, :].rearrange("e q n -> q e n").bitcast(I32))
         load_up_scales(1)
-        load_up_words(2)
-        load_down_words(1)
         load_up_words(3)
-        load_up_scales(2)
         load_up_words(4)
-        for r, pos in enumerate((pos1, pos2, pos3, pos4)):
-            nc.sync.dma_start(pos_t[r][:], pos)
-        nc.sync.dma_start(out=gate_t[:], in_=gate.rearrange("r p t -> p r t"))
+        load_down_words(1)
+        load_up_words(5)
 
         slot_words = [keep.tile([P, 2 * C], U32, name=f"slot_words{q}", align_bytes=64) for q in range(GATHER_LEAD)]
         slot_scales = [keep.tile([P, 2 * C], U8, name=f"slot_scales{q}", align_bytes=64) for q in range(GATHER_LEAD)]
 
         def gather_words(q):
-            nc.vector.tensor_copy(out=slot_words[q % GATHER_LEAD][:],
+            nc.vector.tensor_copy(out=slot_words[WORD_TILE[q]][:],
                                   in_=xw[:].bitcast(U32).indirect(offs_t[:, 16 * q:16 * (q + 1)]))
 
         def gather_scales(q):
-            nc.vector.tensor_copy(out=slot_scales[q % GATHER_LEAD][:], in_=xs[:].indirect(offs_t[:, 16 * q:16 * (q + 1)]))
+            nc.vector.tensor_copy(out=slot_scales[SCALE_TILE[q]][:], in_=xs[:].indirect(offs_t[:, 16 * q:16 * (q + 1)]))
 
         by_word = "s (p u e) -> s u p e"
         as_laid = "s (u p e) -> s u p e"
         h_tiles, turned, quantised = {}, {}, {}
 
-        def up(u):
+        def up(u, a_ps):
             q, j = divmod(u, 2)
             if q < PAIRS:
                 e = u
                 cols = slice(j * C, (j + 1) * C)
-                words, scales = slot_words[q % GATHER_LEAD][:, cols], slot_scales[q % GATHER_LEAD][:, cols]
+                words, scales = slot_words[WORD_TILE[q]][:, cols], slot_scales[SCALE_TILE[q]][:, cols]
             else:
                 e = E
                 cols = slice((u - E) * C, (u - E + 1) * C)
                 words, scales = xw[:, cols], xs[:, cols]
             gw, gs = group_of(WORD_GROUPS, e), group_of(SCALE_GROUPS, e)
             ew, es = e - WORD_GROUPS[gw][0], e - SCALE_GROUPS[gs][0]
-            a_ps, b_ps = s_banks[u % 4], b_banks[u % 4]
+            b_ps = b_banks[u % 4]
             for m, acc in enumerate((a_ps, b_ps)):
                 nc.tensor.matmul_mx(out=acc[:], lhsT=words.bitcast(FP8X4), lhsT_scale=scales,
                                     rhs=up_words[m][gw][:, ew, :].bitcast(FP4X4),
-                                    rhs_scale=up_scales[gs][:, m, es, :], start=True, stop=True)
+                                    rhs_scale=up_scales[gs % 2][:, m, es, :], start=True, stop=True)
             relu_a = work.tile([P, H], F32, name="relu_a")
             nc.scalar.activation(out=relu_a[:].rearrange(as_laid, u=2, e=2),
                                  in_=a_ps[:].rearrange(by_word, u=2, e=2), func=RELU)
@@ -151,7 +154,7 @@ def tile_moe_shr_glu_relu_kernel(
 
         def turn(q, bank):
             t_ps = bank[:].rearrange("p (j u s) -> p j u s", j=2, u=2)
-            for j in range(2):
+            for j in (1, 0):
                 words = h_tiles[2 * q + j][:].bitcast(F32)
                 for u in range(2):
                     nc.tensor.transpose(t_ps[:, j, u, :], words[:, u * P:(u + 1) * P], ident[:])
@@ -189,22 +192,36 @@ def tile_moe_shr_glu_relu_kernel(
         for q in range(GATHER_LEAD):
             gather_words(q)
             gather_scales(q)
-        for q in range(PAIRS + 1):
-            up(2 * q)
-            up(2 * q + 1)
-            if q + GATHER_LEAD < PAIRS:
-                gather_words(q + GATHER_LEAD)
-                gather_scales(q + GATHER_LEAD)
+        for q in range(PAIRS):
+            up(2 * q, s_banks[(2 * q) % 4])
+            up(2 * q + 1, s_banks[(2 * q + 1) % 4])
+            if q == 2:
+                load_up_scales(2)
+                for r, pos in enumerate((pos1, pos2, pos3, pos4)):
+                    nc.sync.dma_start(pos_t[r][:], pos)
+                for g in range(6, len(WORD_GROUPS)):
+                    load_up_words(g)
+                nc.sync.dma_start(out=gate_t[:], in_=gate.rearrange("r p t -> p r t"))
             if q >= 1:
                 turn(q - 1, s_banks[(2 * q) % 4])
                 quantise(q - 1)
+            for later in range(GATHER_LEAD, PAIRS):
+                if previous_tenant(WORD_TILE, later) == q:
+                    gather_words(later)
+                if previous_tenant(SCALE_TILE, later) == q:
+                    gather_scales(later)
             if q >= 2:
                 down(q - 2, s_banks[(2 * q + 1) % 4])
 
         last = PAIRS + SHARED_PAIRS - 1
+        up(E, s_banks[0])
+        turn(PAIRS - 1, s_banks[0])
+        quantise(PAIRS - 1)
+        up(E + 1, s_banks[1])
+        down(PAIRS - 2, s_banks[1])
         down(PAIRS - 1, b_banks[0])
-        up(2 * last)
-        up(2 * last + 1)
+        up(E + 2, s_banks[2])
+        up(E + 3, s_banks[3])
         turn(last - 1, s_banks[0])
         quantise(last - 1)
         ys_ps = b_banks[1]
@@ -212,22 +229,41 @@ def tile_moe_shr_glu_relu_kernel(
         turn(last, s_banks[1])
         prod = [keep.tile([P, T], F32, name=f"prod{r}") for r in range(TOP)]
 
-        def fetch(r):
-            nc.vector.tensor_tensor(out=prod[r][:], in0=y_slots[:].indirect(pos_t[r][:]), in1=gate_t[:, r, :], op=MULT)
+        def fetch(r, cols):
+            nc.vector.tensor_tensor(out=prod[r][:, cols],
+                                    in0=y_slots[:].indirect(pos_t[r][:, cols.start // 16:cols.stop // 16]),
+                                    in1=gate_t[:, r, cols], op=MULT)
 
-        fetch(0)
+        front, back = slice(0, TURNED), slice(TURNED, T)
+        fetch(0, front)
         quantise(last)
         down_shared(last, ys_ps)
-        fetch(1)
-        sum_a = keep.tile([P, T], F32, name="sum_a")
-        sum_b = keep.tile([P, T], F32, name="sum_b")
-        nc.vector.tensor_tensor(out=sum_a[:], in0=ys_ps[:], in1=prod[0][:], op=ADD)
-        fetch(2)
-        nc.vector.tensor_tensor(out=sum_b[:], in0=sum_a[:], in1=prod[1][:], op=ADD)
-        fetch(3)
-        halves = [slice(0, T // 2), slice(T // 2, T)]
-        for cols in halves:
-            nc.vector.tensor_tensor(out=sum_a[:, cols], in0=sum_b[:, cols], in1=prod[2][:, cols], op=ADD)
-        for cols in halves:
-            nc.vector.tensor_tensor(out=sum_b[:, cols], in0=sum_a[:, cols], in1=prod[3][:, cols], op=ADD)
-            nc.sync.dma_start(out=out[:, cols], in_=sum_b[:, cols])
+        ys_sb = keep.tile([P, T], F32, name="ys_sb")
+        nc.scalar.copy(out=ys_sb[:], in_=ys_ps[:])
+        for r in range(1, TOP):
+            fetch(r, front)
+        terms = prod[:TOP - 1] + [ys_sb, prod[TOP - 1]]
+        sum_banks = [s_banks[2], s_banks[3], b_banks[2]]
+        for i, term in enumerate(terms):
+            for c, bank in enumerate(sum_banks):
+                nc.tensor.matmul(bank[:, 0:P], lhsT=term[:, c * C:(c + 1) * C], rhs=ident[:],
+                                 start=(i == 0), stop=(i == len(terms) - 1), is_transpose=True)
+        sum_t = keep.tile([P, TURNED], F32, name="sum_t")
+        result = keep.tile([P, T], F32, name="result")
+        for c, bank in enumerate(sum_banks):
+            nc.scalar.copy(out=sum_t[:, c * C:(c + 1) * C], in_=bank[:, 0:P])
+        for c in range(len(sum_banks)):
+            nc.tensor.transpose(b_banks[3][:, c * C:(c + 1) * C], sum_t[:, c * C:(c + 1) * C], ident[:])
+        nc.scalar.copy(out=result[:, front], in_=b_banks[3][:, front])
+        nc.sync.dma_start(out=out[:, front], in_=result[:, front])
+
+        part = [keep.tile([P, T - TURNED], F32, name=f"part{i}") for i in range(TOP - 1)]
+        fetch(0, back)
+        fetch(1, back)
+        nc.vector.tensor_tensor(out=part[0][:], in0=ys_sb[:, back], in1=prod[0][:, back], op=ADD)
+        fetch(2, back)
+        nc.vector.tensor_tensor(out=part[1][:], in0=part[0][:], in1=prod[1][:, back], op=ADD)
+        fetch(3, back)
+        nc.vector.tensor_tensor(out=part[2][:], in0=part[1][:], in1=prod[2][:, back], op=ADD)
+        nc.vector.tensor_tensor(out=result[:, back], in0=part[2][:], in1=prod[3][:, back], op=ADD)
+        nc.sync.dma_start(out=out[:, back], in_=result[:, back])

@@ -25,10 +25,12 @@ SHARED_PAIRS = T // (2 * C)
 WORD_GROUPS = [(e, min(e + 2, E + 1)) for e in range(0, E + 1, 2)]
 SCALE_GROUPS = [(0, 6), (6, 12), (12, 17)]
 W2_GROUPS = [(0, 6), (6, 17)]
-GATHER_LEAD = 4
+GATHER_LEAD = 3
 TURNED = 3 * C
-WORD_TILE = [0, 1, 2, 3, 0, 1, 3, 0]
-SCALE_TILE = [0, 1, 2, 3, 1, 2, 3, 1]
+TURN_ON_VECTOR = ()
+SLOTS_ON_VECTOR = (6, 7)
+WORD_TILE = [0, 1, 2, 0, 1, 2, 1, 2]
+SCALE_TILE = [0, 1, 2, 0, 2, 0, 2, 0]
 
 
 def group_of(groups, e):
@@ -94,10 +96,10 @@ def tile_moe_shr_glu_relu_kernel(
             nc.sync.dma_start(out=down_words[g][:].bitcast(I32),
                               in_=w2_words[lo:hi, 0].rearrange("e p b -> p e b").bitcast(I32))
 
-        nc.sync.dma_start(offs_t[:], offs)
+        nc.sync.dma_start(out=xw[:], in_=x_words[0].rearrange("p t r -> p (t r)").bitcast(I32))
         for r in range(4):
             nc.sync.dma_start(out=xs[:].bitcast(I32)[r:P:32, :], in_=x_scales[0, r:16:4, :].bitcast(I32))
-        nc.sync.dma_start(out=xw[:], in_=x_words[0].rearrange("p t r -> p (t r)").bitcast(I32))
+        nc.sync.dma_start(offs_t[:], offs)
         load_up_scales(0)
         load_up_words(0)
         load_up_words(1)
@@ -158,9 +160,10 @@ def tile_moe_shr_glu_relu_kernel(
                 words = h_tiles[2 * q + j][:].bitcast(F32)
                 for u in range(2):
                     nc.tensor.transpose(t_ps[:, j, u, :], words[:, u * P:(u + 1) * P], ident[:])
-            ht = work.tile([P, 2 * C * 4], BF16, name="ht", align_bytes=64)
-            nc.scalar.copy(out=ht[:].bitcast(F32).rearrange("p (j s u) -> p j s u", j=2, u=2),
-                           in_=t_ps.rearrange("p j u s -> p j s u"))
+            ht = keep.tile([P, 2 * C * 4], BF16, name="ht", tag=f"turned{q % 4}", align_bytes=64)
+            copy = nc.vector.tensor_copy if q in TURN_ON_VECTOR else nc.scalar.copy
+            copy(out=ht[:].bitcast(F32).rearrange("p (j s u) -> p j s u", j=2, u=2),
+                 in_=t_ps.rearrange("p j u s -> p j s u"))
             turned[q] = ht
 
         def quantise(q):
@@ -181,7 +184,8 @@ def tile_moe_shr_glu_relu_kernel(
                 nc.tensor.matmul_mx(out=y_ps[:, cols], lhsT=w, lhsT_scale=s,
                                     rhs=codes[:, cols].bitcast(FP8X4), rhs_scale=scales[:, cols],
                                     start=True, stop=True)
-            nc.scalar.copy(out=y_slots[:, 2 * C * q:2 * C * (q + 1)], in_=y_ps[:, 0:2 * C])
+            copy = nc.vector.tensor_copy if q in SLOTS_ON_VECTOR else nc.scalar.copy
+            copy(out=y_slots[:, 2 * C * q:2 * C * (q + 1)], in_=y_ps[:, 0:2 * C])
 
         def down_shared(q, ys_ps):
             codes, scales = quantised[q]
@@ -197,10 +201,11 @@ def tile_moe_shr_glu_relu_kernel(
             up(2 * q + 1, s_banks[(2 * q + 1) % 4])
             if q == 2:
                 load_up_scales(2)
+                load_up_words(6)
+                load_up_words(7)
+                load_up_words(8)
                 for r, pos in enumerate((pos1, pos2, pos3, pos4)):
                     nc.sync.dma_start(pos_t[r][:], pos)
-                for g in range(6, len(WORD_GROUPS)):
-                    load_up_words(g)
                 nc.sync.dma_start(out=gate_t[:], in_=gate.rearrange("r p t -> p r t"))
             if q >= 1:
                 turn(q - 1, s_banks[(2 * q) % 4])
@@ -227,7 +232,12 @@ def tile_moe_shr_glu_relu_kernel(
         ys_ps = b_banks[1]
         down_shared(last - 1, ys_ps)
         turn(last, s_banks[1])
-        prod = [keep.tile([P, T], F32, name=f"prod{r}") for r in range(TOP)]
+        quantise(last)
+        down_shared(last, ys_ps)
+        ys_sb = keep.tile([P, T], F32, name="ys_sb")
+        nc.scalar.copy(out=ys_sb[:], in_=ys_ps[:])
+        late = keep.tile([P, 2, T], F32, name="late", tag="turned1", align_bytes=64)
+        prod = [keep.tile([P, T], F32, name="prod0")[:], keep.tile([P, T], F32, name="prod1", tag="turned0", align_bytes=64)[:], late[:, 0, :], late[:, 1, :]]
 
         def fetch(r, cols):
             nc.vector.tensor_tensor(out=prod[r][:, cols],
@@ -235,13 +245,10 @@ def tile_moe_shr_glu_relu_kernel(
                                     in1=gate_t[:, r, cols], op=MULT)
 
         front, back = slice(0, TURNED), slice(TURNED, T)
-        fetch(0, front)
-        quantise(last)
-        down_shared(last, ys_ps)
-        ys_sb = keep.tile([P, T], F32, name="ys_sb")
-        nc.scalar.copy(out=ys_sb[:], in_=ys_ps[:])
-        for r in range(1, TOP):
+        for r in range(TOP - 1):
             fetch(r, front)
+        for c in range(TURNED // C):
+            fetch(TOP - 1, slice(c * C, (c + 1) * C))
         terms = prod[:TOP - 1] + [ys_sb, prod[TOP - 1]]
         sum_banks = [s_banks[2], s_banks[3], b_banks[2]]
         for i, term in enumerate(terms):
@@ -252,10 +259,10 @@ def tile_moe_shr_glu_relu_kernel(
         result = keep.tile([P, T], F32, name="result")
         for c, bank in enumerate(sum_banks):
             nc.scalar.copy(out=sum_t[:, c * C:(c + 1) * C], in_=bank[:, 0:P])
-        for c in range(len(sum_banks)):
-            nc.tensor.transpose(b_banks[3][:, c * C:(c + 1) * C], sum_t[:, c * C:(c + 1) * C], ident[:])
-        nc.scalar.copy(out=result[:, front], in_=b_banks[3][:, front])
-        nc.sync.dma_start(out=out[:, front], in_=result[:, front])
+        for c, bank in enumerate((b_banks[3], s_banks[0], s_banks[1])):
+            nc.tensor.transpose(bank[:, 0:C], sum_t[:, c * C:(c + 1) * C], ident[:])
+            nc.scalar.copy(out=result[:, c * C:(c + 1) * C], in_=bank[:, 0:C])
+        nc.scalar.dma_start(out=out[:, front], in_=result[:, front])
 
         part = [keep.tile([P, T - TURNED], F32, name=f"part{i}") for i in range(TOP - 1)]
         fetch(0, back)

@@ -24,7 +24,7 @@ PAIRS = E // 2
 SHARED_PAIRS = T // (2 * C)
 WORD_GROUPS = [(e, min(e + 2, E + 1)) for e in range(0, E + 1, 2)]
 SCALE_GROUPS = [(0, 6), (6, 12), (12, 17)]
-W2_GROUPS = [(0, 6), (6, 17)]
+W2_GROUPS = [(0, 6), (6, 12), (12, 17)]
 GATHER_LEAD = 3
 TURNED = 3 * C
 TURN_ON_VECTOR = ()
@@ -63,7 +63,7 @@ def tile_moe_shr_glu_relu_kernel(
         down_words = [keep.tile([P, hi - lo, 2 * N], U8, name=f"down_words{g}", align_bytes=64)
                       for g, (lo, hi) in enumerate(W2_GROUPS)]
         down_scales = keep.tile([P, E + 1, N], U8, name="down_scales", align_bytes=64)
-        gate_t = keep.tile([P, TOP, T], F32, name="gate_t")
+        gate_t = [keep.tile([P, T], F32, name=f"gate_t{r}") for r in range(TOP)]
         y_slots = keep.tile([P, E * C], F32, name="y_slots")
         ident = keep.tile([P, P], F32, name="ident")
         warm = keep.tile([P, 8], F32, name="warm")
@@ -100,8 +100,8 @@ def tile_moe_shr_glu_relu_kernel(
         for r in range(4):
             nc.sync.dma_start(out=xs[:].bitcast(I32)[r:P:32, :], in_=x_scales[0, r:16:4, :].bitcast(I32))
         nc.sync.dma_start(offs_t[:], offs)
-        load_up_scales(0)
         load_up_words(0)
+        load_up_scales(0)
         load_up_words(1)
         load_down_words(0)
         load_up_words(2)
@@ -203,10 +203,11 @@ def tile_moe_shr_glu_relu_kernel(
                 load_up_scales(2)
                 load_up_words(6)
                 load_up_words(7)
+                load_down_words(2)
                 load_up_words(8)
                 for r, pos in enumerate((pos1, pos2, pos3, pos4)):
                     nc.sync.dma_start(pos_t[r][:], pos)
-                nc.sync.dma_start(out=gate_t[:], in_=gate.rearrange("r p t -> p r t"))
+                    nc.sync.dma_start(out=gate_t[r][:], in_=gate[r])
             if q >= 1:
                 turn(q - 1, s_banks[(2 * q) % 4])
                 quantise(q - 1)
@@ -242,7 +243,7 @@ def tile_moe_shr_glu_relu_kernel(
         def fetch(r, cols):
             nc.vector.tensor_tensor(out=prod[r][:, cols],
                                     in0=y_slots[:].indirect(pos_t[r][:, cols.start // 16:cols.stop // 16]),
-                                    in1=gate_t[:, r, cols], op=MULT)
+                                    in1=gate_t[r][:, cols], op=MULT)
 
         front, back = slice(0, TURNED), slice(TURNED, T)
         for r in range(TOP - 1):

@@ -21,24 +21,18 @@ RELU = mybir.ActivationFunctionType.Relu
 
 P = 128
 PAIRS = E // 2
-SHARED_PAIRS = T // (2 * C)
+WINDOW = 704
+QUAD = 4 * C
 WORD_GROUPS = [(e, min(e + 2, E + 1)) for e in range(0, E + 1, 2)]
 SCALE_GROUPS = [(0, 6), (6, 12), (12, 17)]
 W2_GROUPS = [(0, 6), (6, 12), (12, 17)]
-GATHER_LEAD = 3
-TURNED = 3 * C
-TURN_ON_VECTOR = ()
-SLOTS_ON_VECTOR = (6, 7)
-WORD_TILE = [0, 1, 2, 0, 1, 2, 1, 2]
-SCALE_TILE = [0, 1, 2, 0, 2, 0, 2, 0]
+QUANT_GROUPS = [(0, 2), (2, 4), (4, 6), (6, 7), (7, 8), (8, 10)]
+WORD_PLACE = [0, 4, 0, 4]
+SCALE_PLACE = [0, 4, 2, 0]
 
 
 def group_of(groups, e):
     return [g for g, (lo, hi) in enumerate(groups) if lo <= e < hi][0]
-
-
-def previous_tenant(tiles, q):
-    return max(p for p in range(q) if tiles[p] == tiles[q])
 
 
 def tile_moe_shr_glu_relu_kernel(
@@ -49,13 +43,12 @@ def tile_moe_shr_glu_relu_kernel(
     with ExitStack() as ctx:
         lists = ctx.enter_context(tc.tile_pool(name="lists", bufs=1))
         keep = ctx.enter_context(tc.tile_pool(name="keep", bufs=1))
-        work = ctx.enter_context(tc.tile_pool(name="work", bufs=4))
         psum = ctx.enter_context(tc.psum_pool(name="psum", bufs=1))
 
         offs_t = lists.tile([P, E * C // 16], U16, name="offs_t")
         pos_t = [lists.tile([P, T // 16], U16, name=f"pos_t{r}") for r in range(TOP)]
-        xw = keep.tile([P, T], I32, name="xw", align_bytes=64)
-        xs = keep.tile([P, T], U8, name="xs", align_bytes=64)
+        xw = keep.tile([P, WINDOW], I32, name="xw", align_bytes=64)
+        xs = keep.tile([P, WINDOW], U8, name="xs", align_bytes=64)
         up_words = [[keep.tile([P, hi - lo, 2 * H], U8, name=f"up_words{m}_{g}", align_bytes=64)
                      for g, (lo, hi) in enumerate(WORD_GROUPS)] for m in range(2)]
         up_scales = [keep.tile([P, 2, hi - lo, H], U8, name=f"up_scales{g}", align_bytes=64)
@@ -66,15 +59,14 @@ def tile_moe_shr_glu_relu_kernel(
         gate_t = [keep.tile([P, T], F32, name=f"gate_t{r}") for r in range(TOP)]
         y_slots = keep.tile([P, E * C], F32, name="y_slots")
         ident = keep.tile([P, P], F32, name="ident")
-        warm = keep.tile([P, 8], F32, name="warm")
 
         nc.gpsimd.memset(xs[:].bitcast(I32), 0)
+        nc.gpsimd.memset(xw[:, T:], 0)
         nc.vector.memset(up_scales[0][:, 0].bitcast(I32), 0)
         nc.vector.memset(up_scales[0][:, 1].bitcast(I32), 0)
         nc.vector.memset(down_scales[:].bitcast(I32), 0)
-        nc.vector.memset(up_scales[1][:].bitcast(I32), 0)
+        nc.gpsimd.memset(up_scales[1][:].bitcast(I32), 0)
         make_identity(nc, ident[:])
-        nc.scalar.activation(out=warm[:], in_=ident[:, 0:8], func=RELU)
         s_banks = [psum.tile([P, H], F32, name=f"s_bank{b}") for b in range(4)]
         b_banks = [psum.tile([P, H], F32, name=f"b_bank{b}") for b in range(4)]
 
@@ -96,9 +88,9 @@ def tile_moe_shr_glu_relu_kernel(
             nc.sync.dma_start(out=down_words[g][:].bitcast(I32),
                               in_=w2_words[lo:hi, 0].rearrange("e p b -> p e b").bitcast(I32))
 
-        nc.sync.dma_start(out=xw[:], in_=x_words[0].rearrange("p t r -> p (t r)").bitcast(I32))
+        nc.sync.dma_start(out=xw[:, 0:T], in_=x_words[0].rearrange("p t r -> p (t r)").bitcast(I32))
         for r in range(4):
-            nc.sync.dma_start(out=xs[:].bitcast(I32)[r:P:32, :], in_=x_scales[0, r:16:4, :].bitcast(I32))
+            nc.sync.dma_start(out=xs[:].bitcast(I32)[r:P:32, 0:T // 4], in_=x_scales[0, r:16:4, :].bitcast(I32))
         nc.sync.dma_start(offs_t[:], offs)
         load_up_words(0)
         load_up_scales(0)
@@ -114,26 +106,30 @@ def tile_moe_shr_glu_relu_kernel(
         load_down_words(1)
         load_up_words(5)
 
-        slot_words = [keep.tile([P, 2 * C], U32, name=f"slot_words{q}", align_bytes=64) for q in range(GATHER_LEAD)]
-        slot_scales = [keep.tile([P, 2 * C], U8, name=f"slot_scales{q}", align_bytes=64) for q in range(GATHER_LEAD)]
+        slot_words = keep.tile([P, 2 * QUAD], U32, name="slot_words", align_bytes=64)
+        slot_scales = keep.tile([P, 2 * QUAD], U8, name="slot_scales", align_bytes=64)
 
-        def gather_words(q):
-            nc.vector.tensor_copy(out=slot_words[WORD_TILE[q]][:],
-                                  in_=xw[:].bitcast(U32).indirect(offs_t[:, 16 * q:16 * (q + 1)]))
+        def gather_words(g):
+            at = WORD_PLACE[g] * C
+            nc.vector.tensor_copy(out=slot_words[:, at:at + QUAD],
+                                  in_=xw[:].bitcast(U32).indirect(offs_t[:, 32 * g:32 * (g + 1)]))
 
-        def gather_scales(q):
-            nc.vector.tensor_copy(out=slot_scales[SCALE_TILE[q]][:], in_=xs[:].indirect(offs_t[:, 16 * q:16 * (q + 1)]))
+        def gather_scales(g):
+            at = SCALE_PLACE[g] * C
+            nc.vector.tensor_copy(out=slot_scales[:, at:at + QUAD], in_=xs[:].indirect(offs_t[:, 32 * g:32 * (g + 1)]))
 
         by_word = "s (p u e) -> s u p e"
         as_laid = "s (u p e) -> s u p e"
-        h_tiles, turned, quantised = {}, {}, {}
+        h_tiles, quantised = {}, {}
+        turned = [keep.tile([P, (hi - lo) * 2 * H], BF16, name=f"turned{g}", tag=f"turned{g}", align_bytes=64)
+                  for g, (lo, hi) in enumerate(QUANT_GROUPS)]
 
         def up(u, a_ps):
-            q, j = divmod(u, 2)
-            if q < PAIRS:
+            if u < E:
                 e = u
-                cols = slice(j * C, (j + 1) * C)
-                words, scales = slot_words[WORD_TILE[q]][:, cols], slot_scales[SCALE_TILE[q]][:, cols]
+                g, j = divmod(u, 4)
+                wa, sa = (WORD_PLACE[g] + j) * C, (SCALE_PLACE[g] + j) * C
+                words, scales = slot_words[:, wa:wa + C], slot_scales[:, sa:sa + C]
             else:
                 e = E
                 cols = slice((u - E) * C, (u - E + 1) * C)
@@ -141,14 +137,14 @@ def tile_moe_shr_glu_relu_kernel(
             gw, gs = group_of(WORD_GROUPS, e), group_of(SCALE_GROUPS, e)
             ew, es = e - WORD_GROUPS[gw][0], e - SCALE_GROUPS[gs][0]
             b_ps = b_banks[u % 4]
-            for m, acc in enumerate((a_ps, b_ps)):
+            for m, acc in ((1, b_ps), (0, a_ps)):
                 nc.tensor.matmul_mx(out=acc[:], lhsT=words.bitcast(FP8X4), lhsT_scale=scales,
                                     rhs=up_words[m][gw][:, ew, :].bitcast(FP4X4),
                                     rhs_scale=up_scales[gs % 2][:, m, es, :], start=True, stop=True)
-            relu_a = work.tile([P, H], F32, name="relu_a")
+            relu_a = keep.tile([P, H], F32, name=f"relu_a{u}")
             nc.scalar.activation(out=relu_a[:].rearrange(as_laid, u=2, e=2),
                                  in_=a_ps[:].rearrange(by_word, u=2, e=2), func=RELU)
-            h = work.tile([P, H], BF16, name="h", align_bytes=64)
+            h = keep.tile([P, H], BF16, name=f"h{u}", align_bytes=64)
             nc.vector.tensor_tensor(out=h[:].rearrange(as_laid, u=2, e=2),
                                     in0=b_ps[:].rearrange(by_word, u=2, e=2),
                                     in1=relu_a[:].rearrange(as_laid, u=2, e=2), op=MULT)
@@ -160,42 +156,36 @@ def tile_moe_shr_glu_relu_kernel(
                 words = h_tiles[2 * q + j][:].bitcast(F32)
                 for u in range(2):
                     nc.tensor.transpose(t_ps[:, j, u, :], words[:, u * P:(u + 1) * P], ident[:])
-            ht = keep.tile([P, 2 * C * 4], BF16, name="ht", tag=f"turned{q % 4}", align_bytes=64)
-            copy = nc.vector.tensor_copy if q in TURN_ON_VECTOR else nc.scalar.copy
-            copy(out=ht[:].bitcast(F32).rearrange("p (j s u) -> p j s u", j=2, u=2),
-                 in_=t_ps.rearrange("p j u s -> p j s u"))
-            turned[q] = ht
+            g = group_of(QUANT_GROUPS, q)
+            at = (q - QUANT_GROUPS[g][0]) * H
+            nc.scalar.copy(out=turned[g][:].bitcast(F32)[:, at:at + H].rearrange("p (j s u) -> p j s u", j=2, u=2),
+                           in_=t_ps.rearrange("p j u s -> p j s u"))
 
-        def quantise(q):
-            codes = work.tile([P, 2 * C], U32, name="codes", align_bytes=64)
-            scales = work.tile([P, 2 * C], U8, name="scales", align_bytes=64)
-            nc.vector.quantize_mx(out=codes[:].bitcast(FP8X4), scales=scales[:], in_=turned[q][:])
-            quantised[q] = (codes, scales)
+        def quantise(g):
+            lo, hi = QUANT_GROUPS[g]
+            codes = keep.tile([P, (hi - lo) * 2 * C], U32, name=f"codes{g}", align_bytes=64)
+            scales = keep.tile([P, (hi - lo) * 2 * C], U8, name=f"scales{g}", align_bytes=64)
+            nc.vector.quantize_mx(out=codes[:].bitcast(FP8X4), scales=scales[:], in_=turned[g][:])
+            quantised[g] = (codes, scales)
 
         def down_weights(e):
             g = group_of(W2_GROUPS, e)
             return down_words[g][:, e - W2_GROUPS[g][0], :].bitcast(FP4X4), down_scales[:, e, :]
 
-        def down(q, y_ps):
-            codes, scales = quantised[q]
-            for j in range(2):
+        def down(g, y_ps):
+            codes, scales = quantised[g]
+            lo, hi = QUANT_GROUPS[g]
+            for j in range(2 * (hi - lo)):
                 cols = slice(j * C, (j + 1) * C)
-                w, s = down_weights(2 * q + j)
+                w, s = down_weights(2 * lo + j)
                 nc.tensor.matmul_mx(out=y_ps[:, cols], lhsT=w, lhsT_scale=s,
                                     rhs=codes[:, cols].bitcast(FP8X4), rhs_scale=scales[:, cols],
                                     start=True, stop=True)
-            copy = nc.vector.tensor_copy if q in SLOTS_ON_VECTOR else nc.scalar.copy
-            copy(out=y_slots[:, 2 * C * q:2 * C * (q + 1)], in_=y_ps[:, 0:2 * C])
+            nc.scalar.copy(out=y_slots[:, 2 * C * lo:2 * C * hi], in_=y_ps[:, 0:2 * C * (hi - lo)])
 
-        def down_shared(q, ys_ps):
-            codes, scales = quantised[q]
-            w, s = down_weights(E)
-            nc.tensor.matmul_mx(out=ys_ps[:, 2 * C * (q - PAIRS):2 * C * (q - PAIRS + 1)], lhsT=w, lhsT_scale=s,
-                                rhs=codes[:].bitcast(FP8X4), rhs_scale=scales[:], start=True, stop=True)
-
-        for q in range(GATHER_LEAD):
-            gather_words(q)
-            gather_scales(q)
+        for g in range(2):
+            gather_words(g)
+            gather_scales(g)
         for q in range(PAIRS):
             up(2 * q, s_banks[(2 * q) % 4])
             up(2 * q + 1, s_banks[(2 * q + 1) % 4])
@@ -208,70 +198,72 @@ def tile_moe_shr_glu_relu_kernel(
                 for r, pos in enumerate((pos1, pos2, pos3, pos4)):
                     nc.sync.dma_start(pos_t[r][:], pos)
                     nc.sync.dma_start(out=gate_t[r][:], in_=gate[r])
-            if q >= 1:
-                turn(q - 1, s_banks[(2 * q) % 4])
-                quantise(q - 1)
-            for later in range(GATHER_LEAD, PAIRS):
-                if previous_tenant(WORD_TILE, later) == q:
-                    gather_words(later)
-                if previous_tenant(SCALE_TILE, later) == q:
-                    gather_scales(later)
             if q >= 2:
-                down(q - 2, s_banks[(2 * q + 1) % 4])
+                turn(q - 2, s_banks[(2 * q) % 4])
+                if q % 2 == 1:
+                    quantise(group_of(QUANT_GROUPS, q - 2))
+            if q in (1, 3):
+                gather_words((q + 3) // 2)
+            if q in (2, 4):
+                gather_scales((q + 2) // 2)
+            if q >= 4 and q % 2 == 0:
+                down((q - 4) // 2, s_banks[(2 * q + 1) % 4])
 
-        last = PAIRS + SHARED_PAIRS - 1
         up(E, s_banks[0])
-        turn(PAIRS - 1, s_banks[0])
-        quantise(PAIRS - 1)
         up(E + 1, s_banks[1])
-        down(PAIRS - 2, s_banks[1])
-        down(PAIRS - 1, b_banks[0])
+        turn(PAIRS - 2, s_banks[0])
+        quantise(3)
+        turn(PAIRS - 1, s_banks[1])
+        quantise(4)
+        down(2, b_banks[0])
         up(E + 2, s_banks[2])
+        down(3, s_banks[0])
         up(E + 3, s_banks[3])
-        turn(last - 1, s_banks[0])
-        quantise(last - 1)
-        ys_ps = b_banks[1]
-        down_shared(last - 1, ys_ps)
-        turn(last, s_banks[1])
-        quantise(last)
-        down_shared(last, ys_ps)
-        ys_sb = keep.tile([P, T], F32, name="ys_sb")
-        nc.scalar.copy(out=ys_sb[:], in_=ys_ps[:])
-        late = keep.tile([P, 2, T], F32, name="late", tag="turned1", align_bytes=64)
-        prod = [keep.tile([P, T], F32, name="prod0")[:], keep.tile([P, T], F32, name="prod1", tag="turned0", align_bytes=64)[:], late[:, 0, :], late[:, 1, :]]
+        down(4, s_banks[1])
+        turn(PAIRS, s_banks[1])
+        turn(PAIRS + 1, s_banks[0])
+        quantise(5)
+
+        late = keep.tile([P, 2, T], F32, name="late", tag="turned5", align_bytes=64)
+        prod = [keep.tile([P, T], F32, name="prod0")[:], keep.tile([P, T], F32, name="prod1")[:],
+                late[:, 0, :], late[:, 1, :]]
+        halves = [slice(0, T // 2), slice(T // 2, T)]
+        sum_banks = [s_banks[2], s_banks[3], b_banks[2], b_banks[3]]
 
         def fetch(r, cols):
             nc.vector.tensor_tensor(out=prod[r][:, cols],
                                     in0=y_slots[:].indirect(pos_t[r][:, cols.start // 16:cols.stop // 16]),
                                     in1=gate_t[r][:, cols], op=MULT)
 
-        front, back = slice(0, TURNED), slice(TURNED, T)
-        for r in range(TOP - 1):
-            fetch(r, front)
-        for c in range(TURNED // C):
-            fetch(TOP - 1, slice(c * C, (c + 1) * C))
-        terms = prod[:TOP - 1] + [ys_sb, prod[TOP - 1]]
-        sum_banks = [s_banks[2], s_banks[3], b_banks[2]]
-        for i, term in enumerate(terms):
-            for c, bank in enumerate(sum_banks):
-                nc.tensor.matmul(bank[:, 0:P], lhsT=term[:, c * C:(c + 1) * C], rhs=ident[:],
-                                 start=(i == 0), stop=(i == len(terms) - 1), is_transpose=True)
-        sum_t = keep.tile([P, TURNED], F32, name="sum_t")
-        result = keep.tile([P, T], F32, name="result")
-        for c, bank in enumerate(sum_banks):
-            nc.scalar.copy(out=sum_t[:, c * C:(c + 1) * C], in_=bank[:, 0:P])
-        for c, bank in enumerate((b_banks[3], s_banks[0], s_banks[1])):
-            nc.tensor.transpose(bank[:, 0:C], sum_t[:, c * C:(c + 1) * C], ident[:])
-            nc.scalar.copy(out=result[:, c * C:(c + 1) * C], in_=bank[:, 0:C])
-        nc.scalar.dma_start(out=out[:, front], in_=result[:, front])
+        def add_turned(r, chunks):
+            for c in chunks:
+                nc.tensor.matmul(sum_banks[c][:, 0:P], lhsT=prod[r][:, c * C:(c + 1) * C], rhs=ident[:],
+                                 start=(r == 0), stop=(r == TOP - 2), is_transpose=True)
 
-        part = [keep.tile([P, T - TURNED], F32, name=f"part{i}") for i in range(TOP - 1)]
-        fetch(0, back)
-        fetch(1, back)
-        nc.vector.tensor_tensor(out=part[0][:], in0=ys_sb[:, back], in1=prod[0][:, back], op=ADD)
-        fetch(2, back)
-        nc.vector.tensor_tensor(out=part[1][:], in0=part[0][:], in1=prod[1][:, back], op=ADD)
-        fetch(3, back)
-        nc.vector.tensor_tensor(out=part[2][:], in0=part[1][:], in1=prod[2][:, back], op=ADD)
-        nc.vector.tensor_tensor(out=result[:, back], in0=part[2][:], in1=prod[3][:, back], op=ADD)
-        nc.sync.dma_start(out=out[:, back], in_=result[:, back])
+        for r in range(2):
+            fetch(r, slice(0, T))
+            add_turned(r, range(4))
+        codes, scales = quantised[5]
+        w, s = down_weights(E)
+        for c in range(4):
+            cols = slice(c * C, (c + 1) * C)
+            nc.tensor.matmul_mx(out=b_banks[1][:, cols], lhsT=codes[:, cols].bitcast(FP8X4), lhsT_scale=scales[:, cols],
+                                rhs=w, rhs_scale=s, start=True, stop=True)
+        ys_t = keep.tile([P, T], F32, name="ys_t")
+        nc.scalar.copy(out=ys_t[:], in_=b_banks[1][:])
+        sum_t = keep.tile([P, T], F32, name="sum_t")
+        result = [keep.tile([P, T // 2], F32, name=f"result{i}") for i in range(2)]
+        for i, half in enumerate(halves):
+            fetch(2, half)
+            add_turned(2, (2 * i, 2 * i + 1))
+            for c in (2 * i, 2 * i + 1):
+                nc.scalar.copy(out=sum_t[:, c * C:(c + 1) * C], in_=sum_banks[c][:, 0:P])
+        for i, half in enumerate(halves):
+            fetch(3, half)
+            for c in (2 * i, 2 * i + 1):
+                for k, term in enumerate((ys_t, sum_t)):
+                    nc.tensor.matmul(s_banks[i][:, (c % 2) * C:(c % 2 + 1) * C], lhsT=term[:, c * C:(c + 1) * C],
+                                     rhs=ident[:], start=(k == 0), stop=(k == 1), is_transpose=True)
+        for i, half in enumerate(halves):
+            nc.vector.tensor_tensor(out=result[i][:], in0=s_banks[i][:, 0:T // 2], in1=prod[3][:, half], op=ADD)
+            nc.sync.dma_start(out=out[:, half], in_=result[i][:])

@@ -25,14 +25,22 @@ WINDOW = 704
 QUAD = 4 * C
 WORD_GROUPS = [(e, min(e + 2, E + 1)) for e in range(0, E + 1, 2)]
 SCALE_GROUPS = [(0, 6), (6, 12), (12, 17)]
-W2_GROUPS = [(0, 6), (6, 12), (12, 17)]
-QUANT_GROUPS = [(0, 2), (2, 4), (4, 6), (6, 7), (7, 8), (8, 10)]
-WORD_PLACE = [0, 4, 0, 4]
-SCALE_PLACE = [0, 4, 2, 0]
+W2_GROUPS = [(e, e + 2) for e in range(0, 12, 2)] + [(12, 17)]
+QUANT_GROUPS = [(q, q + 1) for q in range(PAIRS + 2)]
+WORD_GATHERS = [(0, 2, 0), (2, 4, 2), (4, 6, 4), (6, 8, 6), (8, 10, 0), (10, 12, 2), (12, 14, 4), (14, 16, 6)]
+SCALE_GATHERS = [(0, 2, 0), (2, 4, 2), (4, 6, 4), (6, 8, 6), (8, 10, 0), (10, 12, 2), (12, 14, 4), (14, 16, 6)]
 
 
 def group_of(groups, e):
     return [g for g, (lo, hi) in enumerate(groups) if lo <= e < hi][0]
+
+
+def place_of(gathers, e):
+    return [at + e - lo for lo, hi, at in gathers if lo <= e < hi][0]
+
+
+def last_tenant(gathers, lo, hi, at):
+    return max([p for p in range(lo) if at <= place_of(gathers, p) < at + hi - lo] + [-1])
 
 
 def tile_moe_shr_glu_relu_kernel(
@@ -51,8 +59,8 @@ def tile_moe_shr_glu_relu_kernel(
         xs = keep.tile([P, WINDOW], U8, name="xs", align_bytes=64)
         up_words = [[keep.tile([P, hi - lo, 2 * H], U8, name=f"up_words{m}_{g}", align_bytes=64)
                      for g, (lo, hi) in enumerate(WORD_GROUPS)] for m in range(2)]
-        up_scales = [keep.tile([P, 2, hi - lo, H], U8, name=f"up_scales{g}", align_bytes=64)
-                     for g, (lo, hi) in enumerate(SCALE_GROUPS[:2])]
+        up_scales = [[keep.tile([P, hi - lo, H], U8, name=f"up_scales{m}_{g}", align_bytes=64)
+                      for g, (lo, hi) in enumerate(SCALE_GROUPS[:2])] for m in range(2)]
         down_words = [keep.tile([P, hi - lo, 2 * N], U8, name=f"down_words{g}", align_bytes=64)
                       for g, (lo, hi) in enumerate(W2_GROUPS)]
         down_scales = keep.tile([P, E + 1, N], U8, name="down_scales", align_bytes=64)
@@ -62,26 +70,33 @@ def tile_moe_shr_glu_relu_kernel(
 
         nc.gpsimd.memset(xs[:].bitcast(I32), 0)
         nc.gpsimd.memset(xw[:, T:], 0)
-        nc.vector.memset(up_scales[0][:, 0].bitcast(I32), 0)
-        nc.vector.memset(up_scales[0][:, 1].bitcast(I32), 0)
-        nc.vector.memset(down_scales[:].bitcast(I32), 0)
-        nc.gpsimd.memset(up_scales[1][:].bitcast(I32), 0)
+        nc.vector.memset(up_scales[0][0][:].bitcast(I32), 0)
+        nc.vector.memset(up_scales[1][0][:].bitcast(I32), 0)
+        nc.vector.memset(up_scales[0][1][:].bitcast(I32), 0)
+        nc.gpsimd.memset(down_scales[:].bitcast(I32), 0)
+        nc.gpsimd.memset(up_scales[1][1][:].bitcast(I32), 0)
         make_identity(nc, ident[:])
+        warm = keep.tile([P, 8], F32, name="warm")
+        nc.scalar.activation(out=warm[:], in_=ident[:, 0:8], func=RELU)
         s_banks = [psum.tile([P, H], F32, name=f"s_bank{b}") for b in range(4)]
-        b_banks = [psum.tile([P, H], F32, name=f"b_bank{b}") for b in range(4)]
+        b_banks = [psum.tile([P, H], F32, name=f"b_bank{b}") for b in range(3)]
+        y_bank = psum.tile([P, H], F32, name="y_bank")
 
-        def load_up_words(g):
+        def load_up_words(m, g):
             lo, hi = WORD_GROUPS[g]
-            for m, w in enumerate((w1_words, w3_words)):
-                nc.sync.dma_start(out=up_words[m][g][:].bitcast(I32),
-                                  in_=w[lo:hi, 0].rearrange("e p b -> p e b").bitcast(I32))
+            nc.sync.dma_start(out=up_words[m][g][:].bitcast(I32),
+                              in_=(w1_words, w3_words)[m][lo:hi, 0].rearrange("e p b -> p e b").bitcast(I32))
 
-        def load_up_scales(g):
+        def load_up_scales(m, g):
             lo, hi = SCALE_GROUPS[g]
-            for m, s in enumerate((w1_scales, w3_scales)):
-                for r in range(4):
-                    nc.sync.dma_start(out=up_scales[g % 2][:].bitcast(I32)[r:P:32, m, 0:hi - lo],
-                                      in_=s[lo:hi, 0, r:16:4, :].rearrange("e q i -> q e i").bitcast(I32))
+            for r in range(4):
+                nc.sync.dma_start(out=up_scales[m][g % 2][:].bitcast(I32)[r:P:32, 0:hi - lo],
+                                  in_=(w1_scales, w3_scales)[m][lo:hi, 0, r:16:4, :].rearrange("e q i -> q e i").bitcast(I32))
+
+        def load_down_scales():
+            for r in range(4):
+                nc.sync.dma_start(out=down_scales[:].bitcast(I32)[r:P:32],
+                                  in_=w2_scales[:, 0, r:16:4, :].rearrange("e q n -> q e n").bitcast(I32))
 
         def load_down_words(g):
             lo, hi = W2_GROUPS[g]
@@ -92,63 +107,69 @@ def tile_moe_shr_glu_relu_kernel(
         for r in range(4):
             nc.sync.dma_start(out=xs[:].bitcast(I32)[r:P:32, 0:T // 4], in_=x_scales[0, r:16:4, :].bitcast(I32))
         nc.sync.dma_start(offs_t[:], offs)
-        load_up_words(0)
-        load_up_scales(0)
-        load_up_words(1)
+        load_up_words(0, 0)
+        load_up_words(0, 1)
+        load_up_scales(0, 0)
+        load_up_scales(1, 0)
+        load_up_words(0, 2)
+        load_up_words(1, 0)
+        load_up_scales(0, 1)
+        load_up_words(0, 3)
+        load_up_words(1, 1)
+        load_down_scales()
+        load_up_words(0, 4)
+        load_up_words(1, 2)
         load_down_words(0)
-        load_up_words(2)
-        for r in range(4):
-            nc.sync.dma_start(out=down_scales[:].bitcast(I32)[r:P:32],
-                              in_=w2_scales[:, 0, r:16:4, :].rearrange("e q n -> q e n").bitcast(I32))
-        load_up_scales(1)
-        load_up_words(3)
-        load_up_words(4)
+        load_up_scales(1, 1)
+        load_up_words(0, 5)
+        load_up_words(1, 3)
         load_down_words(1)
-        load_up_words(5)
 
-        slot_words = keep.tile([P, 2 * QUAD], U32, name="slot_words", align_bytes=64)
-        slot_scales = keep.tile([P, 2 * QUAD], U8, name="slot_scales", align_bytes=64)
+        slot_words = keep.tile([P, max(at + hi - lo for lo, hi, at in WORD_GATHERS) * C], U32, name="slot_words", align_bytes=64)
+        slot_scales = keep.tile([P, max(at + hi - lo for lo, hi, at in SCALE_GATHERS) * C], U8, name="slot_scales", align_bytes=64)
 
-        def gather_words(g):
-            at = WORD_PLACE[g] * C
-            nc.vector.tensor_copy(out=slot_words[:, at:at + QUAD],
-                                  in_=xw[:].bitcast(U32).indirect(offs_t[:, 32 * g:32 * (g + 1)]))
-
-        def gather_scales(g):
-            at = SCALE_PLACE[g] * C
-            nc.vector.tensor_copy(out=slot_scales[:, at:at + QUAD], in_=xs[:].indirect(offs_t[:, 32 * g:32 * (g + 1)]))
+        def gather_after(experts):
+            for (lo, hi, at), (slo, shi, sat) in zip(WORD_GATHERS, SCALE_GATHERS):
+                if last_tenant(WORD_GATHERS, lo, hi, at) in experts:
+                    nc.vector.tensor_copy(out=slot_words[:, at * C:(at + hi - lo) * C],
+                                          in_=xw[:].bitcast(U32).indirect(offs_t[:, 8 * lo:8 * hi]))
+                if last_tenant(SCALE_GATHERS, slo, shi, sat) in experts:
+                    nc.vector.tensor_copy(out=slot_scales[:, sat * C:(sat + shi - slo) * C],
+                                          in_=xs[:].indirect(offs_t[:, 8 * slo:8 * shi]))
 
         by_word = "s (p u e) -> s u p e"
         as_laid = "s (u p e) -> s u p e"
-        h_tiles, quantised = {}, {}
+        relu_tiles, h_tiles, quantised = {}, {}, {}
         turned = [keep.tile([P, (hi - lo) * 2 * H], BF16, name=f"turned{g}", tag=f"turned{g}", align_bytes=64)
                   for g, (lo, hi) in enumerate(QUANT_GROUPS)]
 
-        def up(u, a_ps):
+        def first_layer(m, u, acc):
             if u < E:
                 e = u
-                g, j = divmod(u, 4)
-                wa, sa = (WORD_PLACE[g] + j) * C, (SCALE_PLACE[g] + j) * C
+                wa, sa = place_of(WORD_GATHERS, e) * C, place_of(SCALE_GATHERS, e) * C
                 words, scales = slot_words[:, wa:wa + C], slot_scales[:, sa:sa + C]
             else:
                 e = E
                 cols = slice((u - E) * C, (u - E + 1) * C)
                 words, scales = xw[:, cols], xs[:, cols]
             gw, gs = group_of(WORD_GROUPS, e), group_of(SCALE_GROUPS, e)
-            ew, es = e - WORD_GROUPS[gw][0], e - SCALE_GROUPS[gs][0]
-            b_ps = b_banks[u % 4]
-            for m, acc in ((1, b_ps), (0, a_ps)):
-                nc.tensor.matmul_mx(out=acc[:], lhsT=words.bitcast(FP8X4), lhsT_scale=scales,
-                                    rhs=up_words[m][gw][:, ew, :].bitcast(FP4X4),
-                                    rhs_scale=up_scales[gs % 2][:, m, es, :], start=True, stop=True)
-            relu_a = keep.tile([P, H], F32, name=f"relu_a{u}")
-            nc.scalar.activation(out=relu_a[:].rearrange(as_laid, u=2, e=2),
+            nc.tensor.matmul_mx(out=acc[:], lhsT=words.bitcast(FP8X4), lhsT_scale=scales,
+                                rhs=up_words[m][gw][:, e - WORD_GROUPS[gw][0], :].bitcast(FP4X4),
+                                rhs_scale=up_scales[m][gs % 2][:, e - SCALE_GROUPS[gs][0], :], start=True, stop=True)
+
+        def gate_side(u, a_ps):
+            first_layer(0, u, a_ps)
+            relu_tiles[u] = keep.tile([P, H], F32, name=f"relu_a{u}")
+            nc.scalar.activation(out=relu_tiles[u][:].rearrange(as_laid, u=2, e=2),
                                  in_=a_ps[:].rearrange(by_word, u=2, e=2), func=RELU)
-            h = keep.tile([P, H], BF16, name=f"h{u}", align_bytes=64)
-            nc.vector.tensor_tensor(out=h[:].rearrange(as_laid, u=2, e=2),
+
+        def value_side(u):
+            b_ps = b_banks[u % 3]
+            first_layer(1, u, b_ps)
+            h_tiles[u] = keep.tile([P, H], BF16, name=f"h{u}", align_bytes=64)
+            nc.vector.tensor_tensor(out=h_tiles[u][:].rearrange(as_laid, u=2, e=2),
                                     in0=b_ps[:].rearrange(by_word, u=2, e=2),
-                                    in1=relu_a[:].rearrange(as_laid, u=2, e=2), op=MULT)
-            h_tiles[u] = h
+                                    in1=relu_tiles[u][:].rearrange(as_laid, u=2, e=2), op=MULT)
 
         def turn(q, bank):
             t_ps = bank[:].rearrange("p (j u s) -> p j u s", j=2, u=2)
@@ -172,7 +193,7 @@ def tile_moe_shr_glu_relu_kernel(
             g = group_of(W2_GROUPS, e)
             return down_words[g][:, e - W2_GROUPS[g][0], :].bitcast(FP4X4), down_scales[:, e, :]
 
-        def down(g, y_ps):
+        def down(g, y_ps, copy):
             codes, scales = quantised[g]
             lo, hi = QUANT_GROUPS[g]
             for j in range(2 * (hi - lo)):
@@ -181,54 +202,66 @@ def tile_moe_shr_glu_relu_kernel(
                 nc.tensor.matmul_mx(out=y_ps[:, cols], lhsT=w, lhsT_scale=s,
                                     rhs=codes[:, cols].bitcast(FP8X4), rhs_scale=scales[:, cols],
                                     start=True, stop=True)
-            nc.scalar.copy(out=y_slots[:, 2 * C * lo:2 * C * hi], in_=y_ps[:, 0:2 * C * (hi - lo)])
+            copy(out=y_slots[:, 2 * C * lo:2 * C * hi], in_=y_ps[:, 0:2 * C * (hi - lo)])
 
-        for g in range(2):
-            gather_words(g)
-            gather_scales(g)
+        gather_after([-1])
+        for u in range(4):
+            gate_side(u, s_banks[u % 4])
         for q in range(PAIRS):
-            up(2 * q, s_banks[(2 * q) % 4])
-            up(2 * q + 1, s_banks[(2 * q + 1) % 4])
-            if q == 2:
-                load_up_scales(2)
-                load_up_words(6)
-                load_up_words(7)
+            if q < PAIRS - 2:
+                gate_side(2 * q + 4, s_banks[(2 * q) % 4])
+                gate_side(2 * q + 5, s_banks[(2 * q + 1) % 4])
+            if q == 6:
+                gate_side(E, s_banks[(2 * q) % 4])
+                gate_side(E + 1, s_banks[(2 * q + 1) % 4])
+            value_side(2 * q)
+            value_side(2 * q + 1)
+            if q == 0:
+                load_up_scales(0, 2)
+                load_up_words(0, 6)
+                load_up_words(1, 4)
                 load_down_words(2)
-                load_up_words(8)
+                load_up_words(0, 7)
+                load_up_words(1, 5)
+                load_down_words(3)
+            if q == 2:
+                load_up_scales(1, 2)
+                load_up_words(0, 8)
+                load_up_words(1, 6)
+                load_down_words(4)
+                load_up_words(1, 7)
+                load_down_words(5)
+                load_up_words(1, 8)
+                load_down_words(6)
                 for r, pos in enumerate((pos1, pos2, pos3, pos4)):
                     nc.sync.dma_start(pos_t[r][:], pos)
                     nc.sync.dma_start(out=gate_t[r][:], in_=gate[r])
+            if q >= 1:
+                turn(q - 1, s_banks[(2 * q) % 4])
+                quantise(q - 1)
+            gather_after([2 * q, 2 * q + 1])
             if q >= 2:
-                turn(q - 2, s_banks[(2 * q) % 4])
-                if q % 2 == 1:
-                    quantise(group_of(QUANT_GROUPS, q - 2))
-            if q in (1, 3):
-                gather_words((q + 3) // 2)
-            if q in (2, 4):
-                gather_scales((q + 2) // 2)
-            if q >= 4 and q % 2 == 0:
-                down((q - 4) // 2, s_banks[(2 * q + 1) % 4])
-
-        up(E, s_banks[0])
-        up(E + 1, s_banks[1])
-        turn(PAIRS - 2, s_banks[0])
-        quantise(3)
-        turn(PAIRS - 1, s_banks[1])
-        quantise(4)
-        down(2, b_banks[0])
-        up(E + 2, s_banks[2])
-        down(3, s_banks[0])
-        up(E + 3, s_banks[3])
-        down(4, s_banks[1])
+                down(q - 2, y_bank, nc.scalar.copy)
+        value_side(E)
+        value_side(E + 1)
+        turn(PAIRS - 1, s_banks[0])
+        quantise(PAIRS - 1)
+        down(PAIRS - 2, s_banks[1], nc.scalar.copy)
         turn(PAIRS, s_banks[1])
+        quantise(PAIRS)
+        gate_side(E + 2, s_banks[3])
+        down(PAIRS - 1, y_bank, nc.scalar.copy)
+        gate_side(E + 3, s_banks[3])
+        value_side(E + 2)
+        value_side(E + 3)
         turn(PAIRS + 1, s_banks[0])
-        quantise(5)
+        quantise(PAIRS + 1)
 
-        late = keep.tile([P, 2, T], F32, name="late", tag="turned5", align_bytes=64)
+        late = keep.tile([P, 2, T], F32, name="late", tag="turned9", align_bytes=64)
         prod = [keep.tile([P, T], F32, name="prod0")[:], keep.tile([P, T], F32, name="prod1")[:],
                 late[:, 0, :], late[:, 1, :]]
         halves = [slice(0, T // 2), slice(T // 2, T)]
-        sum_banks = [s_banks[2], s_banks[3], b_banks[2], b_banks[3]]
+        sum_banks = [s_banks[2], s_banks[3], b_banks[2], b_banks[0]]
 
         def fetch(r, cols):
             nc.vector.tensor_tensor(out=prod[r][:, cols],
@@ -243,14 +276,15 @@ def tile_moe_shr_glu_relu_kernel(
         for r in range(2):
             fetch(r, slice(0, T))
             add_turned(r, range(4))
-        codes, scales = quantised[5]
         w, s = down_weights(E)
-        for c in range(4):
-            cols = slice(c * C, (c + 1) * C)
-            nc.tensor.matmul_mx(out=b_banks[1][:, cols], lhsT=codes[:, cols].bitcast(FP8X4), lhsT_scale=scales[:, cols],
-                                rhs=w, rhs_scale=s, start=True, stop=True)
         ys_t = keep.tile([P, T], F32, name="ys_t")
-        nc.scalar.copy(out=ys_t[:], in_=b_banks[1][:])
+        for i, (half, bank) in enumerate(zip(halves, (b_banks[1], y_bank))):
+            codes, scales = quantised[PAIRS + i]
+            for j in range(2):
+                cols = slice(j * C, (j + 1) * C)
+                nc.tensor.matmul_mx(out=bank[:, cols], lhsT=codes[:, cols].bitcast(FP8X4), lhsT_scale=scales[:, cols],
+                                    rhs=w, rhs_scale=s, start=True, stop=True)
+            nc.scalar.copy(out=ys_t[:, half], in_=bank[:, 0:T // 2])
         sum_t = keep.tile([P, T], F32, name="sum_t")
         result = [keep.tile([P, T // 2], F32, name=f"result{i}") for i in range(2)]
         for i, half in enumerate(halves):

@@ -21,7 +21,6 @@ RELU = mybir.ActivationFunctionType.Relu
 
 P = 128
 PAIRS = E // 2
-WINDOW = 704
 QUAD = 4 * C
 WORD_GROUPS = [(e, min(e + 2, E + 1)) for e in range(0, E + 1, 2)]
 SCALE_GROUPS = [(0, 6), (6, 12), (12, 17)]
@@ -55,8 +54,8 @@ def tile_moe_shr_glu_relu_kernel(
 
         offs_t = lists.tile([P, E * C // 16], U16, name="offs_t")
         pos_t = [lists.tile([P, T // 16], U16, name=f"pos_t{r}") for r in range(TOP)]
-        xw = keep.tile([P, WINDOW], I32, name="xw", align_bytes=64)
-        xs = keep.tile([P, WINDOW], U8, name="xs", align_bytes=64)
+        xw = keep.tile([P, T], I32, name="xw", align_bytes=64)
+        xs = keep.tile([P, T], U8, name="xs", align_bytes=64)
         up_words = [[keep.tile([P, hi - lo, 2 * H], U8, name=f"up_words{m}_{g}", align_bytes=64)
                      for g, (lo, hi) in enumerate(WORD_GROUPS)] for m in range(2)]
         up_scales = [[keep.tile([P, hi - lo, H], U8, name=f"up_scales{m}_{g}", align_bytes=64)
@@ -69,15 +68,12 @@ def tile_moe_shr_glu_relu_kernel(
         ident = keep.tile([P, P], F32, name="ident")
 
         nc.gpsimd.memset(xs[:].bitcast(I32), 0)
-        nc.gpsimd.memset(xw[:, T:], 0)
         nc.vector.memset(up_scales[0][0][:].bitcast(I32), 0)
         nc.vector.memset(up_scales[1][0][:].bitcast(I32), 0)
         nc.vector.memset(up_scales[0][1][:].bitcast(I32), 0)
-        nc.gpsimd.memset(down_scales[:].bitcast(I32), 0)
+        nc.vector.memset(down_scales[:].bitcast(I32), 0)
         nc.gpsimd.memset(up_scales[1][1][:].bitcast(I32), 0)
         make_identity(nc, ident[:])
-        warm = keep.tile([P, 8], F32, name="warm")
-        nc.scalar.activation(out=warm[:], in_=ident[:, 0:8], func=RELU)
         s_banks = [psum.tile([P, H], F32, name=f"s_bank{b}") for b in range(4)]
         b_banks = [psum.tile([P, H], F32, name=f"b_bank{b}") for b in range(3)]
         y_bank = psum.tile([P, H], F32, name="y_bank")
@@ -103,16 +99,16 @@ def tile_moe_shr_glu_relu_kernel(
             nc.sync.dma_start(out=down_words[g][:].bitcast(I32),
                               in_=w2_words[lo:hi, 0].rearrange("e p b -> p e b").bitcast(I32))
 
-        nc.sync.dma_start(out=xw[:, 0:T], in_=x_words[0].rearrange("p t r -> p (t r)").bitcast(I32))
+        nc.sync.dma_start(out=xw[:], in_=x_words[0].rearrange("p t r -> p (t r)").bitcast(I32))
         for r in range(4):
-            nc.sync.dma_start(out=xs[:].bitcast(I32)[r:P:32, 0:T // 4], in_=x_scales[0, r:16:4, :].bitcast(I32))
+            nc.sync.dma_start(out=xs[:].bitcast(I32)[r:P:32], in_=x_scales[0, r:16:4, :].bitcast(I32))
         nc.sync.dma_start(offs_t[:], offs)
         load_up_words(0, 0)
         load_up_words(0, 1)
         load_up_scales(0, 0)
         load_up_scales(1, 0)
-        load_up_words(0, 2)
         load_up_words(1, 0)
+        load_up_words(0, 2)
         load_up_scales(0, 1)
         load_up_words(0, 3)
         load_up_words(1, 1)
@@ -241,17 +237,17 @@ def tile_moe_shr_glu_relu_kernel(
                 quantise(q - 1)
             gather_after([2 * q, 2 * q + 1])
             if q >= 2:
-                down(q - 2, y_bank, nc.scalar.copy)
+                down(q - 2, s_banks[(2 * q + 1) % 4], nc.scalar.copy)
         value_side(E)
         value_side(E + 1)
         turn(PAIRS - 1, s_banks[0])
         quantise(PAIRS - 1)
         down(PAIRS - 2, s_banks[1], nc.scalar.copy)
-        turn(PAIRS, s_banks[1])
+        turn(PAIRS, s_banks[2])
         quantise(PAIRS)
-        gate_side(E + 2, s_banks[3])
-        down(PAIRS - 1, y_bank, nc.scalar.copy)
-        gate_side(E + 3, s_banks[3])
+        gate_side(E + 2, y_bank)
+        down(PAIRS - 1, s_banks[3], nc.scalar.copy)
+        gate_side(E + 3, y_bank)
         value_side(E + 2)
         value_side(E + 3)
         turn(PAIRS + 1, s_banks[0])
@@ -286,18 +282,21 @@ def tile_moe_shr_glu_relu_kernel(
                                     rhs=w, rhs_scale=s, start=True, stop=True)
             nc.scalar.copy(out=ys_t[:, half], in_=bank[:, 0:T // 2])
         sum_t = keep.tile([P, T], F32, name="sum_t")
-        result = [keep.tile([P, T // 2], F32, name=f"result{i}") for i in range(2)]
-        for i, half in enumerate(halves):
-            fetch(2, half)
-            add_turned(2, (2 * i, 2 * i + 1))
-            for c in (2 * i, 2 * i + 1):
+        pieces = [range(c, c + 1) for c in range(4)]
+        back_banks = [s_banks[0], s_banks[1], b_banks[1], y_bank]
+        for piece in pieces:
+            fetch(2, slice(piece.start * C, piece.stop * C))
+            add_turned(2, piece)
+            for c in piece:
                 nc.scalar.copy(out=sum_t[:, c * C:(c + 1) * C], in_=sum_banks[c][:, 0:P])
-        for i, half in enumerate(halves):
-            fetch(3, half)
-            for c in (2 * i, 2 * i + 1):
+        for piece, bank in zip(pieces, back_banks):
+            fetch(3, slice(piece.start * C, piece.stop * C))
+            for j, c in enumerate(piece):
                 for k, term in enumerate((ys_t, sum_t)):
-                    nc.tensor.matmul(s_banks[i][:, (c % 2) * C:(c % 2 + 1) * C], lhsT=term[:, c * C:(c + 1) * C],
+                    nc.tensor.matmul(bank[:, j * C:(j + 1) * C], lhsT=term[:, c * C:(c + 1) * C],
                                      rhs=ident[:], start=(k == 0), stop=(k == 1), is_transpose=True)
-        for i, half in enumerate(halves):
-            nc.vector.tensor_tensor(out=result[i][:], in0=s_banks[i][:, 0:T // 2], in1=prod[3][:, half], op=ADD)
-            nc.sync.dma_start(out=out[:, half], in_=result[i][:])
+        for i, (piece, bank) in enumerate(zip(pieces, back_banks)):
+            cols = slice(piece.start * C, piece.stop * C)
+            result = keep.tile([P, len(piece) * C], F32, name=f"result{i}")
+            nc.vector.tensor_tensor(out=result[:], in0=bank[:, 0:len(piece) * C], in1=prod[3][:, cols], op=ADD)
+            nc.sync.dma_start(out=out[:, cols], in_=result[:])

@@ -24,7 +24,7 @@ PAIRS = E // 2
 QUAD = 4 * C
 WORD_GROUPS = [(e, min(e + 2, E + 1)) for e in range(0, E + 1, 2)]
 SCALE_GROUPS = [(0, 6), (6, 12), (12, 17)]
-W2_GROUPS = [(e, e + 2) for e in range(0, 12, 2)] + [(12, 17)]
+W2_GROUPS = [(0, 4), (4, 8), (8, 12), (12, 17)]
 QUANT_GROUPS = [(q, q + 1) for q in range(PAIRS + 2)]
 WORD_GATHERS = [(0, 2, 0), (2, 4, 2), (4, 6, 4), (6, 8, 6), (8, 10, 0), (10, 12, 2), (12, 14, 4), (14, 16, 6)]
 SCALE_GATHERS = [(0, 2, 0), (2, 4, 2), (4, 6, 4), (6, 8, 6), (8, 10, 0), (10, 12, 2), (12, 14, 4), (14, 16, 6)]
@@ -109,17 +109,14 @@ def tile_moe_shr_glu_relu_kernel(
         load_up_scales(1, 0)
         load_up_words(1, 0)
         load_up_words(0, 2)
+        load_up_words(1, 1)
         load_up_scales(0, 1)
         load_up_words(0, 3)
-        load_up_words(1, 1)
-        load_down_scales()
         load_up_words(0, 4)
         load_up_words(1, 2)
-        load_down_words(0)
         load_up_scales(1, 1)
         load_up_words(0, 5)
         load_up_words(1, 3)
-        load_down_words(1)
 
         slot_words = keep.tile([P, max(at + hi - lo for lo, hi, at in WORD_GATHERS) * C], U32, name="slot_words", align_bytes=64)
         slot_scales = keep.tile([P, max(at + hi - lo for lo, hi, at in SCALE_GATHERS) * C], U8, name="slot_scales", align_bytes=64)
@@ -189,16 +186,16 @@ def tile_moe_shr_glu_relu_kernel(
             g = group_of(W2_GROUPS, e)
             return down_words[g][:, e - W2_GROUPS[g][0], :].bitcast(FP4X4), down_scales[:, e, :]
 
-        def down(g, y_ps, copy):
-            codes, scales = quantised[g]
-            lo, hi = QUANT_GROUPS[g]
-            for j in range(2 * (hi - lo)):
-                cols = slice(j * C, (j + 1) * C)
-                w, s = down_weights(2 * lo + j)
-                nc.tensor.matmul_mx(out=y_ps[:, cols], lhsT=w, lhsT_scale=s,
-                                    rhs=codes[:, cols].bitcast(FP8X4), rhs_scale=scales[:, cols],
-                                    start=True, stop=True)
-            copy(out=y_slots[:, 2 * C * lo:2 * C * hi], in_=y_ps[:, 0:2 * C * (hi - lo)])
+        def down(pairs, y_ps):
+            for i, q in enumerate(pairs):
+                codes, scales = quantised[q]
+                for j in range(2):
+                    cols = slice(j * C, (j + 1) * C)
+                    w, s = down_weights(2 * q + j)
+                    nc.tensor.matmul_mx(out=y_ps[:, (2 * i + j) * C:(2 * i + j + 1) * C], lhsT=w, lhsT_scale=s,
+                                        rhs=codes[:, cols].bitcast(FP8X4), rhs_scale=scales[:, cols],
+                                        start=True, stop=True)
+            nc.scalar.copy(out=y_slots[:, 2 * C * pairs.start:2 * C * pairs.stop], in_=y_ps[:, 0:2 * C * len(pairs)])
 
         gather_after([-1])
         for u in range(4):
@@ -216,19 +213,19 @@ def tile_moe_shr_glu_relu_kernel(
                 load_up_scales(0, 2)
                 load_up_words(0, 6)
                 load_up_words(1, 4)
-                load_down_words(2)
+                load_down_scales()
                 load_up_words(0, 7)
                 load_up_words(1, 5)
-                load_down_words(3)
+                load_down_words(0)
             if q == 2:
                 load_up_scales(1, 2)
                 load_up_words(0, 8)
                 load_up_words(1, 6)
-                load_down_words(4)
+                load_down_words(1)
                 load_up_words(1, 7)
-                load_down_words(5)
+                load_down_words(2)
                 load_up_words(1, 8)
-                load_down_words(6)
+                load_down_words(3)
                 for r, pos in enumerate((pos1, pos2, pos3, pos4)):
                     nc.sync.dma_start(pos_t[r][:], pos)
                     nc.sync.dma_start(out=gate_t[r][:], in_=gate[r])
@@ -236,17 +233,17 @@ def tile_moe_shr_glu_relu_kernel(
                 turn(q - 1, s_banks[(2 * q) % 4])
                 quantise(q - 1)
             gather_after([2 * q, 2 * q + 1])
-            if q >= 2:
-                down(q - 2, s_banks[(2 * q + 1) % 4], nc.scalar.copy)
+            if q >= 5:
+                down(range(2 * q - 10, 2 * q - 8), s_banks[(2 * q + 1) % 4])
         value_side(E)
         value_side(E + 1)
         turn(PAIRS - 1, s_banks[0])
         quantise(PAIRS - 1)
-        down(PAIRS - 2, s_banks[1], nc.scalar.copy)
+        down(range(6, 7), s_banks[1])
         turn(PAIRS, s_banks[2])
         quantise(PAIRS)
         gate_side(E + 2, y_bank)
-        down(PAIRS - 1, s_banks[3], nc.scalar.copy)
+        down(range(PAIRS - 1, PAIRS), s_banks[3])
         gate_side(E + 3, y_bank)
         value_side(E + 2)
         value_side(E + 3)

@@ -3,7 +3,7 @@ from contextlib import ExitStack
 import concourse.mybir as mybir
 from concourse.masks import make_identity
 
-K, T, E, C, H, N = 512, 512, 16, 128, 512, 128
+T, E, C, H, N = 512, 16, 128, 512, 128
 TOP = 4
 FLOPS = 3019898880
 
@@ -20,26 +20,25 @@ ADD = mybir.AluOpType.add
 RELU = mybir.ActivationFunctionType.Relu
 
 P = 128
+W1, W3 = 0, 1
 PAIRS = E // 2
-QUAD = 4 * C
-WORD_GROUPS = [(e, min(e + 2, E + 1)) for e in range(0, E + 1, 2)]
-SCALE_GROUPS = [(0, 6), (6, 12), (12, 17)]
-W2_GROUPS = [(0, 4), (4, 8), (8, 12), (12, 17)]
-QUANT_GROUPS = [(q, q + 1) for q in range(PAIRS + 2)]
-WORD_GATHERS = [(0, 2, 0), (2, 4, 2), (4, 6, 4), (6, 8, 6), (8, 10, 0), (10, 12, 2), (12, 14, 4), (14, 16, 6)]
-SCALE_GATHERS = [(0, 2, 0), (2, 4, 2), (4, 6, 4), (6, 8, 6), (8, 10, 0), (10, 12, 2), (12, 14, 4), (14, 16, 6)]
+CHUNKS = T // C
+LIST_COLUMNS = C // 16
+RELU_AHEAD = 2
+GATHER_AHEAD = 4
+B_BANKS = 3
+SCALE_RUNS = [range(e, min(e + 6, E + 1)) for e in range(0, E + 1, 6)]
+W2_LOADS = [range(0, 4), range(4, 8), range(8, 12), range(12, E + 1)]
+LOAD_AHEAD = 4
 
 
-def group_of(groups, e):
-    return [g for g, (lo, hi) in enumerate(groups) if lo <= e < hi][0]
+def holder(groups, e):
+    g = [n for n, members in enumerate(groups) if e in members][0]
+    return g, e - groups[g].start
 
 
-def place_of(gathers, e):
-    return [at + e - lo for lo, hi, at in gathers if lo <= e < hi][0]
-
-
-def last_tenant(gathers, lo, hi, at):
-    return max([p for p in range(lo) if at <= place_of(gathers, p) < at + hi - lo] + [-1])
+def block(j, width=C):
+    return slice(j * width, (j + 1) * width)
 
 
 def tile_moe_shr_glu_relu_kernel(
@@ -47,253 +46,238 @@ def tile_moe_shr_glu_relu_kernel(
     gate, offs, pos1, pos2, pos3, pos4, out,
 ):
     nc = tc.nc
+    word_loads = [range(e, min(e + 2, E + 1)) for e in range(0, E + 1, 2)]
     with ExitStack() as ctx:
         lists = ctx.enter_context(tc.tile_pool(name="lists", bufs=1))
         keep = ctx.enter_context(tc.tile_pool(name="keep", bufs=1))
         psum = ctx.enter_context(tc.psum_pool(name="psum", bufs=1))
 
-        offs_t = lists.tile([P, E * C // 16], U16, name="offs_t")
-        pos_t = [lists.tile([P, T // 16], U16, name=f"pos_t{r}") for r in range(TOP)]
+        offs_t = lists.tile([P, E * LIST_COLUMNS], U16, name="offs_t")
+        pos_t = [lists.tile([P, CHUNKS * LIST_COLUMNS], U16, name=f"pos_t{r}") for r in range(TOP)]
         xw = keep.tile([P, T], I32, name="xw", align_bytes=64)
         xs = keep.tile([P, T], U8, name="xs", align_bytes=64)
-        up_words = [[keep.tile([P, hi - lo, 2 * H], U8, name=f"up_words{m}_{g}", align_bytes=64)
-                     for g, (lo, hi) in enumerate(WORD_GROUPS)] for m in range(2)]
-        up_scales = [[keep.tile([P, hi - lo, H], U8, name=f"up_scales{m}_{g}", align_bytes=64)
-                      for g, (lo, hi) in enumerate(SCALE_GROUPS[:2])] for m in range(2)]
-        down_words = [keep.tile([P, hi - lo, 2 * N], U8, name=f"down_words{g}", align_bytes=64)
-                      for g, (lo, hi) in enumerate(W2_GROUPS)]
-        down_scales = keep.tile([P, E + 1, N], U8, name="down_scales", align_bytes=64)
+        up_words = [[keep.tile([P, len(members), 2 * H], U8, name=f"up_words{m}_{g}", align_bytes=64)
+                     for g, members in enumerate(word_loads)] for m in (W1, W3)]
+        up_planes = [[keep.tile([P, len(members), H], U8, name=f"up_planes{m}_{g}", align_bytes=64)
+                      for g, members in enumerate(SCALE_RUNS[:2])] for m in (W1, W3)]
+        down_words = [keep.tile([P, len(members), 2 * N], U8, name=f"down_words{g}", align_bytes=64)
+                      for g, members in enumerate(W2_LOADS)]
+        down_plane = keep.tile([P, E + 1, N], U8, name="down_plane", align_bytes=64)
         gate_t = [keep.tile([P, T], F32, name=f"gate_t{r}") for r in range(TOP)]
         y_slots = keep.tile([P, E * C], F32, name="y_slots")
         ident = keep.tile([P, P], F32, name="ident")
 
         nc.gpsimd.memset(xs[:].bitcast(I32), 0)
-        nc.vector.memset(up_scales[0][0][:].bitcast(I32), 0)
-        nc.vector.memset(up_scales[1][0][:].bitcast(I32), 0)
-        nc.vector.memset(up_scales[0][1][:].bitcast(I32), 0)
-        nc.vector.memset(down_scales[:].bitcast(I32), 0)
-        nc.gpsimd.memset(up_scales[1][1][:].bitcast(I32), 0)
+        nc.vector.memset(up_planes[W1][0][:].bitcast(I32), 0)
+        nc.vector.memset(up_planes[W3][0][:].bitcast(I32), 0)
+        nc.vector.memset(up_planes[W1][1][:].bitcast(I32), 0)
+        nc.vector.memset(down_plane[:].bitcast(I32), 0)
+        nc.gpsimd.memset(up_planes[W3][1][:].bitcast(I32), 0)
         make_identity(nc, ident[:])
-        s_banks = [psum.tile([P, H], F32, name=f"s_bank{b}") for b in range(4)]
-        b_banks = [psum.tile([P, H], F32, name=f"b_bank{b}") for b in range(3)]
-        y_bank = psum.tile([P, H], F32, name="y_bank")
 
-        def load_up_words(m, g):
-            lo, hi = WORD_GROUPS[g]
-            nc.sync.dma_start(out=up_words[m][g][:].bitcast(I32),
-                              in_=(w1_words, w3_words)[m][lo:hi, 0].rearrange("e p b -> p e b").bitcast(I32))
+        a_banks = [psum.tile([P, H], F32, name=f"a_bank{b}") for b in range(4)]
+        b_banks = [psum.tile([P, H], F32, name=f"b_bank{b}") for b in range(B_BANKS)]
+        spare_bank = psum.tile([P, H], F32, name="spare_bank")
 
-        def load_up_scales(m, g):
-            lo, hi = SCALE_GROUPS[g]
+        def load_up_words(m, pair):
+            members = word_loads[pair]
+            nc.sync.dma_start(
+                out=up_words[m][pair][:].bitcast(I32),
+                in_=(w1_words, w3_words)[m][members.start:members.stop, 0].rearrange("e p b -> p e b").bitcast(I32))
+
+        def load_up_scales(m, run):
+            members = SCALE_RUNS[run]
+            rows = (w1_scales, w3_scales)[m][members.start:members.stop, 0]
             for r in range(4):
-                nc.sync.dma_start(out=up_scales[m][g % 2][:].bitcast(I32)[r:P:32, 0:hi - lo],
-                                  in_=(w1_scales, w3_scales)[m][lo:hi, 0, r:16:4, :].rearrange("e q i -> q e i").bitcast(I32))
-
-        def load_down_scales():
-            for r in range(4):
-                nc.sync.dma_start(out=down_scales[:].bitcast(I32)[r:P:32],
-                                  in_=w2_scales[:, 0, r:16:4, :].rearrange("e q n -> q e n").bitcast(I32))
+                nc.sync.dma_start(out=up_planes[m][run % 2][:].bitcast(I32)[r:P:32, 0:len(members)],
+                                  in_=rows[:, r:16:4, :].rearrange("e q i -> q e i").bitcast(I32))
 
         def load_down_words(g):
-            lo, hi = W2_GROUPS[g]
+            members = W2_LOADS[g]
             nc.sync.dma_start(out=down_words[g][:].bitcast(I32),
-                              in_=w2_words[lo:hi, 0].rearrange("e p b -> p e b").bitcast(I32))
+                              in_=w2_words[members.start:members.stop, 0].rearrange("e p b -> p e b").bitcast(I32))
+
+        def load_scales_for(m, pair):
+            run, place = holder(SCALE_RUNS, 2 * pair)
+            if place == 0:
+                load_up_scales(m, run)
+
+        def load_step(q):
+            load_scales_for(W3, q)
+            if q + RELU_AHEAD <= PAIRS:
+                load_scales_for(W1, q + RELU_AHEAD)
+                load_up_words(W1, q + RELU_AHEAD)
+            load_up_words(W3, q)
+
+        def load_rest():
+            for r in range(4):
+                nc.sync.dma_start(out=down_plane[:].bitcast(I32)[r:P:32],
+                                  in_=w2_scales[:, 0, r:16:4, :].rearrange("e q n -> q e n").bitcast(I32))
+            load_down_words(0)
+            load_down_words(1)
+            load_up_words(W3, PAIRS)
+            load_down_words(2)
+            load_down_words(3)
+            for r, pos in enumerate((pos1, pos2, pos3, pos4)):
+                nc.sync.dma_start(pos_t[r][:], pos)
+                nc.sync.dma_start(out=gate_t[r][:], in_=gate[r])
 
         nc.sync.dma_start(out=xw[:], in_=x_words[0].rearrange("p t r -> p (t r)").bitcast(I32))
         for r in range(4):
             nc.sync.dma_start(out=xs[:].bitcast(I32)[r:P:32], in_=x_scales[0, r:16:4, :].bitcast(I32))
         nc.sync.dma_start(offs_t[:], offs)
-        load_up_words(0, 0)
-        load_up_words(0, 1)
-        load_up_scales(0, 0)
-        load_up_scales(1, 0)
-        load_up_words(1, 0)
-        load_up_words(0, 2)
-        load_up_words(1, 1)
-        load_up_scales(0, 1)
-        load_up_words(0, 3)
-        load_up_words(0, 4)
-        load_up_words(1, 2)
-        load_up_scales(1, 1)
-        load_up_words(0, 5)
-        load_up_words(1, 3)
+        load_up_words(W1, 0)
+        load_up_words(W3, 0)
+        load_up_scales(W1, 0)
+        load_up_scales(W3, 0)
+        load_up_words(W1, 1)
+        load_up_words(W1, RELU_AHEAD)
+        load_up_words(W3, 1)
+        load_scales_for(W1, 1 + RELU_AHEAD)
+        load_up_words(W1, 1 + RELU_AHEAD)
+        for q in range(2, LOAD_AHEAD):
+            load_step(q)
 
-        slot_words = keep.tile([P, max(at + hi - lo for lo, hi, at in WORD_GATHERS) * C], U32, name="slot_words", align_bytes=64)
-        slot_scales = keep.tile([P, max(at + hi - lo for lo, hi, at in SCALE_GATHERS) * C], U8, name="slot_scales", align_bytes=64)
+        slot_words = keep.tile([P, GATHER_AHEAD * 2 * C], U32, name="slot_words", align_bytes=64)
+        slot_plane = keep.tile([P, GATHER_AHEAD * 2 * C], U8, name="slot_plane", align_bytes=64)
 
-        def gather_after(experts):
-            for (lo, hi, at), (slo, shi, sat) in zip(WORD_GATHERS, SCALE_GATHERS):
-                if last_tenant(WORD_GATHERS, lo, hi, at) in experts:
-                    nc.vector.tensor_copy(out=slot_words[:, at * C:(at + hi - lo) * C],
-                                          in_=xw[:].bitcast(U32).indirect(offs_t[:, 8 * lo:8 * hi]))
-                if last_tenant(SCALE_GATHERS, slo, shi, sat) in experts:
-                    nc.vector.tensor_copy(out=slot_scales[:, sat * C:(sat + shi - slo) * C],
-                                          in_=xs[:].indirect(offs_t[:, 8 * slo:8 * shi]))
+        def gather(pair):
+            place = block(pair % GATHER_AHEAD, 2 * C)
+            entries = offs_t[:, block(pair, 2 * LIST_COLUMNS)]
+            nc.vector.tensor_copy(out=slot_words[:, place], in_=xw[:].bitcast(U32).indirect(entries))
+            nc.vector.tensor_copy(out=slot_plane[:, place], in_=xs[:].indirect(entries))
 
-        by_word = "s (p u e) -> s u p e"
-        as_laid = "s (u p e) -> s u p e"
-        relu_tiles, h_tiles, quantised = {}, {}, {}
-        turned = [keep.tile([P, (hi - lo) * 2 * H], BF16, name=f"turned{g}", tag=f"turned{g}", align_bytes=64)
-                  for g, (lo, hi) in enumerate(QUANT_GROUPS)]
+        from_bank = "s (p u v) -> s u p v"
+        as_laid = "s (u p v) -> s u p v"
+        relu_a, h, quantised = {}, {}, {}
+        turned = [keep.tile([P, 2 * H], BF16, name=f"turned{q}", tag=f"turned{q}", align_bytes=64)
+                  for q in range(PAIRS + 2)]
 
-        def first_layer(m, u, acc):
-            if u < E:
-                e = u
-                wa, sa = place_of(WORD_GATHERS, e) * C, place_of(SCALE_GATHERS, e) * C
-                words, scales = slot_words[:, wa:wa + C], slot_scales[:, sa:sa + C]
+        def first_layer(m, unit, bank):
+            if unit < E:
+                cols = block(unit % (2 * GATHER_AHEAD))
+                words, plane = slot_words[:, cols], slot_plane[:, cols]
             else:
-                e = E
-                cols = slice((u - E) * C, (u - E + 1) * C)
-                words, scales = xw[:, cols], xs[:, cols]
-            gw, gs = group_of(WORD_GROUPS, e), group_of(SCALE_GROUPS, e)
-            nc.tensor.matmul_mx(out=acc[:], lhsT=words.bitcast(FP8X4), lhsT_scale=scales,
-                                rhs=up_words[m][gw][:, e - WORD_GROUPS[gw][0], :].bitcast(FP4X4),
-                                rhs_scale=up_scales[m][gs % 2][:, e - SCALE_GROUPS[gs][0], :], start=True, stop=True)
+                cols = block(unit - E)
+                words, plane = xw[:, cols], xs[:, cols]
+            e = min(unit, E)
+            load, place = holder(word_loads, e)
+            run, row = holder(SCALE_RUNS, e)
+            nc.tensor.matmul_mx(out=bank[:], lhsT=words.bitcast(FP8X4), lhsT_scale=plane,
+                                rhs=up_words[m][load][:, place, :].bitcast(FP4X4),
+                                rhs_scale=up_planes[m][run % 2][:, row, :], start=True, stop=True)
 
-        def gate_side(u, a_ps):
-            first_layer(0, u, a_ps)
-            relu_tiles[u] = keep.tile([P, H], F32, name=f"relu_a{u}")
-            nc.scalar.activation(out=relu_tiles[u][:].rearrange(as_laid, u=2, e=2),
-                                 in_=a_ps[:].rearrange(by_word, u=2, e=2), func=RELU)
+        def w1_side(unit, bank):
+            first_layer(W1, unit, bank)
+            relu_a[unit] = keep.tile([P, H], F32, name=f"relu_a{unit}")
+            nc.scalar.activation(out=relu_a[unit][:].rearrange(as_laid, u=2, v=2),
+                                 in_=bank[:].rearrange(from_bank, u=2, v=2), func=RELU)
 
-        def value_side(u):
-            b_ps = b_banks[u % 3]
-            first_layer(1, u, b_ps)
-            h_tiles[u] = keep.tile([P, H], BF16, name=f"h{u}", align_bytes=64)
-            nc.vector.tensor_tensor(out=h_tiles[u][:].rearrange(as_laid, u=2, e=2),
-                                    in0=b_ps[:].rearrange(by_word, u=2, e=2),
-                                    in1=relu_tiles[u][:].rearrange(as_laid, u=2, e=2), op=MULT)
+        def w3_side(unit):
+            bank = b_banks[unit % B_BANKS]
+            first_layer(W3, unit, bank)
+            h[unit] = keep.tile([P, H], BF16, name=f"h{unit}", align_bytes=64)
+            nc.vector.tensor_tensor(out=h[unit][:].rearrange(as_laid, u=2, v=2),
+                                    in0=bank[:].rearrange(from_bank, u=2, v=2),
+                                    in1=relu_a[unit][:].rearrange(as_laid, u=2, v=2), op=MULT)
 
-        def turn(q, bank):
-            t_ps = bank[:].rearrange("p (j u s) -> p j u s", j=2, u=2)
+        def turn_and_quantise(pair, bank):
+            blocks = bank[:].rearrange("p (j u s) -> p j u s", j=2, u=2)
             for j in (1, 0):
-                words = h_tiles[2 * q + j][:].bitcast(F32)
+                words = h[2 * pair + j][:].bitcast(F32)
                 for u in range(2):
-                    nc.tensor.transpose(t_ps[:, j, u, :], words[:, u * P:(u + 1) * P], ident[:])
-            g = group_of(QUANT_GROUPS, q)
-            at = (q - QUANT_GROUPS[g][0]) * H
-            nc.scalar.copy(out=turned[g][:].bitcast(F32)[:, at:at + H].rearrange("p (j s u) -> p j s u", j=2, u=2),
-                           in_=t_ps.rearrange("p j u s -> p j s u"))
+                    nc.tensor.transpose(blocks[:, j, u, :], words[:, block(u)], ident[:])
+            nc.scalar.copy(out=turned[pair][:].bitcast(F32).rearrange("p (j s u) -> p j s u", j=2, u=2),
+                           in_=blocks.rearrange("p j u s -> p j s u"))
+            codes = keep.tile([P, 2 * C], U32, name=f"codes{pair}", align_bytes=64)
+            plane = keep.tile([P, 2 * C], U8, name=f"h_plane{pair}", align_bytes=64)
+            nc.vector.quantize_mx(out=codes[:].bitcast(FP8X4), scales=plane[:], in_=turned[pair][:])
+            quantised[pair] = (codes, plane)
 
-        def quantise(g):
-            lo, hi = QUANT_GROUPS[g]
-            codes = keep.tile([P, (hi - lo) * 2 * C], U32, name=f"codes{g}", align_bytes=64)
-            scales = keep.tile([P, (hi - lo) * 2 * C], U8, name=f"scales{g}", align_bytes=64)
-            nc.vector.quantize_mx(out=codes[:].bitcast(FP8X4), scales=scales[:], in_=turned[g][:])
-            quantised[g] = (codes, scales)
+        def h_operand(unit):
+            codes, plane = quantised[unit // 2]
+            return codes[:, block(unit % 2)].bitcast(FP8X4), plane[:, block(unit % 2)]
 
-        def down_weights(e):
-            g = group_of(W2_GROUPS, e)
-            return down_words[g][:, e - W2_GROUPS[g][0], :].bitcast(FP4X4), down_scales[:, e, :]
+        def w2_operand(e):
+            load, place = holder(W2_LOADS, e)
+            return down_words[load][:, place, :].bitcast(FP4X4), down_plane[:, e, :]
 
-        def down(pairs, y_ps):
-            for i, q in enumerate(pairs):
-                codes, scales = quantised[q]
-                for j in range(2):
-                    cols = slice(j * C, (j + 1) * C)
-                    w, s = down_weights(2 * q + j)
-                    nc.tensor.matmul_mx(out=y_ps[:, (2 * i + j) * C:(2 * i + j + 1) * C], lhsT=w, lhsT_scale=s,
-                                        rhs=codes[:, cols].bitcast(FP8X4), rhs_scale=scales[:, cols],
-                                        start=True, stop=True)
-            nc.scalar.copy(out=y_slots[:, 2 * C * pairs.start:2 * C * pairs.stop], in_=y_ps[:, 0:2 * C * len(pairs)])
+        def second_layer(g, bank):
+            for j in range(4):
+                words, plane = w2_operand(4 * g + j)
+                codes, h_plane = h_operand(4 * g + j)
+                nc.tensor.matmul_mx(out=bank[:, block(j)], lhsT=words, lhsT_scale=plane,
+                                    rhs=codes, rhs_scale=h_plane, start=True, stop=True)
+            nc.scalar.copy(out=y_slots[:, block(g, 4 * C)], in_=bank[:])
 
-        gather_after([-1])
-        for u in range(4):
-            gate_side(u, s_banks[u % 4])
+        for pair in range(GATHER_AHEAD):
+            gather(pair)
+        for unit in range(2 * RELU_AHEAD):
+            w1_side(unit, a_banks[unit])
         for q in range(PAIRS):
-            if q < PAIRS - 2:
-                gate_side(2 * q + 4, s_banks[(2 * q) % 4])
-                gate_side(2 * q + 5, s_banks[(2 * q + 1) % 4])
-            if q == 6:
-                gate_side(E, s_banks[(2 * q) % 4])
-                gate_side(E + 1, s_banks[(2 * q + 1) % 4])
-            value_side(2 * q)
-            value_side(2 * q + 1)
-            if q == 0:
-                load_up_scales(0, 2)
-                load_up_words(0, 6)
-                load_up_words(1, 4)
-                load_down_scales()
-                load_up_words(0, 7)
-                load_up_words(1, 5)
-                load_down_words(0)
-            if q == 2:
-                load_up_scales(1, 2)
-                load_up_words(0, 8)
-                load_up_words(1, 6)
-                load_down_words(1)
-                load_up_words(1, 7)
-                load_down_words(2)
-                load_up_words(1, 8)
-                load_down_words(3)
-                for r, pos in enumerate((pos1, pos2, pos3, pos4)):
-                    nc.sync.dma_start(pos_t[r][:], pos)
-                    nc.sync.dma_start(out=gate_t[r][:], in_=gate[r])
+            if q + RELU_AHEAD <= PAIRS:
+                for j in range(2):
+                    w1_side(2 * (q + RELU_AHEAD) + j, a_banks[(2 * q + j) % 4])
+            w3_side(2 * q)
+            w3_side(2 * q + 1)
+            if q + LOAD_AHEAD < PAIRS:
+                load_step(q + LOAD_AHEAD)
+            if q + LOAD_AHEAD == PAIRS:
+                load_rest()
             if q >= 1:
-                turn(q - 1, s_banks[(2 * q) % 4])
-                quantise(q - 1)
-            gather_after([2 * q, 2 * q + 1])
-            if q >= 5:
-                down(range(2 * q - 10, 2 * q - 8), s_banks[(2 * q + 1) % 4])
-        value_side(E)
-        value_side(E + 1)
-        turn(PAIRS - 1, s_banks[0])
-        quantise(PAIRS - 1)
-        down(range(6, 7), s_banks[1])
-        turn(PAIRS, s_banks[2])
-        quantise(PAIRS)
-        gate_side(E + 2, y_bank)
-        down(range(PAIRS - 1, PAIRS), s_banks[3])
-        gate_side(E + 3, y_bank)
-        value_side(E + 2)
-        value_side(E + 3)
-        turn(PAIRS + 1, s_banks[0])
-        quantise(PAIRS + 1)
+                turn_and_quantise(q - 1, a_banks[(2 * q) % 4])
+            if q + GATHER_AHEAD < PAIRS:
+                gather(q + GATHER_AHEAD)
 
-        late = keep.tile([P, 2, T], F32, name="late", tag="turned9", align_bytes=64)
+        w3_side(E)
+        w3_side(E + 1)
+        turn_and_quantise(PAIRS - 1, a_banks[0])
+        w1_side(E + 2, spare_bank)
+        w1_side(E + 3, spare_bank)
+        for g, bank in enumerate((a_banks[3], a_banks[1], spare_bank, a_banks[0])):
+            second_layer(g, bank)
+        turn_and_quantise(PAIRS, a_banks[2])
+        w3_side(E + 2)
+        w3_side(E + 3)
+        turn_and_quantise(PAIRS + 1, a_banks[0])
+
+        late = keep.tile([P, 2, T], F32, name="late", tag=f"turned{PAIRS + 1}", align_bytes=64)
         prod = [keep.tile([P, T], F32, name="prod0")[:], keep.tile([P, T], F32, name="prod1")[:],
                 late[:, 0, :], late[:, 1, :]]
-        halves = [slice(0, T // 2), slice(T // 2, T)]
-        sum_banks = [s_banks[2], s_banks[3], b_banks[2], b_banks[0]]
+        sum_banks = [a_banks[2], a_banks[3], b_banks[2], b_banks[0]]
+        back_banks = [a_banks[0], a_banks[1], b_banks[1], spare_bank]
 
-        def fetch(r, cols):
+        def fetch(r, first, last):
+            cols = slice(first * C, last * C)
             nc.vector.tensor_tensor(out=prod[r][:, cols],
-                                    in0=y_slots[:].indirect(pos_t[r][:, cols.start // 16:cols.stop // 16]),
+                                    in0=y_slots[:].indirect(pos_t[r][:, first * LIST_COLUMNS:last * LIST_COLUMNS]),
                                     in1=gate_t[r][:, cols], op=MULT)
 
-        def add_turned(r, chunks):
-            for c in chunks:
-                nc.tensor.matmul(sum_banks[c][:, 0:P], lhsT=prod[r][:, c * C:(c + 1) * C], rhs=ident[:],
-                                 start=(r == 0), stop=(r == TOP - 2), is_transpose=True)
+        def add_turned(bank, term, start, stop):
+            nc.tensor.matmul(bank[:, 0:P], lhsT=term, rhs=ident[:], start=start, stop=stop, is_transpose=True)
 
         for r in range(2):
-            fetch(r, slice(0, T))
-            add_turned(r, range(4))
-        w, s = down_weights(E)
-        ys_t = keep.tile([P, T], F32, name="ys_t")
-        for i, (half, bank) in enumerate(zip(halves, (b_banks[1], y_bank))):
-            codes, scales = quantised[PAIRS + i]
+            fetch(r, 0, CHUNKS)
+            for c in range(CHUNKS):
+                add_turned(sum_banks[c], prod[r][:, block(c)], r == 0, False)
+        words, plane = w2_operand(E)
+        shared_t = keep.tile([P, T], F32, name="shared_t")
+        for i, bank in enumerate((b_banks[1], spare_bank)):
             for j in range(2):
-                cols = slice(j * C, (j + 1) * C)
-                nc.tensor.matmul_mx(out=bank[:, cols], lhsT=codes[:, cols].bitcast(FP8X4), lhsT_scale=scales[:, cols],
-                                    rhs=w, rhs_scale=s, start=True, stop=True)
-            nc.scalar.copy(out=ys_t[:, half], in_=bank[:, 0:T // 2])
+                codes, h_plane = h_operand(E + 2 * i + j)
+                nc.tensor.matmul_mx(out=bank[:, block(j)], lhsT=codes, lhsT_scale=h_plane,
+                                    rhs=words, rhs_scale=plane, start=True, stop=True)
+            nc.scalar.copy(out=shared_t[:, block(i, 2 * C)], in_=bank[:, 0:2 * C])
         sum_t = keep.tile([P, T], F32, name="sum_t")
-        pieces = [range(c, c + 1) for c in range(4)]
-        back_banks = [s_banks[0], s_banks[1], b_banks[1], y_bank]
-        for piece in pieces:
-            fetch(2, slice(piece.start * C, piece.stop * C))
-            add_turned(2, piece)
-            for c in piece:
-                nc.scalar.copy(out=sum_t[:, c * C:(c + 1) * C], in_=sum_banks[c][:, 0:P])
-        for piece, bank in zip(pieces, back_banks):
-            fetch(3, slice(piece.start * C, piece.stop * C))
-            for j, c in enumerate(piece):
-                for k, term in enumerate((ys_t, sum_t)):
-                    nc.tensor.matmul(bank[:, j * C:(j + 1) * C], lhsT=term[:, c * C:(c + 1) * C],
-                                     rhs=ident[:], start=(k == 0), stop=(k == 1), is_transpose=True)
-        for i, (piece, bank) in enumerate(zip(pieces, back_banks)):
-            cols = slice(piece.start * C, piece.stop * C)
-            result = keep.tile([P, len(piece) * C], F32, name=f"result{i}")
-            nc.vector.tensor_tensor(out=result[:], in0=bank[:, 0:len(piece) * C], in1=prod[3][:, cols], op=ADD)
-            nc.sync.dma_start(out=out[:, cols], in_=result[:])
+        for c in range(CHUNKS):
+            fetch(2, c, c + 1)
+            add_turned(sum_banks[c], prod[2][:, block(c)], False, True)
+            nc.scalar.copy(out=sum_t[:, block(c)], in_=sum_banks[c][:, 0:P])
+        for c in range(CHUNKS):
+            fetch(3, c, c + 1)
+            add_turned(back_banks[c], shared_t[:, block(c)], True, False)
+            add_turned(back_banks[c], sum_t[:, block(c)], False, True)
+        for c in range(CHUNKS):
+            result = keep.tile([P, C], F32, name=f"result{c}")
+            nc.vector.tensor_tensor(out=result[:], in0=back_banks[c][:, 0:C], in1=prod[3][:, block(c)], op=ADD)
+            nc.sync.dma_start(out=out[:, block(c)], in_=result[:])

@@ -30,6 +30,9 @@ B_BANKS = 3
 SCALE_RUNS = [range(e, min(e + 6, E + 1)) for e in range(0, E + 1, 6)]
 W2_LOADS = [range(0, 4), range(4, 8), range(8, 12), range(12, E + 1)]
 LOAD_AHEAD = 4
+LATE_GROUPS = 3
+QUANT_GROUPS = ([range(2 * g, 2 * g + 2) for g in range(LATE_GROUPS)]
+                + [range(q, q + 1) for q in range(2 * LATE_GROUPS, PAIRS + 2)])
 
 
 def holder(groups, e):
@@ -56,13 +59,15 @@ def tile_moe_shr_glu_relu_kernel(
         pos_t = [lists.tile([P, CHUNKS * LIST_COLUMNS], U16, name=f"pos_t{r}") for r in range(TOP)]
         xw = keep.tile([P, T], I32, name="xw", align_bytes=64)
         xs = keep.tile([P, T], U8, name="xs", align_bytes=64)
-        up_words = [[keep.tile([P, len(members), 2 * H], U8, name=f"up_words{m}_{g}", align_bytes=64)
+        up_words = [[keep.tile([P, len(members), 2 * H], U8, name=f"up_words{m}_{g}", tag=f"up_words{m}_{g}",
+                               align_bytes=64)
                      for g, members in enumerate(word_loads)] for m in (W1, W3)]
         up_planes = [[keep.tile([P, len(members), H], U8, name=f"up_planes{m}_{g}", align_bytes=64)
                       for g, members in enumerate(SCALE_RUNS[:2])] for m in (W1, W3)]
         down_words = [keep.tile([P, len(members), 2 * N], U8, name=f"down_words{g}", align_bytes=64)
                       for g, members in enumerate(W2_LOADS)]
-        down_plane = keep.tile([P, E + 1, N], U8, name="down_plane", align_bytes=64)
+        plane_bytes = up_planes[W1][1][:].rearrange("p e i -> p (e i)")
+        down_plane = plane_bytes[:, 0:(E + 1) * N].rearrange("p (e n) -> p e n", n=N)
         gate_t = [keep.tile([P, T], F32, name=f"gate_t{r}") for r in range(TOP)]
         y_slots = keep.tile([P, E * C], F32, name="y_slots")
         ident = keep.tile([P, P], F32, name="ident")
@@ -71,7 +76,6 @@ def tile_moe_shr_glu_relu_kernel(
         nc.vector.memset(up_planes[W1][0][:].bitcast(I32), 0)
         nc.vector.memset(up_planes[W3][0][:].bitcast(I32), 0)
         nc.vector.memset(up_planes[W1][1][:].bitcast(I32), 0)
-        nc.vector.memset(down_plane[:].bitcast(I32), 0)
         nc.gpsimd.memset(up_planes[W3][1][:].bitcast(I32), 0)
         make_identity(nc, ident[:])
 
@@ -111,7 +115,7 @@ def tile_moe_shr_glu_relu_kernel(
 
         def load_rest():
             for r in range(4):
-                nc.sync.dma_start(out=down_plane[:].bitcast(I32)[r:P:32],
+                nc.sync.dma_start(out=down_plane.bitcast(I32)[r:P:32],
                                   in_=w2_scales[:, 0, r:16:4, :].rearrange("e q n -> q e n").bitcast(I32))
             load_down_words(0)
             load_down_words(1)
@@ -150,8 +154,8 @@ def tile_moe_shr_glu_relu_kernel(
         from_bank = "s (p u v) -> s u p v"
         as_laid = "s (u p v) -> s u p v"
         relu_a, h, quantised = {}, {}, {}
-        turned = [keep.tile([P, 2 * H], BF16, name=f"turned{q}", tag=f"turned{q}", align_bytes=64)
-                  for q in range(PAIRS + 2)]
+        turned = [keep.tile([P, len(group) * 2 * H], BF16, name=f"turned{g}", tag=f"turned{g}", align_bytes=64)
+                  for g, group in enumerate(QUANT_GROUPS)]
 
         def first_layer(m, unit, bank):
             if unit < E:
@@ -181,22 +185,34 @@ def tile_moe_shr_glu_relu_kernel(
                                     in0=bank[:].rearrange(from_bank, u=2, v=2),
                                     in1=relu_a[unit][:].rearrange(as_laid, u=2, v=2), op=MULT)
 
-        def turn_and_quantise(pair, bank):
+        def turn(pair, bank):
             blocks = bank[:].rearrange("p (j u s) -> p j u s", j=2, u=2)
             for j in (1, 0):
                 words = h[2 * pair + j][:].bitcast(F32)
                 for u in range(2):
                     nc.tensor.transpose(blocks[:, j, u, :], words[:, block(u)], ident[:])
-            nc.scalar.copy(out=turned[pair][:].bitcast(F32).rearrange("p (j s u) -> p j s u", j=2, u=2),
+            g, place = holder(QUANT_GROUPS, pair)
+            laid = turned[g][:].bitcast(F32)[:, block(place, H)]
+            nc.scalar.copy(out=laid.rearrange("p (j s u) -> p j s u", j=2, u=2),
                            in_=blocks.rearrange("p j u s -> p j s u"))
-            codes = keep.tile([P, 2 * C], U32, name=f"codes{pair}", align_bytes=64)
-            plane = keep.tile([P, 2 * C], U8, name=f"h_plane{pair}", align_bytes=64)
-            nc.vector.quantize_mx(out=codes[:].bitcast(FP8X4), scales=plane[:], in_=turned[pair][:])
-            quantised[pair] = (codes, plane)
+
+        def quantise(g):
+            width = len(QUANT_GROUPS[g]) * 2 * C
+            tag = f"up_words{W3}_{GATHER_AHEAD + g}" if g < LATE_GROUPS else f"codes{g}"
+            codes = keep.tile([P, width], U32, name=f"codes{g}", tag=tag, align_bytes=64)
+            plane = keep.tile([P, width], U8, name=f"h_plane{g}", align_bytes=64)
+            nc.vector.quantize_mx(out=codes[:].bitcast(FP8X4), scales=plane[:], in_=turned[g][:])
+            quantised[g] = (codes, plane)
+
+        def turn_and_quantise(pair, bank):
+            turn(pair, bank)
+            quantise(holder(QUANT_GROUPS, pair)[0])
 
         def h_operand(unit):
-            codes, plane = quantised[unit // 2]
-            return codes[:, block(unit % 2)].bitcast(FP8X4), plane[:, block(unit % 2)]
+            g, place = holder(QUANT_GROUPS, unit // 2)
+            codes, plane = quantised[g]
+            cols = block(2 * place + unit % 2)
+            return codes[:, cols].bitcast(FP8X4), plane[:, cols]
 
         def w2_operand(e):
             load, place = holder(W2_LOADS, e)
@@ -225,7 +241,9 @@ def tile_moe_shr_glu_relu_kernel(
             if q + LOAD_AHEAD == PAIRS:
                 load_rest()
             if q >= 1:
-                turn_and_quantise(q - 1, a_banks[(2 * q) % 4])
+                turn(q - 1, a_banks[(2 * q) % 4])
+            if q >= GATHER_AHEAD:
+                quantise(q - GATHER_AHEAD)
             if q + GATHER_AHEAD < PAIRS:
                 gather(q + GATHER_AHEAD)
 
@@ -241,7 +259,7 @@ def tile_moe_shr_glu_relu_kernel(
         w3_side(E + 3)
         turn_and_quantise(PAIRS + 1, a_banks[0])
 
-        late = keep.tile([P, 2, T], F32, name="late", tag=f"turned{PAIRS + 1}", align_bytes=64)
+        late = keep.tile([P, 2, T], F32, name="late", tag=f"turned{len(QUANT_GROUPS) - 1}", align_bytes=64)
         prod = [keep.tile([P, T], F32, name="prod0")[:], keep.tile([P, T], F32, name="prod1")[:],
                 late[:, 0, :], late[:, 1, :]]
         sum_banks = [a_banks[2], a_banks[3], b_banks[2], b_banks[0]]

@@ -25,19 +25,26 @@ PAIRS = E // 2
 CHUNKS = T // C
 LIST_COLUMNS = C // 16
 RELU_AHEAD = 2
-GATHER_AHEAD = 4
+GATHER_AHEAD = 5
 B_BANKS = 3
-SCALE_RUNS = [range(e, min(e + 6, E + 1)) for e in range(0, E + 1, 6)]
-W2_LOADS = [range(0, 4), range(4, 8), range(8, 12), range(12, E + 1)]
+SCALE_RUNS = [range(12, E + 1), range(6, 12), range(0, 6)]
+W2_LOADS = [range(12, E + 1), range(8, 12), range(4, 8), range(0, 4)]
+EARLY_SHARED = 4
+W3_FIRST = 5
 LOAD_AHEAD = 4
 LATE_GROUPS = 3
 QUANT_GROUPS = ([range(2 * g, 2 * g + 2) for g in range(LATE_GROUPS)]
-                + [range(q, q + 1) for q in range(2 * LATE_GROUPS, PAIRS + 2)])
+                + [range(q, q + 1) for q in range(2 * LATE_GROUPS, PAIRS)] + [range(PAIRS, PAIRS + 2)])
+QUANT_AFTER = {0: f"up_words{W3}_3", 1: f"up_words{W3}_5", 2: f"up_words{W3}_7"}
 
 
 def holder(groups, e):
     g = [n for n, members in enumerate(groups) if e in members][0]
     return g, e - groups[g].start
+
+
+def expert(unit):
+    return E - 2 - unit + 2 * (unit % 2) if unit < E else E
 
 
 def block(j, width=C):
@@ -49,7 +56,7 @@ def tile_moe_shr_glu_relu_kernel(
     gate, offs, pos1, pos2, pos3, pos4, out,
 ):
     nc = tc.nc
-    word_loads = [range(e, min(e + 2, E + 1)) for e in range(0, E + 1, 2)]
+    word_loads = [range(e, e + 2) for e in range(E - 2, -1, -2)] + [range(E, E + 1)]
     with ExitStack() as ctx:
         lists = ctx.enter_context(tc.tile_pool(name="lists", bufs=1))
         keep = ctx.enter_context(tc.tile_pool(name="keep", bufs=1))
@@ -60,23 +67,27 @@ def tile_moe_shr_glu_relu_kernel(
         xw = keep.tile([P, T], I32, name="xw", align_bytes=64)
         xs = keep.tile([P, T], U8, name="xs", align_bytes=64)
         up_words = [[keep.tile([P, len(members), 2 * H], U8, name=f"up_words{m}_{g}", tag=f"up_words{m}_{g}",
-                               align_bytes=64)
-                     for g, members in enumerate(word_loads)] for m in (W1, W3)]
-        up_planes = [[keep.tile([P, len(members), H], U8, name=f"up_planes{m}_{g}", align_bytes=64)
-                      for g, members in enumerate(SCALE_RUNS[:2])] for m in (W1, W3)]
+                               align_bytes=64)[:]
+                     for g, members in enumerate(word_loads) if m == W3 or 0 < g < PAIRS] for m in (W1, W3)]
+        first_words = keep.tile([P, 3, 2 * H], U8, name="first_words", align_bytes=64)
+        up_words[W1] = [first_words[:, 0:2]] + up_words[W1] + [first_words[:, 2:3]]
+        zeroed = [[keep.tile([P, 6 if g else (6, 5)[m], H], U8, name=f"up_planes{m}_{g}", align_bytes=64)
+                   for g in range(2)] for m in (W1, W3)]
+        up_planes = [[zeroed[W1][0][:], zeroed[W1][1][:], zeroed[W1][0][:]],
+                     [zeroed[W3][0][:], zeroed[W3][1][:],
+                      first_words[:].rearrange("p e (two i) -> p (e two) i", two=2)]]
         down_words = [keep.tile([P, len(members), 2 * N], U8, name=f"down_words{g}", align_bytes=64)
                       for g, members in enumerate(W2_LOADS)]
-        plane_bytes = up_planes[W1][1][:].rearrange("p e i -> p (e i)")
-        down_plane = plane_bytes[:, 0:(E + 1) * N].rearrange("p (e n) -> p e n", n=N)
-        gate_t = [keep.tile([P, T], F32, name=f"gate_t{r}") for r in range(TOP)]
+        down_plane = keep.tile([P, E + 1, N], U8, name="down_plane", align_bytes=64)
+        gate_t = [keep.tile([P, T], F32, name=f"gate_t{r}", tag=f"gate_t{r}", align_bytes=64) for r in range(TOP)]
         y_slots = keep.tile([P, E * C], F32, name="y_slots")
         ident = keep.tile([P, P], F32, name="ident")
 
         nc.gpsimd.memset(xs[:].bitcast(I32), 0)
-        nc.vector.memset(up_planes[W1][0][:].bitcast(I32), 0)
-        nc.vector.memset(up_planes[W3][0][:].bitcast(I32), 0)
-        nc.vector.memset(up_planes[W1][1][:].bitcast(I32), 0)
-        nc.gpsimd.memset(up_planes[W3][1][:].bitcast(I32), 0)
+        for run in range(2):
+            for m in (W1, W3):
+                nc.vector.memset(zeroed[m][run][:].bitcast(I32), 0)
+        nc.vector.memset(down_plane[:].bitcast(I32), 0)
         make_identity(nc, ident[:])
 
         a_banks = [psum.tile([P, H], F32, name=f"a_bank{b}") for b in range(4)]
@@ -86,14 +97,14 @@ def tile_moe_shr_glu_relu_kernel(
         def load_up_words(m, pair):
             members = word_loads[pair]
             nc.sync.dma_start(
-                out=up_words[m][pair][:].bitcast(I32),
+                out=up_words[m][pair].bitcast(I32),
                 in_=(w1_words, w3_words)[m][members.start:members.stop, 0].rearrange("e p b -> p e b").bitcast(I32))
 
         def load_up_scales(m, run):
             members = SCALE_RUNS[run]
             rows = (w1_scales, w3_scales)[m][members.start:members.stop, 0]
             for r in range(4):
-                nc.sync.dma_start(out=up_planes[m][run % 2][:].bitcast(I32)[r:P:32, 0:len(members)],
+                nc.sync.dma_start(out=up_planes[m][run].bitcast(I32)[r:P:32, 0:len(members)],
                                   in_=rows[:, r:16:4, :].rearrange("e q i -> q e i").bitcast(I32))
 
         def load_down_words(g):
@@ -102,52 +113,53 @@ def tile_moe_shr_glu_relu_kernel(
                               in_=w2_words[members.start:members.stop, 0].rearrange("e p b -> p e b").bitcast(I32))
 
         def load_scales_for(m, pair):
-            run, place = holder(SCALE_RUNS, 2 * pair)
-            if place == 0:
+            run, place = holder(SCALE_RUNS, expert(2 * pair + 1))
+            if place == len(SCALE_RUNS[run]) - 1:
                 load_up_scales(m, run)
 
-        def load_step(q):
+        def load_step(q, w3_too=True):
             load_scales_for(W3, q)
-            if q + RELU_AHEAD <= PAIRS:
+            if q >= W3_FIRST:
+                load_up_words(W3, q)
+            if q + RELU_AHEAD < PAIRS:
                 load_scales_for(W1, q + RELU_AHEAD)
+                if q == 3:
+                    for r in range(4):
+                        nc.sync.dma_start(out=down_plane[:].bitcast(I32)[r:P:32],
+                                          in_=w2_scales[:, 0, r:16:4, :].rearrange("e q n -> q e n").bitcast(I32))
                 load_up_words(W1, q + RELU_AHEAD)
-            load_up_words(W3, q)
+            if w3_too and q < W3_FIRST:
+                load_up_words(W3, q)
 
         def load_rest():
-            for r in range(4):
-                nc.sync.dma_start(out=down_plane.bitcast(I32)[r:P:32],
-                                  in_=w2_scales[:, 0, r:16:4, :].rearrange("e q n -> q e n").bitcast(I32))
             load_down_words(0)
-            load_down_words(1)
             load_up_words(W3, PAIRS)
+            load_down_words(1)
             load_down_words(2)
             load_down_words(3)
             for r, pos in enumerate((pos1, pos2, pos3, pos4)):
                 nc.sync.dma_start(pos_t[r][:], pos)
                 nc.sync.dma_start(out=gate_t[r][:], in_=gate[r])
 
-        nc.sync.dma_start(out=xw[:], in_=x_words[0].rearrange("p t r -> p (t r)").bitcast(I32))
+        nc.sync.dma_start(offs_t[:], offs)
         for r in range(4):
             nc.sync.dma_start(out=xs[:].bitcast(I32)[r:P:32], in_=x_scales[0, r:16:4, :].bitcast(I32))
-        nc.sync.dma_start(offs_t[:], offs)
-        load_up_words(W1, 0)
-        load_up_words(W3, 0)
+        nc.sync.dma_start(out=xw[:], in_=x_words[0].rearrange("p t r -> p (t r)").bitcast(I32))
+        load_up_words(W1, PAIRS)
         load_up_scales(W1, 0)
-        load_up_scales(W3, 0)
+        load_up_words(W1, 0)
         load_up_words(W1, 1)
-        load_up_words(W1, RELU_AHEAD)
-        load_up_words(W3, 1)
-        load_scales_for(W1, 1 + RELU_AHEAD)
-        load_up_words(W1, 1 + RELU_AHEAD)
-        for q in range(2, LOAD_AHEAD):
-            load_step(q)
+        load_up_scales(W3, 0)
+        load_up_words(W3, 0)
+        load_step(0, w3_too=False)
+        load_step(1)
 
         slot_words = keep.tile([P, GATHER_AHEAD * 2 * C], U32, name="slot_words", align_bytes=64)
         slot_plane = keep.tile([P, GATHER_AHEAD * 2 * C], U8, name="slot_plane", align_bytes=64)
 
         def gather(pair):
             place = block(pair % GATHER_AHEAD, 2 * C)
-            entries = offs_t[:, block(pair, 2 * LIST_COLUMNS)]
+            entries = offs_t[:, block(PAIRS - 1 - pair, 2 * LIST_COLUMNS)]
             nc.vector.tensor_copy(out=slot_words[:, place], in_=xw[:].bitcast(U32).indirect(entries))
             nc.vector.tensor_copy(out=slot_plane[:, place], in_=xs[:].indirect(entries))
 
@@ -164,12 +176,12 @@ def tile_moe_shr_glu_relu_kernel(
             else:
                 cols = block(unit - E)
                 words, plane = xw[:, cols], xs[:, cols]
-            e = min(unit, E)
+            e = expert(unit)
             load, place = holder(word_loads, e)
             run, row = holder(SCALE_RUNS, e)
             nc.tensor.matmul_mx(out=bank[:], lhsT=words.bitcast(FP8X4), lhsT_scale=plane,
                                 rhs=up_words[m][load][:, place, :].bitcast(FP4X4),
-                                rhs_scale=up_planes[m][run % 2][:, row, :], start=True, stop=True)
+                                rhs_scale=up_planes[m][run][:, row, :], start=True, stop=True)
 
         def w1_side(unit, bank):
             first_layer(W1, unit, bank)
@@ -198,7 +210,7 @@ def tile_moe_shr_glu_relu_kernel(
 
         def quantise(g):
             width = len(QUANT_GROUPS[g]) * 2 * C
-            tag = f"up_words{W3}_{GATHER_AHEAD + g}" if g < LATE_GROUPS else f"codes{g}"
+            tag = QUANT_AFTER.get(g, f"codes{g}")
             codes = keep.tile([P, width], U32, name=f"codes{g}", tag=tag, align_bytes=64)
             plane = keep.tile([P, width], U8, name=f"h_plane{g}", align_bytes=64)
             nc.vector.quantize_mx(out=codes[:].bitcast(FP8X4), scales=plane[:], in_=turned[g][:])
@@ -218,22 +230,27 @@ def tile_moe_shr_glu_relu_kernel(
             load, place = holder(W2_LOADS, e)
             return down_words[load][:, place, :].bitcast(FP4X4), down_plane[:, e, :]
 
-        def second_layer(g, bank):
-            for j in range(4):
-                words, plane = w2_operand(4 * g + j)
-                codes, h_plane = h_operand(4 * g + j)
-                nc.tensor.matmul_mx(out=bank[:, block(j)], lhsT=words, lhsT_scale=plane,
+        def second_layer(units, bank):
+            first = min(expert(unit) for unit in units)
+            for unit in reversed(units):
+                words, plane = w2_operand(expert(unit))
+                codes, h_plane = h_operand(unit)
+                nc.tensor.matmul_mx(out=bank[:, block(expert(unit) - first)], lhsT=words, lhsT_scale=plane,
                                     rhs=codes, rhs_scale=h_plane, start=True, stop=True)
-            nc.scalar.copy(out=y_slots[:, block(g, 4 * C)], in_=bank[:])
+            nc.scalar.copy(out=y_slots[:, first * C:(first + len(units)) * C], in_=bank[:, 0:len(units) * C])
 
         for pair in range(GATHER_AHEAD):
             gather(pair)
+        for j in range(EARLY_SHARED):
+            w1_side(E + j, (b_banks + [spare_bank])[j])
         for unit in range(2 * RELU_AHEAD):
             w1_side(unit, a_banks[unit])
+        for q in range(2, LOAD_AHEAD):
+            load_step(q)
         for q in range(PAIRS):
-            if q + RELU_AHEAD <= PAIRS:
+            if q + RELU_AHEAD < PAIRS + (EARLY_SHARED == 2):
                 for j in range(2):
-                    w1_side(2 * (q + RELU_AHEAD) + j, a_banks[(2 * q + j) % 4])
+                    w1_side(2 * (q + RELU_AHEAD) + j + 2 * (q + RELU_AHEAD == PAIRS), a_banks[(2 * q + j) % 4])
             w3_side(2 * q)
             w3_side(2 * q + 1)
             if q + LOAD_AHEAD < PAIRS:
@@ -242,28 +259,31 @@ def tile_moe_shr_glu_relu_kernel(
                 load_rest()
             if q >= 1:
                 turn(q - 1, a_banks[(2 * q) % 4])
-            if q >= GATHER_AHEAD:
-                quantise(q - GATHER_AHEAD)
+            if q in (3, 5):
+                quantise(q // 2 - 1)
             if q + GATHER_AHEAD < PAIRS:
                 gather(q + GATHER_AHEAD)
 
-        w3_side(E)
-        w3_side(E + 1)
-        turn_and_quantise(PAIRS - 1, a_banks[0])
-        w1_side(E + 2, spare_bank)
-        w1_side(E + 3, spare_bank)
-        for g, bank in enumerate((a_banks[3], a_banks[1], spare_bank, a_banks[0])):
-            second_layer(g, bank)
-        turn_and_quantise(PAIRS, a_banks[2])
-        w3_side(E + 2)
-        w3_side(E + 3)
-        turn_and_quantise(PAIRS + 1, a_banks[0])
+        second_layer(range(0, 4), a_banks[1])
+        turn(PAIRS - 1, spare_bank)
+        second_layer(range(4, 8), a_banks[2])
+        quantise(2)
+        quantise(3)
+        quantise(4)
+        for unit in range(E, E + CHUNKS):
+            w3_side(unit)
+        second_layer(range(8, 12), a_banks[0])
+        second_layer(range(12, 14), a_banks[1])
+        second_layer(range(14, 16), a_banks[3])
+        turn(PAIRS, a_banks[1])
+        turn(PAIRS + 1, a_banks[3])
 
+        quantise(len(QUANT_GROUPS) - 1)
         late = keep.tile([P, 2, T], F32, name="late", tag=f"turned{len(QUANT_GROUPS) - 1}", align_bytes=64)
         prod = [keep.tile([P, T], F32, name="prod0")[:], keep.tile([P, T], F32, name="prod1")[:],
                 late[:, 0, :], late[:, 1, :]]
-        sum_banks = [a_banks[2], a_banks[3], b_banks[2], b_banks[0]]
-        back_banks = [a_banks[0], a_banks[1], b_banks[1], spare_bank]
+        sum_banks = b_banks + [spare_bank]
+        back_banks = [a_banks[1], a_banks[3], a_banks[0], a_banks[2]]
 
         def fetch(r, first, last):
             cols = slice(first * C, last * C)
@@ -280,7 +300,7 @@ def tile_moe_shr_glu_relu_kernel(
                 add_turned(sum_banks[c], prod[r][:, block(c)], r == 0, False)
         words, plane = w2_operand(E)
         shared_t = keep.tile([P, T], F32, name="shared_t")
-        for i, bank in enumerate((b_banks[1], spare_bank)):
+        for i, bank in enumerate((a_banks[0], a_banks[2])):
             for j in range(2):
                 codes, h_plane = h_operand(E + 2 * i + j)
                 nc.tensor.matmul_mx(out=bank[:, block(j)], lhsT=codes, lhsT_scale=h_plane,

@@ -31,7 +31,7 @@ SCALE_RUNS = [range(12, E + 1), range(6, 12), range(0, 6)]
 W2_LOADS = [range(12, E + 1), range(8, 12), range(4, 8), range(0, 4)]
 EARLY_SHARED = 4
 W3_FIRST = 5
-LOAD_AHEAD = 4
+LOAD_AHEAD = 3
 LATE_GROUPS = 3
 QUANT_GROUPS = ([range(2 * g, 2 * g + 2) for g in range(LATE_GROUPS)]
                 + [range(q, q + 1) for q in range(2 * LATE_GROUPS, PAIRS)] + [range(PAIRS, PAIRS + 2)])
@@ -68,18 +68,20 @@ def tile_moe_shr_glu_relu_kernel(
         xs = keep.tile([P, T], U8, name="xs", align_bytes=64)
         up_words = [[keep.tile([P, len(members), 2 * H], U8, name=f"up_words{m}_{g}", tag=f"up_words{m}_{g}",
                                align_bytes=64)[:]
-                     for g, members in enumerate(word_loads) if m == W3 or 0 < g < PAIRS] for m in (W1, W3)]
-        first_words = keep.tile([P, 3, 2 * H], U8, name="first_words", align_bytes=64)
-        up_words[W1] = [first_words[:, 0:2]] + up_words[W1] + [first_words[:, 2:3]]
+                     for g, members in enumerate(word_loads) if m == W3 or 2 < g < PAIRS] for m in (W1, W3)]
+        first_words = keep.tile([P, 7, 2 * H], U8, name="first_words", align_bytes=64)
+        up_words[W1] = ([first_words[:, 4:6], first_words[:, 2:4], first_words[:, 0:2]] + up_words[W1]
+                        + [first_words[:, 6:7]])
         zeroed = [[keep.tile([P, 6 if g else (6, 5)[m], H], U8, name=f"up_planes{m}_{g}", align_bytes=64)
                    for g in range(2)] for m in (W1, W3)]
         up_planes = [[zeroed[W1][0][:], zeroed[W1][1][:], zeroed[W1][0][:]],
                      [zeroed[W3][0][:], zeroed[W3][1][:],
-                      first_words[:].rearrange("p e (two i) -> p (e two) i", two=2)]]
+                      first_words[:, 4:7].rearrange("p e (two i) -> p (e two) i", two=2)]]
         down_words = [keep.tile([P, len(members), 2 * N], U8, name=f"down_words{g}", align_bytes=64)
                       for g, members in enumerate(W2_LOADS)]
-        down_plane = keep.tile([P, E + 1, N], U8, name="down_plane", align_bytes=64)
-        gate_t = [keep.tile([P, T], F32, name=f"gate_t{r}", tag=f"gate_t{r}", align_bytes=64) for r in range(TOP)]
+        down_plane = first_words[:].rearrange("p e b -> p (e b)")[:, 0:(E + 1) * N].rearrange("p (e n) -> p e n", n=N)
+        gate_pairs = [keep.tile([P, 2, T], F32, name=f"gate_pair{i}") for i in range(2)]
+        gate_t = [gate_pairs[r // 2][:, r % 2] for r in range(TOP)]
         y_slots = keep.tile([P, E * C], F32, name="y_slots")
         ident = keep.tile([P, P], F32, name="ident")
 
@@ -87,7 +89,6 @@ def tile_moe_shr_glu_relu_kernel(
         for run in range(2):
             for m in (W1, W3):
                 nc.vector.memset(zeroed[m][run][:].bitcast(I32), 0)
-        nc.vector.memset(down_plane[:].bitcast(I32), 0)
         make_identity(nc, ident[:])
 
         a_banks = [psum.tile([P, H], F32, name=f"a_bank{b}") for b in range(4)]
@@ -125,7 +126,7 @@ def tile_moe_shr_glu_relu_kernel(
                 load_scales_for(W1, q + RELU_AHEAD)
                 if q == 3:
                     for r in range(4):
-                        nc.sync.dma_start(out=down_plane[:].bitcast(I32)[r:P:32],
+                        nc.sync.dma_start(out=down_plane.bitcast(I32)[r:P:32],
                                           in_=w2_scales[:, 0, r:16:4, :].rearrange("e q n -> q e n").bitcast(I32))
                 load_up_words(W1, q + RELU_AHEAD)
             if w3_too and q < W3_FIRST:
@@ -137,9 +138,10 @@ def tile_moe_shr_glu_relu_kernel(
             load_down_words(1)
             load_down_words(2)
             load_down_words(3)
-            for r, pos in enumerate((pos1, pos2, pos3, pos4)):
-                nc.sync.dma_start(pos_t[r][:], pos)
-                nc.sync.dma_start(out=gate_t[r][:], in_=gate[r])
+            for i, pair in enumerate(((pos1, pos2), (pos3, pos4))):
+                for j, pos in enumerate(pair):
+                    nc.sync.dma_start(pos_t[2 * i + j][:], pos)
+                nc.sync.dma_start(out=gate_pairs[i][:], in_=gate[2 * i:2 * i + 2].rearrange("r n t -> n r t"))
 
         nc.sync.dma_start(offs_t[:], offs)
         for r in range(4):
@@ -279,9 +281,7 @@ def tile_moe_shr_glu_relu_kernel(
         turn(PAIRS + 1, a_banks[3])
 
         quantise(len(QUANT_GROUPS) - 1)
-        late = keep.tile([P, 2, T], F32, name="late", tag=f"turned{len(QUANT_GROUPS) - 1}", align_bytes=64)
-        prod = [keep.tile([P, T], F32, name="prod0")[:], keep.tile([P, T], F32, name="prod1")[:],
-                late[:, 0, :], late[:, 1, :]]
+        prod = [keep.tile([P, T], F32, name=f"prod{r}") for r in range(TOP)]
         sum_banks = b_banks + [spare_bank]
         back_banks = [a_banks[1], a_banks[3], a_banks[0], a_banks[2]]
 

@@ -26,15 +26,14 @@ CHUNKS = T // C
 LIST_COLUMNS = C // 16
 RELU_AHEAD = 2
 GATHER_AHEAD = 5
-B_BANKS = 3
+B_BANKS = 4
 SCALE_RUNS = [range(12, E + 1), range(6, 12), range(0, 6)]
 W2_LOADS = [range(12, E + 1), range(8, 12), range(4, 8), range(0, 4)]
 EARLY_SHARED = 4
 W3_FIRST = 5
 LOAD_AHEAD = 3
 LATE_GROUPS = 3
-QUANT_GROUPS = ([range(2 * g, 2 * g + 2) for g in range(LATE_GROUPS)]
-                + [range(q, q + 1) for q in range(2 * LATE_GROUPS, PAIRS)] + [range(PAIRS, PAIRS + 2)])
+QUANT_GROUPS = [range(0, 4), range(4, 8), range(8, 12), range(12, 14), range(14, 16), range(16, 20)]
 QUANT_AFTER = {0: f"up_words{W3}_3", 1: f"up_words{W3}_5", 2: f"up_words{W3}_7"}
 
 
@@ -93,7 +92,6 @@ def tile_moe_shr_glu_relu_kernel(
 
         a_banks = [psum.tile([P, H], F32, name=f"a_bank{b}") for b in range(4)]
         b_banks = [psum.tile([P, H], F32, name=f"b_bank{b}") for b in range(B_BANKS)]
-        spare_bank = psum.tile([P, H], F32, name="spare_bank")
 
         def load_up_words(m, pair):
             members = word_loads[pair]
@@ -133,8 +131,8 @@ def tile_moe_shr_glu_relu_kernel(
                 load_up_words(W3, q)
 
         def load_rest():
-            load_down_words(0)
             load_up_words(W3, PAIRS)
+            load_down_words(0)
             load_down_words(1)
             load_down_words(2)
             load_down_words(3)
@@ -168,7 +166,7 @@ def tile_moe_shr_glu_relu_kernel(
         from_bank = "s (p u v) -> s u p v"
         as_laid = "s (u p v) -> s u p v"
         relu_a, h, quantised = {}, {}, {}
-        turned = [keep.tile([P, len(group) * 2 * H], BF16, name=f"turned{g}", tag=f"turned{g}", align_bytes=64)
+        turned = [keep.tile([P, len(group) * H], BF16, name=f"turned{g}", tag=f"turned{g}", align_bytes=64)
                   for g, group in enumerate(QUANT_GROUPS)]
 
         def first_layer(m, unit, bank):
@@ -194,39 +192,37 @@ def tile_moe_shr_glu_relu_kernel(
         def w3_side(unit):
             bank = b_banks[unit % B_BANKS]
             first_layer(W3, unit, bank)
-            h[unit] = keep.tile([P, H], BF16, name=f"h{unit}", align_bytes=64)
+            h[unit] = last_h[:, unit - E - 2] if unit >= E + 2 else keep.tile([P, H], BF16, name=f"h{unit}", align_bytes=64)
             nc.vector.tensor_tensor(out=h[unit][:].rearrange(as_laid, u=2, v=2),
                                     in0=bank[:].rearrange(from_bank, u=2, v=2),
                                     in1=relu_a[unit][:].rearrange(as_laid, u=2, v=2), op=MULT)
 
-        def turn(pair, bank):
-            blocks = bank[:].rearrange("p (j u s) -> p j u s", j=2, u=2)
-            for j in (1, 0):
-                words = h[2 * pair + j][:].bitcast(F32)
+        def turn(units, bank):
+            blocks = bank[:, 0:len(units) * H // 2].rearrange("p (j u s) -> p j u s", u=2, s=C)
+            for j in reversed(range(len(units))):
+                words = h[units[j]][:].bitcast(F32)
                 for u in range(2):
                     nc.tensor.transpose(blocks[:, j, u, :], words[:, block(u)], ident[:])
-            g, place = holder(QUANT_GROUPS, pair)
-            laid = turned[g][:].bitcast(F32)[:, block(place, H)]
-            nc.scalar.copy(out=laid.rearrange("p (j s u) -> p j s u", j=2, u=2),
+            g, place = holder(QUANT_GROUPS, units.start)
+            laid = turned[g][:].bitcast(F32)[:, place * H // 2:(place + len(units)) * H // 2]
+            nc.scalar.copy(out=laid.rearrange("p (j s u) -> p j s u", u=2, s=C),
                            in_=blocks.rearrange("p j u s -> p j s u"))
 
         def quantise(g):
-            width = len(QUANT_GROUPS[g]) * 2 * C
+            width = len(QUANT_GROUPS[g]) * C
             tag = QUANT_AFTER.get(g, f"codes{g}")
             codes = keep.tile([P, width], U32, name=f"codes{g}", tag=tag, align_bytes=64)
             plane = keep.tile([P, width], U8, name=f"h_plane{g}", align_bytes=64)
             nc.vector.quantize_mx(out=codes[:].bitcast(FP8X4), scales=plane[:], in_=turned[g][:])
             quantised[g] = (codes, plane)
 
-        def turn_and_quantise(pair, bank):
-            turn(pair, bank)
-            quantise(holder(QUANT_GROUPS, pair)[0])
-
         def h_operand(unit):
-            g, place = holder(QUANT_GROUPS, unit // 2)
+            g, place = holder(QUANT_GROUPS, unit)
             codes, plane = quantised[g]
-            cols = block(2 * place + unit % 2)
-            return codes[:, cols].bitcast(FP8X4), plane[:, cols]
+            return codes[:, block(place)].bitcast(FP8X4), plane[:, block(place)]
+
+        def pair_units(q):
+            return range(2 * q, 2 * q + 2)
 
         def w2_operand(e):
             load, place = holder(W2_LOADS, e)
@@ -244,7 +240,7 @@ def tile_moe_shr_glu_relu_kernel(
         for pair in range(GATHER_AHEAD):
             gather(pair)
         for j in range(EARLY_SHARED):
-            w1_side(E + j, (b_banks + [spare_bank])[j])
+            w1_side(E + j, b_banks[j])
         for unit in range(2 * RELU_AHEAD):
             w1_side(unit, a_banks[unit])
         for q in range(2, LOAD_AHEAD):
@@ -259,31 +255,41 @@ def tile_moe_shr_glu_relu_kernel(
                 load_step(q + LOAD_AHEAD)
             if q + LOAD_AHEAD == PAIRS:
                 load_rest()
-            if q >= 1:
-                turn(q - 1, a_banks[(2 * q) % 4])
+            if q in (1, 2):
+                turn(pair_units(q - 1), a_banks[(2 * q) % 4])
+            if q == 4:
+                turn(pair_units(2), a_banks[0])
+                turn(pair_units(3), a_banks[1])
+            if q == 6:
+                turn(pair_units(4), a_banks[2])
+                turn(pair_units(5), a_banks[0])
             if q in (3, 5):
                 quantise(q // 2 - 1)
             if q + GATHER_AHEAD < PAIRS:
                 gather(q + GATHER_AHEAD)
 
         second_layer(range(0, 4), a_banks[1])
-        turn(PAIRS - 1, spare_bank)
-        second_layer(range(4, 8), a_banks[2])
+        second_layer(range(4, 8), a_banks[3])
         quantise(2)
+        w3_side(E)
+        w3_side(E + 1)
+        turn(pair_units(PAIRS - 2), a_banks[2])
+        turn(pair_units(PAIRS - 1), a_banks[0])
         quantise(3)
         quantise(4)
-        for unit in range(E, E + CHUNKS):
-            w3_side(unit)
-        second_layer(range(8, 12), a_banks[0])
-        second_layer(range(12, 14), a_banks[1])
-        second_layer(range(14, 16), a_banks[3])
-        turn(PAIRS, a_banks[1])
-        turn(PAIRS + 1, a_banks[3])
+        last_h = keep.tile([P, 2, H], BF16, name="last_h", tag="turned4", align_bytes=64)
+        second_layer(range(8, 12), a_banks[1])
+        second_layer(range(12, 14), a_banks[3])
+        second_layer(range(14, 16), a_banks[2])
+        w3_side(E + 2)
+        w3_side(E + 3)
+        turn(pair_units(PAIRS), b_banks[2])
+        turn(pair_units(PAIRS + 1), b_banks[3])
 
         quantise(len(QUANT_GROUPS) - 1)
         prod = [keep.tile([P, T], F32, name=f"prod{r}") for r in range(TOP)]
-        sum_banks = b_banks + [spare_bank]
-        back_banks = [a_banks[1], a_banks[3], a_banks[0], a_banks[2]]
+        sum_banks = [b_banks[0], b_banks[1], a_banks[3], a_banks[2]]
+        back_banks = [b_banks[2], b_banks[3], a_banks[0], a_banks[1]]
 
         def fetch(r, first, last):
             cols = slice(first * C, last * C)
@@ -300,7 +306,7 @@ def tile_moe_shr_glu_relu_kernel(
                 add_turned(sum_banks[c], prod[r][:, block(c)], r == 0, False)
         words, plane = w2_operand(E)
         shared_t = keep.tile([P, T], F32, name="shared_t")
-        for i, bank in enumerate((a_banks[0], a_banks[2])):
+        for i, bank in enumerate(a_banks[:2]):
             for j in range(2):
                 codes, h_plane = h_operand(E + 2 * i + j)
                 nc.tensor.matmul_mx(out=bank[:, block(j)], lhsT=codes, lhsT_scale=h_plane,

@@ -28,7 +28,7 @@ RELU_AHEAD = 2
 GATHER_AHEAD = 5
 B_BANKS = 4
 SCALE_RUNS = [range(12, E + 1), range(6, 12), range(0, 6)]
-W2_LOADS = [range(12, E + 1), range(8, 12), range(4, 8), range(0, 4)]
+W2_LOADS = [range(12, E + 1), range(8, 12), range(0, 8)]
 EARLY_SHARED = 4
 W3_FIRST = 5
 LOAD_AHEAD = 3
@@ -135,7 +135,6 @@ def tile_moe_shr_glu_relu_kernel(
             load_down_words(0)
             load_down_words(1)
             load_down_words(2)
-            load_down_words(3)
             for i, pair in enumerate(((pos1, pos2), (pos3, pos4))):
                 for j, pos in enumerate(pair):
                     nc.sync.dma_start(pos_t[2 * i + j][:], pos)
@@ -143,7 +142,7 @@ def tile_moe_shr_glu_relu_kernel(
 
         nc.sync.dma_start(offs_t[:], offs)
         for r in range(4):
-            nc.sync.dma_start(out=xs[:].bitcast(I32)[r:P:32], in_=x_scales[0, r:16:4, :].bitcast(I32))
+            (nc.sync, nc.scalar)[r // 2].dma_start(out=xs[:].bitcast(I32)[r:P:32], in_=x_scales[0, r:16:4, :].bitcast(I32))
         nc.sync.dma_start(out=xw[:], in_=x_words[0].rearrange("p t r -> p (t r)").bitcast(I32))
         load_up_words(W1, PAIRS)
         load_up_scales(W1, 0)
@@ -269,17 +268,17 @@ def tile_moe_shr_glu_relu_kernel(
                 gather(q + GATHER_AHEAD)
 
         second_layer(range(0, 4), a_banks[1])
-        second_layer(range(4, 8), a_banks[3])
         quantise(2)
         w3_side(E)
         w3_side(E + 1)
         turn(pair_units(PAIRS - 2), a_banks[2])
         turn(pair_units(PAIRS - 1), a_banks[0])
+        second_layer(range(4, 8), a_banks[3])
         quantise(3)
         quantise(4)
         last_h = keep.tile([P, 2, H], BF16, name="last_h", tag="turned4", align_bytes=64)
         second_layer(range(8, 12), a_banks[1])
-        second_layer(range(12, 14), a_banks[3])
+        second_layer(range(12, 14), a_banks[0])
         second_layer(range(14, 16), a_banks[2])
         w3_side(E + 2)
         w3_side(E + 3)
@@ -321,7 +320,9 @@ def tile_moe_shr_glu_relu_kernel(
             fetch(3, c, c + 1)
             add_turned(back_banks[c], shared_t[:, block(c)], True, False)
             add_turned(back_banks[c], sum_t[:, block(c)], False, True)
+        result = keep.tile([P, T], F32, name="result")
         for c in range(CHUNKS):
-            result = keep.tile([P, C], F32, name=f"result{c}")
-            nc.vector.tensor_tensor(out=result[:], in0=back_banks[c][:, 0:C], in1=prod[3][:, block(c)], op=ADD)
-            nc.sync.dma_start(out=out[:, block(c)], in_=result[:])
+            nc.vector.tensor_tensor(out=result[:, block(c)], in0=back_banks[c][:, 0:C], in1=prod[3][:, block(c)],
+                                    op=ADD)
+            if c % 2:
+                nc.sync.dma_start(out=out[:, block(c // 2, 2 * C)], in_=result[:, block(c // 2, 2 * C)])

@@ -24,17 +24,16 @@ W1, W3 = 0, 1
 PAIRS = E // 2
 CHUNKS = T // C
 LIST_COLUMNS = C // 16
+WORD_LOADS = [range(e, e + 2) for e in range(E - 2, -1, -2)] + [range(E, E + 1)]
 RELU_AHEAD = 2
 GATHER_AHEAD = 5
-B_BANKS = 4
 SCALE_RUNS = [range(12, E + 1), range(6, 12), range(0, 6)]
+FIRST_PAIRS = 3
 W2_LOADS = [range(12, E + 1), range(8, 12), range(0, 8)]
-EARLY_SHARED = 4
-W3_FIRST = 5
 LOAD_AHEAD = 3
-LATE_GROUPS = 3
-QUANT_GROUPS = [range(0, 4), range(4, 8), range(8, 12), range(12, 14), range(14, 16), range(16, 20)]
-QUANT_AFTER = {0: f"up_words{W3}_3", 1: f"up_words{W3}_5", 2: f"up_words{W3}_7"}
+W3_FIRST = 5
+QUANT_GROUPS = [range(0, 4), range(4, 8), range(8, 12), range(12, 14), range(14, 16), range(E, E + CHUNKS)]
+QUANT_STEPS = (PAIRS - GATHER_AHEAD, PAIRS - GATHER_AHEAD + 2, PAIRS - 1)
 
 
 def holder(groups, e):
@@ -43,7 +42,11 @@ def holder(groups, e):
 
 
 def expert(unit):
-    return E - 2 - unit + 2 * (unit % 2) if unit < E else E
+    return WORD_LOADS[unit // 2].start + unit % 2 if unit < E else E
+
+
+def pair_units(pair):
+    return range(2 * pair, 2 * pair + 2)
 
 
 def block(j, width=C):
@@ -55,7 +58,6 @@ def tile_moe_shr_glu_relu_kernel(
     gate, offs, pos1, pos2, pos3, pos4, out,
 ):
     nc = tc.nc
-    word_loads = [range(e, e + 2) for e in range(E - 2, -1, -2)] + [range(E, E + 1)]
     with ExitStack() as ctx:
         lists = ctx.enter_context(tc.tile_pool(name="lists", bufs=1))
         keep = ctx.enter_context(tc.tile_pool(name="keep", bufs=1))
@@ -65,22 +67,32 @@ def tile_moe_shr_glu_relu_kernel(
         pos_t = [lists.tile([P, CHUNKS * LIST_COLUMNS], U16, name=f"pos_t{r}") for r in range(TOP)]
         xw = keep.tile([P, T], I32, name="xw", align_bytes=64)
         xs = keep.tile([P, T], U8, name="xs", align_bytes=64)
-        up_words = [[keep.tile([P, len(members), 2 * H], U8, name=f"up_words{m}_{g}", tag=f"up_words{m}_{g}",
-                               align_bytes=64)[:]
-                     for g, members in enumerate(word_loads) if m == W3 or 2 < g < PAIRS] for m in (W1, W3)]
-        first_words = keep.tile([P, 7, 2 * H], U8, name="first_words", align_bytes=64)
-        up_words[W1] = ([first_words[:, 4:6], first_words[:, 2:4], first_words[:, 0:2]] + up_words[W1]
-                        + [first_words[:, 6:7]])
-        zeroed = [[keep.tile([P, 6 if g else (6, 5)[m], H], U8, name=f"up_planes{m}_{g}", align_bytes=64)
-                   for g in range(2)] for m in (W1, W3)]
+
+        def words_tile(m, load):
+            name = f"up_words{m}_{load}"
+            return keep.tile([P, len(WORD_LOADS[load]), 2 * H], U8, name=name, tag=name, align_bytes=64)[:]
+
+        later_w1 = [words_tile(W1, load) for load in range(FIRST_PAIRS, PAIRS)]
+        all_w3 = [words_tile(W3, load) for load in range(PAIRS + 1)]
+        first_words = keep.tile([P, 2 * FIRST_PAIRS + 1, 2 * H], U8, name="first_words", align_bytes=64)
+        first_expert = E - 2 * FIRST_PAIRS
+
+        def first_rows(members):
+            return first_words[:, members.start - first_expert:members.stop - first_expert]
+
+        up_words = [[first_rows(members) for members in WORD_LOADS[:FIRST_PAIRS]] + later_w1
+                    + [first_rows(WORD_LOADS[PAIRS])], all_w3]
+        plane_rows = [[len(SCALE_RUNS[2]), len(SCALE_RUNS[1])], [len(SCALE_RUNS[0]), len(SCALE_RUNS[1])]]
+        zeroed = [[keep.tile([P, rows, H], U8, name=f"up_planes{m}_{run}", align_bytes=64)
+                   for run, rows in enumerate(plane_rows[m])] for m in (W1, W3)]
+        spent_words = first_rows(range(WORD_LOADS[0].start, E + 1))
         up_planes = [[zeroed[W1][0][:], zeroed[W1][1][:], zeroed[W1][0][:]],
-                     [zeroed[W3][0][:], zeroed[W3][1][:],
-                      first_words[:, 4:7].rearrange("p e (two i) -> p (e two) i", two=2)]]
+                     [zeroed[W3][0][:], zeroed[W3][1][:], spent_words.rearrange("p e (two i) -> p (e two) i", two=2)]]
         down_words = [keep.tile([P, len(members), 2 * N], U8, name=f"down_words{g}", align_bytes=64)
                       for g, members in enumerate(W2_LOADS)]
         down_plane = first_words[:].rearrange("p e b -> p (e b)")[:, 0:(E + 1) * N].rearrange("p (e n) -> p e n", n=N)
-        gate_pairs = [keep.tile([P, 2, T], F32, name=f"gate_pair{i}") for i in range(2)]
-        gate_t = [gate_pairs[r // 2][:, r % 2] for r in range(TOP)]
+        gate_halves = [keep.tile([P, 2, T], F32, name=f"gate_half{i}") for i in range(TOP // 2)]
+        gate_t = [gate_halves[r // 2][:, r % 2] for r in range(TOP)]
         y_slots = keep.tile([P, E * C], F32, name="y_slots")
         ident = keep.tile([P, P], F32, name="ident")
 
@@ -90,67 +102,62 @@ def tile_moe_shr_glu_relu_kernel(
                 nc.vector.memset(zeroed[m][run][:].bitcast(I32), 0)
         make_identity(nc, ident[:])
 
-        a_banks = [psum.tile([P, H], F32, name=f"a_bank{b}") for b in range(4)]
-        b_banks = [psum.tile([P, H], F32, name=f"b_bank{b}") for b in range(B_BANKS)]
+        a_banks = [psum.tile([P, H], F32, name=f"a_bank{b}") for b in range(2 * RELU_AHEAD)]
+        b_banks = [psum.tile([P, H], F32, name=f"b_bank{b}") for b in range(8 - 2 * RELU_AHEAD)]
 
-        def load_up_words(m, pair):
-            members = word_loads[pair]
-            nc.sync.dma_start(
-                out=up_words[m][pair].bitcast(I32),
-                in_=(w1_words, w3_words)[m][members.start:members.stop, 0].rearrange("e p b -> p e b").bitcast(I32))
+        def load_words(tile, words, members):
+            nc.sync.dma_start(out=tile.bitcast(I32),
+                              in_=words[members.start:members.stop, 0].rearrange("e p b -> p e b").bitcast(I32))
 
-        def load_up_scales(m, run):
-            members = SCALE_RUNS[run]
-            rows = (w1_scales, w3_scales)[m][members.start:members.stop, 0]
+        def load_scales(plane, scales, members):
+            rows = scales[members.start:members.stop, 0]
             for r in range(4):
-                nc.sync.dma_start(out=up_planes[m][run].bitcast(I32)[r:P:32, 0:len(members)],
+                nc.sync.dma_start(out=plane.bitcast(I32)[r:P:32, 0:len(members)],
                                   in_=rows[:, r:16:4, :].rearrange("e q i -> q e i").bitcast(I32))
 
-        def load_down_words(g):
-            members = W2_LOADS[g]
-            nc.sync.dma_start(out=down_words[g][:].bitcast(I32),
-                              in_=w2_words[members.start:members.stop, 0].rearrange("e p b -> p e b").bitcast(I32))
+        def load_up_words(m, load):
+            load_words(up_words[m][load], (w1_words, w3_words)[m], WORD_LOADS[load])
 
-        def load_scales_for(m, pair):
-            run, place = holder(SCALE_RUNS, expert(2 * pair + 1))
-            if place == len(SCALE_RUNS[run]) - 1:
-                load_up_scales(m, run)
+        def load_run_opened_by(m, pair):
+            for run, members in enumerate(SCALE_RUNS):
+                if members.stop == WORD_LOADS[pair].stop:
+                    load_scales(up_planes[m][run], (w1_scales, w3_scales)[m], members)
 
-        def load_step(q, w3_too=True):
-            load_scales_for(W3, q)
+        def load_w1_of(pair):
+            load_run_opened_by(W1, pair)
+            if WORD_LOADS[pair].stop == SCALE_RUNS[-1].stop:
+                load_scales(down_plane, w2_scales, range(E + 1))
+            load_up_words(W1, pair)
+
+        def load_step(q):
+            load_run_opened_by(W3, q)
             if q >= W3_FIRST:
                 load_up_words(W3, q)
             if q + RELU_AHEAD < PAIRS:
-                load_scales_for(W1, q + RELU_AHEAD)
-                if q == 3:
-                    for r in range(4):
-                        nc.sync.dma_start(out=down_plane.bitcast(I32)[r:P:32],
-                                          in_=w2_scales[:, 0, r:16:4, :].rearrange("e q n -> q e n").bitcast(I32))
-                load_up_words(W1, q + RELU_AHEAD)
-            if w3_too and q < W3_FIRST:
+                load_w1_of(q + RELU_AHEAD)
+            if q < W3_FIRST:
                 load_up_words(W3, q)
 
         def load_rest():
             load_up_words(W3, PAIRS)
-            load_down_words(0)
-            load_down_words(1)
-            load_down_words(2)
-            for i, pair in enumerate(((pos1, pos2), (pos3, pos4))):
-                for j, pos in enumerate(pair):
+            for g, members in enumerate(W2_LOADS):
+                load_words(down_words[g][:], w2_words, members)
+            for i, half in enumerate(((pos1, pos2), (pos3, pos4))):
+                for j, pos in enumerate(half):
                     nc.sync.dma_start(pos_t[2 * i + j][:], pos)
-                nc.sync.dma_start(out=gate_pairs[i][:], in_=gate[2 * i:2 * i + 2].rearrange("r n t -> n r t"))
+                nc.sync.dma_start(out=gate_halves[i][:], in_=gate[2 * i:2 * i + 2].rearrange("r n t -> n r t"))
 
         nc.sync.dma_start(offs_t[:], offs)
         for r in range(4):
-            (nc.sync, nc.scalar)[r // 2].dma_start(out=xs[:].bitcast(I32)[r:P:32], in_=x_scales[0, r:16:4, :].bitcast(I32))
+            nc.sync.dma_start(out=xs[:].bitcast(I32)[r:P:32], in_=x_scales[0, r:16:4, :].bitcast(I32))
         nc.sync.dma_start(out=xw[:], in_=x_words[0].rearrange("p t r -> p (t r)").bitcast(I32))
         load_up_words(W1, PAIRS)
-        load_up_scales(W1, 0)
-        load_up_words(W1, 0)
-        load_up_words(W1, 1)
-        load_up_scales(W3, 0)
+        load_scales(up_planes[W1][0], w1_scales, SCALE_RUNS[0])
+        for pair in range(RELU_AHEAD):
+            load_up_words(W1, pair)
+        load_scales(up_planes[W3][0], w3_scales, SCALE_RUNS[0])
         load_up_words(W3, 0)
-        load_step(0, w3_too=False)
+        load_w1_of(RELU_AHEAD)
         load_step(1)
 
         slot_words = keep.tile([P, GATHER_AHEAD * 2 * C], U32, name="slot_words", align_bytes=64)
@@ -158,7 +165,7 @@ def tile_moe_shr_glu_relu_kernel(
 
         def gather(pair):
             place = block(pair % GATHER_AHEAD, 2 * C)
-            entries = offs_t[:, block(PAIRS - 1 - pair, 2 * LIST_COLUMNS)]
+            entries = offs_t[:, WORD_LOADS[pair].start * LIST_COLUMNS:WORD_LOADS[pair].stop * LIST_COLUMNS]
             nc.vector.tensor_copy(out=slot_words[:, place], in_=xw[:].bitcast(U32).indirect(entries))
             nc.vector.tensor_copy(out=slot_plane[:, place], in_=xs[:].indirect(entries))
 
@@ -175,9 +182,8 @@ def tile_moe_shr_glu_relu_kernel(
             else:
                 cols = block(unit - E)
                 words, plane = xw[:, cols], xs[:, cols]
-            e = expert(unit)
-            load, place = holder(word_loads, e)
-            run, row = holder(SCALE_RUNS, e)
+            load, place = holder(WORD_LOADS, expert(unit))
+            run, row = holder(SCALE_RUNS, expert(unit))
             nc.tensor.matmul_mx(out=bank[:], lhsT=words.bitcast(FP8X4), lhsT_scale=plane,
                                 rhs=up_words[m][load][:, place, :].bitcast(FP4X4),
                                 rhs_scale=up_planes[m][run][:, row, :], start=True, stop=True)
@@ -188,28 +194,32 @@ def tile_moe_shr_glu_relu_kernel(
             nc.scalar.activation(out=relu_a[unit][:].rearrange(as_laid, u=2, v=2),
                                  in_=bank[:].rearrange(from_bank, u=2, v=2), func=RELU)
 
-        def w3_side(unit):
-            bank = b_banks[unit % B_BANKS]
+        def w3_side(unit, h_unit):
+            bank = b_banks[unit % len(b_banks)]
             first_layer(W3, unit, bank)
-            h[unit] = last_h[:, unit - E - 2] if unit >= E + 2 else keep.tile([P, H], BF16, name=f"h{unit}", align_bytes=64)
-            nc.vector.tensor_tensor(out=h[unit][:].rearrange(as_laid, u=2, v=2),
+            h[unit] = h_unit
+            nc.vector.tensor_tensor(out=h_unit.rearrange(as_laid, u=2, v=2),
                                     in0=bank[:].rearrange(from_bank, u=2, v=2),
                                     in1=relu_a[unit][:].rearrange(as_laid, u=2, v=2), op=MULT)
 
-        def turn(units, bank):
-            blocks = bank[:, 0:len(units) * H // 2].rearrange("p (j u s) -> p j u s", u=2, s=C)
-            for j in reversed(range(len(units))):
-                words = h[units[j]][:].bitcast(F32)
+        def products(pair):
+            for unit in pair_units(pair):
+                w3_side(unit, keep.tile([P, H], BF16, name=f"h{unit}", align_bytes=64)[:])
+
+        def turn(pair, bank):
+            blocks = bank[:].rearrange("p (j u s) -> p j u s", j=2, u=2)
+            for j in (1, 0):
+                words = h[2 * pair + j].bitcast(F32)
                 for u in range(2):
                     nc.tensor.transpose(blocks[:, j, u, :], words[:, block(u)], ident[:])
-            g, place = holder(QUANT_GROUPS, units.start)
-            laid = turned[g][:].bitcast(F32)[:, place * H // 2:(place + len(units)) * H // 2]
-            nc.scalar.copy(out=laid.rearrange("p (j s u) -> p j s u", u=2, s=C),
+            g, place = holder(QUANT_GROUPS, 2 * pair)
+            laid = turned[g][:].bitcast(F32)[:, block(place // 2, H)]
+            nc.scalar.copy(out=laid.rearrange("p (j s u) -> p j s u", j=2, u=2),
                            in_=blocks.rearrange("p j u s -> p j s u"))
 
         def quantise(g):
             width = len(QUANT_GROUPS[g]) * C
-            tag = QUANT_AFTER.get(g, f"codes{g}")
+            tag = f"up_words{W3}_{QUANT_STEPS[g]}" if g < len(QUANT_STEPS) else f"codes{g}"
             codes = keep.tile([P, width], U32, name=f"codes{g}", tag=tag, align_bytes=64)
             plane = keep.tile([P, width], U8, name=f"h_plane{g}", align_bytes=64)
             nc.vector.quantize_mx(out=codes[:].bitcast(FP8X4), scales=plane[:], in_=turned[g][:])
@@ -220,75 +230,71 @@ def tile_moe_shr_glu_relu_kernel(
             codes, plane = quantised[g]
             return codes[:, block(place)].bitcast(FP8X4), plane[:, block(place)]
 
-        def pair_units(q):
-            return range(2 * q, 2 * q + 2)
-
         def w2_operand(e):
             load, place = holder(W2_LOADS, e)
             return down_words[load][:, place, :].bitcast(FP4X4), down_plane[:, e, :]
 
-        def second_layer(units, bank):
-            first = min(expert(unit) for unit in units)
+        def second_layer(g, bank):
+            units = QUANT_GROUPS[g]
+            lowest = min(expert(unit) for unit in units)
             for unit in reversed(units):
                 words, plane = w2_operand(expert(unit))
                 codes, h_plane = h_operand(unit)
-                nc.tensor.matmul_mx(out=bank[:, block(expert(unit) - first)], lhsT=words, lhsT_scale=plane,
+                nc.tensor.matmul_mx(out=bank[:, block(expert(unit) - lowest)], lhsT=words, lhsT_scale=plane,
                                     rhs=codes, rhs_scale=h_plane, start=True, stop=True)
-            nc.scalar.copy(out=y_slots[:, first * C:(first + len(units)) * C], in_=bank[:, 0:len(units) * C])
+            nc.scalar.copy(out=y_slots[:, lowest * C:(lowest + len(units)) * C], in_=bank[:, 0:len(units) * C])
 
         for pair in range(GATHER_AHEAD):
             gather(pair)
-        for j in range(EARLY_SHARED):
+        for j in range(CHUNKS):
             w1_side(E + j, b_banks[j])
         for unit in range(2 * RELU_AHEAD):
             w1_side(unit, a_banks[unit])
-        for q in range(2, LOAD_AHEAD):
-            load_step(q)
+        load_step(2)
+
         for q in range(PAIRS):
-            if q + RELU_AHEAD < PAIRS + (EARLY_SHARED == 2):
-                for j in range(2):
-                    w1_side(2 * (q + RELU_AHEAD) + j + 2 * (q + RELU_AHEAD == PAIRS), a_banks[(2 * q + j) % 4])
-            w3_side(2 * q)
-            w3_side(2 * q + 1)
+            ahead = q + RELU_AHEAD
+            if ahead < PAIRS:
+                for unit in pair_units(ahead):
+                    w1_side(unit, a_banks[unit % len(a_banks)])
+            products(q)
             if q + LOAD_AHEAD < PAIRS:
                 load_step(q + LOAD_AHEAD)
             if q + LOAD_AHEAD == PAIRS:
                 load_rest()
-            if q in (1, 2):
-                turn(pair_units(q - 1), a_banks[(2 * q) % 4])
-            if q == 4:
-                turn(pair_units(2), a_banks[0])
-                turn(pair_units(3), a_banks[1])
-            if q == 6:
-                turn(pair_units(4), a_banks[2])
-                turn(pair_units(5), a_banks[0])
-            if q in (3, 5):
-                quantise(q // 2 - 1)
+            newest = 2 * min(ahead, PAIRS - 1) % len(a_banks)
+            if 1 <= q < PAIRS - GATHER_AHEAD:
+                turn(q - 1, a_banks[newest])
+            elif q > PAIRS - GATHER_AHEAD and q % 2 == 0:
+                turn(q - 2, a_banks[newest])
+                turn(q - 1, a_banks[newest + 1 if ahead < PAIRS else 0])
+            if q in QUANT_STEPS[:-1]:
+                quantise(QUANT_STEPS.index(q))
             if q + GATHER_AHEAD < PAIRS:
                 gather(q + GATHER_AHEAD)
 
-        second_layer(range(0, 4), a_banks[1])
+        second_layer(0, a_banks[1])
         quantise(2)
-        w3_side(E)
-        w3_side(E + 1)
-        turn(pair_units(PAIRS - 2), a_banks[2])
-        turn(pair_units(PAIRS - 1), a_banks[0])
-        second_layer(range(4, 8), a_banks[3])
+        products(PAIRS)
+        turn(PAIRS - 2, a_banks[2])
+        turn(PAIRS - 1, a_banks[0])
+        second_layer(1, a_banks[3])
         quantise(3)
         quantise(4)
         last_h = keep.tile([P, 2, H], BF16, name="last_h", tag="turned4", align_bytes=64)
-        second_layer(range(8, 12), a_banks[1])
-        second_layer(range(12, 14), a_banks[0])
-        second_layer(range(14, 16), a_banks[2])
-        w3_side(E + 2)
-        w3_side(E + 3)
-        turn(pair_units(PAIRS), b_banks[2])
-        turn(pair_units(PAIRS + 1), b_banks[3])
+        second_layer(2, a_banks[1])
+        second_layer(3, a_banks[0])
+        second_layer(4, a_banks[2])
+        for j, unit in enumerate(pair_units(PAIRS + 1)):
+            w3_side(unit, last_h[:, j])
+        turn(PAIRS, b_banks[2])
+        turn(PAIRS + 1, b_banks[3])
+        quantise(5)
 
-        quantise(len(QUANT_GROUPS) - 1)
         prod = [keep.tile([P, T], F32, name=f"prod{r}") for r in range(TOP)]
         sum_banks = [b_banks[0], b_banks[1], a_banks[3], a_banks[2]]
-        back_banks = [b_banks[2], b_banks[3], a_banks[0], a_banks[1]]
+        shared_banks = a_banks[:2]
+        back_banks = b_banks[2:] + shared_banks
 
         def fetch(r, first, last):
             cols = slice(first * C, last * C)
@@ -305,9 +311,9 @@ def tile_moe_shr_glu_relu_kernel(
                 add_turned(sum_banks[c], prod[r][:, block(c)], r == 0, False)
         words, plane = w2_operand(E)
         shared_t = keep.tile([P, T], F32, name="shared_t")
-        for i, bank in enumerate(a_banks[:2]):
-            for j in range(2):
-                codes, h_plane = h_operand(E + 2 * i + j)
+        for i, bank in enumerate(shared_banks):
+            for j, unit in enumerate(pair_units(PAIRS + i)):
+                codes, h_plane = h_operand(unit)
                 nc.tensor.matmul_mx(out=bank[:, block(j)], lhsT=codes, lhsT_scale=h_plane,
                                     rhs=words, rhs_scale=plane, start=True, stop=True)
             nc.scalar.copy(out=shared_t[:, block(i, 2 * C)], in_=bank[:, 0:2 * C])
@@ -321,8 +327,8 @@ def tile_moe_shr_glu_relu_kernel(
             add_turned(back_banks[c], shared_t[:, block(c)], True, False)
             add_turned(back_banks[c], sum_t[:, block(c)], False, True)
         result = keep.tile([P, T], F32, name="result")
-        for c in range(CHUNKS):
-            nc.vector.tensor_tensor(out=result[:, block(c)], in0=back_banks[c][:, 0:C], in1=prod[3][:, block(c)],
-                                    op=ADD)
-            if c % 2:
-                nc.sync.dma_start(out=out[:, block(c // 2, 2 * C)], in_=result[:, block(c // 2, 2 * C)])
+        for half in range(2):
+            for c in range(2 * half, 2 * half + 2):
+                nc.vector.tensor_tensor(out=result[:, block(c)], in0=back_banks[c][:, 0:C], in1=prod[3][:, block(c)],
+                                        op=ADD)
+            nc.sync.dma_start(out=out[:, block(half, 2 * C)], in_=result[:, block(half, 2 * C)])

@@ -29,7 +29,7 @@ RELU_AHEAD = 2
 GATHER_AHEAD = 5
 SCALE_RUNS = [range(12, E + 1), range(6, 12), range(0, 6)]
 FIRST_PAIRS = 3
-W2_LOADS = [range(12, E + 1), range(8, 12), range(0, 8)]
+W2_LOADS = [range(E + 1)]
 LOAD_AHEAD = 3
 W3_FIRST = 5
 QUANT_GROUPS = [range(0, 4), range(4, 8), range(8, 12), range(12, 14), range(14, 16), range(E, E + CHUNKS)]
@@ -90,7 +90,7 @@ def tile_moe_shr_glu_relu_kernel(
                      [zeroed[W3][0][:], zeroed[W3][1][:], spent_words.rearrange("p e (two i) -> p (e two) i", two=2)]]
         down_words = [keep.tile([P, len(members), 2 * N], U8, name=f"down_words{g}", align_bytes=64)
                       for g, members in enumerate(W2_LOADS)]
-        down_plane = first_words[:].rearrange("p e b -> p (e b)")[:, 0:(E + 1) * N].rearrange("p (e n) -> p e n", n=N)
+        down_plane = zeroed[W1][1][:].rearrange("p e b -> p (e b)")[:, 0:(E + 1) * N].rearrange("p (e n) -> p e n", n=N)
         gate_halves = [keep.tile([P, 2, T], F32, name=f"gate_half{i}") for i in range(TOP // 2)]
         gate_t = [gate_halves[r // 2][:, r % 2] for r in range(TOP)]
         y_slots = keep.tile([P, E * C], F32, name="y_slots")
@@ -125,8 +125,6 @@ def tile_moe_shr_glu_relu_kernel(
 
         def load_w1_of(pair):
             load_run_opened_by(W1, pair)
-            if WORD_LOADS[pair].stop == SCALE_RUNS[-1].stop:
-                load_scales(down_plane, w2_scales, range(E + 1))
             load_up_words(W1, pair)
 
         def load_step(q):
@@ -140,6 +138,7 @@ def tile_moe_shr_glu_relu_kernel(
 
         def load_rest():
             load_up_words(W3, PAIRS)
+            load_scales(down_plane, w2_scales, range(E + 1))
             for g, members in enumerate(W2_LOADS):
                 load_words(down_words[g][:], w2_words, members)
             for i, half in enumerate(((pos1, pos2), (pos3, pos4))):
@@ -194,8 +193,7 @@ def tile_moe_shr_glu_relu_kernel(
             nc.scalar.activation(out=relu_a[unit][:].rearrange(as_laid, u=2, v=2),
                                  in_=bank[:].rearrange(from_bank, u=2, v=2), func=RELU)
 
-        def w3_side(unit, h_unit):
-            bank = b_banks[unit % len(b_banks)]
+        def w3_side(unit, h_unit, bank):
             first_layer(W3, unit, bank)
             h[unit] = h_unit
             nc.vector.tensor_tensor(out=h_unit.rearrange(as_laid, u=2, v=2),
@@ -204,7 +202,7 @@ def tile_moe_shr_glu_relu_kernel(
 
         def products(pair):
             for unit in pair_units(pair):
-                w3_side(unit, keep.tile([P, H], BF16, name=f"h{unit}", align_bytes=64)[:])
+                w3_side(unit, keep.tile([P, H], BF16, name=f"h{unit}", align_bytes=64)[:], b_banks[unit % len(b_banks)])
 
         def turn(pair, bank):
             blocks = bank[:].rearrange("p (j u s) -> p j u s", j=2, u=2)
@@ -273,28 +271,28 @@ def tile_moe_shr_glu_relu_kernel(
             if q + GATHER_AHEAD < PAIRS:
                 gather(q + GATHER_AHEAD)
 
-        second_layer(0, a_banks[1])
         quantise(2)
         products(PAIRS)
         turn(PAIRS - 2, a_banks[2])
         turn(PAIRS - 1, a_banks[0])
-        second_layer(1, a_banks[3])
         quantise(3)
         quantise(4)
         last_h = keep.tile([P, 2, H], BF16, name="last_h", tag="turned4", align_bytes=64)
-        second_layer(2, a_banks[1])
+        second_layer(0, a_banks[1])
+        second_layer(1, a_banks[3])
+        second_layer(2, b_banks[2])
         second_layer(3, a_banks[0])
         second_layer(4, a_banks[2])
-        for j, unit in enumerate(pair_units(PAIRS + 1)):
-            w3_side(unit, last_h[:, j])
-        turn(PAIRS, b_banks[2])
-        turn(PAIRS + 1, b_banks[3])
+        w3_side(E + 2, last_h[:, 0], b_banks[3])
+        w3_side(E + 3, last_h[:, 1], a_banks[1])
+        turn(PAIRS, a_banks[1])
+        turn(PAIRS + 1, a_banks[3])
         quantise(5)
 
         prod = [keep.tile([P, T], F32, name=f"prod{r}") for r in range(TOP)]
-        sum_banks = [b_banks[0], b_banks[1], a_banks[3], a_banks[2]]
-        shared_banks = a_banks[:2]
-        back_banks = b_banks[2:] + shared_banks
+        sum_banks = b_banks
+        shared_banks = [a_banks[0], a_banks[2]]
+        back_banks = [a_banks[1], a_banks[3]] + shared_banks
 
         def fetch(r, first, last):
             cols = slice(first * C, last * C)

from contextlib import ExitStack

import concourse.mybir as mybir
from concourse.masks import make_identity

T, E, C, H, N = 512, 16, 128, 512, 128
TOP = 4
FLOPS = 3019898880

F32 = mybir.dt.float32
BF16 = mybir.dt.bfloat16
I32 = mybir.dt.int32
U32 = mybir.dt.uint32
U16 = mybir.dt.uint16
U8 = mybir.dt.uint8
FP8X4 = mybir.dt.float8_e4m3fn_x4
FP4X4 = mybir.dt.float4_e2m1fn_x4
MULT = mybir.AluOpType.mult
ADD = mybir.AluOpType.add
RELU = mybir.ActivationFunctionType.Relu

P = 128
W1, W3 = 0, 1
PAIRS = E // 2
CHUNKS = T // C
LIST_COLUMNS = C // 16
WORD_LOADS = [range(e, e + 2) for e in range(E - 2, -1, -2)] + [range(E, E + 1)]
RELU_AHEAD = 2
GATHER_AHEAD = 5
SCALE_RUNS = [range(12, E + 1), range(6, 12), range(0, 6)]
FIRST_PAIRS = 3
W2_LOADS = [range(E + 1)]
LOAD_AHEAD = 3
W3_FIRST = 5
QUANT_GROUPS = [range(0, 4), range(4, 8), range(8, 12), range(12, 14), range(14, 16), range(E, E + CHUNKS)]
QUANT_STEPS = (PAIRS - GATHER_AHEAD, PAIRS - GATHER_AHEAD + 2, PAIRS - 1)


def holder(groups, e):
    g = [n for n, members in enumerate(groups) if e in members][0]
    return g, e - groups[g].start


def expert(unit):
    return WORD_LOADS[unit // 2].start + unit % 2 if unit < E else E


def pair_units(pair):
    return range(2 * pair, 2 * pair + 2)


def block(j, width=C):
    return slice(j * width, (j + 1) * width)


def tile_moe_shr_glu_relu_kernel(
    tc, x_words, x_scales, w1_words, w1_scales, w3_words, w3_scales, w2_words, w2_scales,
    gate, offs, pos1, pos2, pos3, pos4, out,
):
    nc = tc.nc
    with ExitStack() as ctx:
        lists = ctx.enter_context(tc.tile_pool(name="lists", bufs=1))
        keep = ctx.enter_context(tc.tile_pool(name="keep", bufs=1))
        psum = ctx.enter_context(tc.psum_pool(name="psum", bufs=1))

        offs_t = lists.tile([P, E * LIST_COLUMNS], U16, name="offs_t")
        pos_t = [lists.tile([P, CHUNKS * LIST_COLUMNS], U16, name=f"pos_t{r}") for r in range(TOP)]
        xw = keep.tile([P, T], I32, name="xw", align_bytes=64)
        xs = keep.tile([P, T], U8, name="xs", align_bytes=64)

        def words_tile(m, load):
            name = f"up_words{m}_{load}"
            return keep.tile([P, len(WORD_LOADS[load]), 2 * H], U8, name=name, tag=name, align_bytes=64)[:]

        later_w1 = [words_tile(W1, load) for load in range(FIRST_PAIRS, PAIRS)]
        all_w3 = [words_tile(W3, load) for load in range(PAIRS + 1)]
        first_words = keep.tile([P, 2 * FIRST_PAIRS + 1, 2 * H], U8, name="first_words", align_bytes=64)
        first_expert = E - 2 * FIRST_PAIRS

        def first_rows(members):
            return first_words[:, members.start - first_expert:members.stop - first_expert]

        up_words = [[first_rows(members) for members in WORD_LOADS[:FIRST_PAIRS]] + later_w1
                    + [first_rows(WORD_LOADS[PAIRS])], all_w3]
        plane_rows = [[len(SCALE_RUNS[2]), len(SCALE_RUNS[1])], [len(SCALE_RUNS[0]), len(SCALE_RUNS[1])]]
        zeroed = [[keep.tile([P, rows, H], U8, name=f"up_planes{m}_{run}", align_bytes=64)
                   for run, rows in enumerate(plane_rows[m])] for m in (W1, W3)]
        spent_words = first_rows(range(WORD_LOADS[0].start, E + 1))
        up_planes = [[zeroed[W1][0][:], zeroed[W1][1][:], zeroed[W1][0][:]],
                     [zeroed[W3][0][:], zeroed[W3][1][:], spent_words.rearrange("p e (two i) -> p (e two) i", two=2)]]
        down_words = [keep.tile([P, len(members), 2 * N], U8, name=f"down_words{g}", align_bytes=64)
                      for g, members in enumerate(W2_LOADS)]
        down_plane = zeroed[W1][1][:].rearrange("p e b -> p (e b)")[:, 0:(E + 1) * N].rearrange("p (e n) -> p e n", n=N)
        gate_halves = [keep.tile([P, 2, T], F32, name=f"gate_half{i}") for i in range(TOP // 2)]
        gate_t = [gate_halves[r // 2][:, r % 2] for r in range(TOP)]
        y_slots = keep.tile([P, E * C], F32, name="y_slots")
        ident = keep.tile([P, P], F32, name="ident")

        nc.gpsimd.memset(xs[:].bitcast(I32), 0)
        for run in range(2):
            for m in (W1, W3):
                nc.vector.memset(zeroed[m][run][:].bitcast(I32), 0)
        make_identity(nc, ident[:])

        a_banks = [psum.tile([P, H], F32, name=f"a_bank{b}") for b in range(2 * RELU_AHEAD)]
        b_banks = [psum.tile([P, H], F32, name=f"b_bank{b}") for b in range(8 - 2 * RELU_AHEAD)]

        def load_words(tile, words, members):
            nc.sync.dma_start(out=tile.bitcast(I32),
                              in_=words[members.start:members.stop, 0].rearrange("e p b -> p e b").bitcast(I32))

        def load_scales(plane, scales, members):
            rows = scales[members.start:members.stop, 0]
            for r in range(4):
                nc.sync.dma_start(out=plane.bitcast(I32)[r:P:32, 0:len(members)],
                                  in_=rows[:, r:16:4, :].rearrange("e q i -> q e i").bitcast(I32))

        def load_up_words(m, load):
            load_words(up_words[m][load], (w1_words, w3_words)[m], WORD_LOADS[load])

        def load_run_opened_by(m, pair):
            for run, members in enumerate(SCALE_RUNS):
                if members.stop == WORD_LOADS[pair].stop:
                    load_scales(up_planes[m][run], (w1_scales, w3_scales)[m], members)

        def load_w1_of(pair):
            load_run_opened_by(W1, pair)
            load_up_words(W1, pair)

        def load_step(q):
            load_run_opened_by(W3, q)
            if q >= W3_FIRST:
                load_up_words(W3, q)
            if q + RELU_AHEAD < PAIRS:
                load_w1_of(q + RELU_AHEAD)
            if q < W3_FIRST:
                load_up_words(W3, q)

        def load_rest():
            load_up_words(W3, PAIRS)
            load_scales(down_plane, w2_scales, range(E + 1))
            for g, members in enumerate(W2_LOADS):
                load_words(down_words[g][:], w2_words, members)
            for i, half in enumerate(((pos1, pos2), (pos3, pos4))):
                for j, pos in enumerate(half):
                    nc.sync.dma_start(pos_t[2 * i + j][:], pos)
                nc.sync.dma_start(out=gate_halves[i][:], in_=gate[2 * i:2 * i + 2].rearrange("r n t -> n r t"))

        nc.sync.dma_start(offs_t[:], offs)
        for r in range(4):
            nc.sync.dma_start(out=xs[:].bitcast(I32)[r:P:32], in_=x_scales[0, r:16:4, :].bitcast(I32))
        nc.sync.dma_start(out=xw[:], in_=x_words[0].rearrange("p t r -> p (t r)").bitcast(I32))
        load_up_words(W1, PAIRS)
        load_scales(up_planes[W1][0], w1_scales, SCALE_RUNS[0])
        for pair in range(RELU_AHEAD):
            load_up_words(W1, pair)
        load_scales(up_planes[W3][0], w3_scales, SCALE_RUNS[0])
        load_up_words(W3, 0)
        load_w1_of(RELU_AHEAD)
        load_step(1)

        slot_words = keep.tile([P, GATHER_AHEAD * 2 * C], U32, name="slot_words", align_bytes=64)
        slot_plane = keep.tile([P, GATHER_AHEAD * 2 * C], U8, name="slot_plane", align_bytes=64)

        def gather(pair):
            place = block(pair % GATHER_AHEAD, 2 * C)
            entries = offs_t[:, WORD_LOADS[pair].start * LIST_COLUMNS:WORD_LOADS[pair].stop * LIST_COLUMNS]
            nc.vector.tensor_copy(out=slot_words[:, place], in_=xw[:].bitcast(U32).indirect(entries))
            nc.vector.tensor_copy(out=slot_plane[:, place], in_=xs[:].indirect(entries))

        from_bank = "s (p u v) -> s u p v"
        as_laid = "s (u p v) -> s u p v"
        relu_a, h, quantised = {}, {}, {}
        turned = [keep.tile([P, len(group) * H], BF16, name=f"turned{g}", tag=f"turned{g}", align_bytes=64)
                  for g, group in enumerate(QUANT_GROUPS)]

        def first_layer(m, unit, bank):
            if unit < E:
                cols = block(unit % (2 * GATHER_AHEAD))
                words, plane = slot_words[:, cols], slot_plane[:, cols]
            else:
                cols = block(unit - E)
                words, plane = xw[:, cols], xs[:, cols]
            load, place = holder(WORD_LOADS, expert(unit))
            run, row = holder(SCALE_RUNS, expert(unit))
            nc.tensor.matmul_mx(out=bank[:], lhsT=words.bitcast(FP8X4), lhsT_scale=plane,
                                rhs=up_words[m][load][:, place, :].bitcast(FP4X4),
                                rhs_scale=up_planes[m][run][:, row, :], start=True, stop=True)

        def w1_side(unit, bank):
            first_layer(W1, unit, bank)
            relu_a[unit] = keep.tile([P, H], F32, name=f"relu_a{unit}")
            nc.scalar.activation(out=relu_a[unit][:].rearrange(as_laid, u=2, v=2),
                                 in_=bank[:].rearrange(from_bank, u=2, v=2), func=RELU)

        def w3_side(unit, h_unit, bank):
            first_layer(W3, unit, bank)
            h[unit] = h_unit
            nc.vector.tensor_tensor(out=h_unit.rearrange(as_laid, u=2, v=2),
                                    in0=bank[:].rearrange(from_bank, u=2, v=2),
                                    in1=relu_a[unit][:].rearrange(as_laid, u=2, v=2), op=MULT)

        def products(pair):
            for unit in pair_units(pair):
                w3_side(unit, keep.tile([P, H], BF16, name=f"h{unit}", align_bytes=64)[:], b_banks[unit % len(b_banks)])

        def turn(pair, bank):
            blocks = bank[:].rearrange("p (j u s) -> p j u s", j=2, u=2)
            for j in (1, 0):
                words = h[2 * pair + j].bitcast(F32)
                for u in range(2):
                    nc.tensor.transpose(blocks[:, j, u, :], words[:, block(u)], ident[:])
            g, place = holder(QUANT_GROUPS, 2 * pair)
            laid = turned[g][:].bitcast(F32)[:, block(place // 2, H)]
            nc.scalar.copy(out=laid.rearrange("p (j s u) -> p j s u", j=2, u=2),
                           in_=blocks.rearrange("p j u s -> p j s u"))

        def quantise(g):
            width = len(QUANT_GROUPS[g]) * C
            tag = f"up_words{W3}_{QUANT_STEPS[g]}" if g < len(QUANT_STEPS) else f"codes{g}"
            codes = keep.tile([P, width], U32, name=f"codes{g}", tag=tag, align_bytes=64)
            plane = keep.tile([P, width], U8, name=f"h_plane{g}", align_bytes=64)
            nc.vector.quantize_mx(out=codes[:].bitcast(FP8X4), scales=plane[:], in_=turned[g][:])
            quantised[g] = (codes, plane)

        def h_operand(unit):
            g, place = holder(QUANT_GROUPS, unit)
            codes, plane = quantised[g]
            return codes[:, block(place)].bitcast(FP8X4), plane[:, block(place)]

        def w2_operand(e):
            load, place = holder(W2_LOADS, e)
            return down_words[load][:, place, :].bitcast(FP4X4), down_plane[:, e, :]

        def second_layer(g, bank):
            units = QUANT_GROUPS[g]
            lowest = min(expert(unit) for unit in units)
            for unit in reversed(units):
                words, plane = w2_operand(expert(unit))
                codes, h_plane = h_operand(unit)
                nc.tensor.matmul_mx(out=bank[:, block(expert(unit) - lowest)], lhsT=words, lhsT_scale=plane,
                                    rhs=codes, rhs_scale=h_plane, start=True, stop=True)
            nc.scalar.copy(out=y_slots[:, lowest * C:(lowest + len(units)) * C], in_=bank[:, 0:len(units) * C])

        for pair in range(GATHER_AHEAD):
            gather(pair)
        for j in range(CHUNKS):
            w1_side(E + j, b_banks[j])
        for unit in range(2 * RELU_AHEAD):
            w1_side(unit, a_banks[unit])
        load_step(2)

        for q in range(PAIRS):
            ahead = q + RELU_AHEAD
            if ahead < PAIRS:
                for unit in pair_units(ahead):
                    w1_side(unit, a_banks[unit % len(a_banks)])
            products(q)
            if q + LOAD_AHEAD < PAIRS:
                load_step(q + LOAD_AHEAD)
            if q + LOAD_AHEAD == PAIRS:
                load_rest()
            newest = 2 * min(ahead, PAIRS - 1) % len(a_banks)
            if 1 <= q < PAIRS - GATHER_AHEAD:
                turn(q - 1, a_banks[newest])
            elif q > PAIRS - GATHER_AHEAD and q % 2 == 0:
                turn(q - 2, a_banks[newest])
                turn(q - 1, a_banks[newest + 1 if ahead < PAIRS else 0])
            if q in QUANT_STEPS[:-1]:
                quantise(QUANT_STEPS.index(q))
            if q + GATHER_AHEAD < PAIRS:
                gather(q + GATHER_AHEAD)

        quantise(2)
        products(PAIRS)
        turn(PAIRS - 2, a_banks[2])
        turn(PAIRS - 1, a_banks[0])
        quantise(3)
        quantise(4)
        last_h = keep.tile([P, 2, H], BF16, name="last_h", tag="turned4", align_bytes=64)
        second_layer(0, a_banks[1])
        second_layer(1, a_banks[3])
        second_layer(2, b_banks[2])
        second_layer(3, a_banks[0])
        second_layer(4, a_banks[2])
        w3_side(E + 2, last_h[:, 0], b_banks[3])
        w3_side(E + 3, last_h[:, 1], a_banks[1])
        turn(PAIRS, a_banks[1])
        turn(PAIRS + 1, a_banks[3])
        quantise(5)

        prod = [keep.tile([P, T], F32, name=f"prod{r}") for r in range(TOP)]
        sum_banks = b_banks
        shared_banks = [a_banks[0], a_banks[2]]
        back_banks = [a_banks[1], a_banks[3]] + shared_banks

        def fetch(r, first, last):
            cols = slice(first * C, last * C)
            nc.vector.tensor_tensor(out=prod[r][:, cols],
                                    in0=y_slots[:].indirect(pos_t[r][:, first * LIST_COLUMNS:last * LIST_COLUMNS]),
                                    in1=gate_t[r][:, cols], op=MULT)

        def add_turned(bank, term, start, stop):
            nc.tensor.matmul(bank[:, 0:P], lhsT=term, rhs=ident[:], start=start, stop=stop, is_transpose=True)

        for r in range(2):
            fetch(r, 0, CHUNKS)
            for c in range(CHUNKS):
                add_turned(sum_banks[c], prod[r][:, block(c)], r == 0, False)
        words, plane = w2_operand(E)
        shared_t = keep.tile([P, T], F32, name="shared_t")
        for i, bank in enumerate(shared_banks):
            for j, unit in enumerate(pair_units(PAIRS + i)):
                codes, h_plane = h_operand(unit)
                nc.tensor.matmul_mx(out=bank[:, block(j)], lhsT=codes, lhsT_scale=h_plane,
                                    rhs=words, rhs_scale=plane, start=True, stop=True)
            nc.scalar.copy(out=shared_t[:, block(i, 2 * C)], in_=bank[:, 0:2 * C])
        sum_t = keep.tile([P, T], F32, name="sum_t")
        for c in range(CHUNKS):
            fetch(2, c, c + 1)
            add_turned(sum_banks[c], prod[2][:, block(c)], False, True)
            nc.scalar.copy(out=sum_t[:, block(c)], in_=sum_banks[c][:, 0:P])
        for c in range(CHUNKS):
            fetch(3, c, c + 1)
            add_turned(back_banks[c], shared_t[:, block(c)], True, False)
            add_turned(back_banks[c], sum_t[:, block(c)], False, True)
        result = keep.tile([P, T], F32, name="result")
        for half in range(2):
            for c in range(2 * half, 2 * half + 2):
                nc.vector.tensor_tensor(out=result[:, block(c)], in0=back_banks[c][:, 0:C], in1=prod[3][:, block(c)],
                                        op=ADD)
            nc.sync.dma_start(out=out[:, block(half, 2 * C)], in_=result[:, block(half, 2 * C)])
